import numpy as np, ml_dtypes
CORES = [24,25,26,27,28,29,30,31]
N = 8
import mx_ref
BF = ml_dtypes.bfloat16
def entries(a):
    return np.ascontiguousarray(a.T).reshape(-1)
def table(e):
    return np.ascontiguousarray(np.reshape(e, (-1, 16)).T).astype(np.int32)
def cols(t, e):
    v = np.concatenate([t.reshape(128, -1, 4), np.zeros((128, 1, 4), BF)], axis=1)
    return np.ascontiguousarray(v[:, e]).reshape(128, -1)
def f(rng, *shape):
    return mx_ref.flush((rng.standard_normal(shape, dtype=np.float32) * np.exp2(rng.integers(-2, 3, shape[:-1] + (1,)))).astype(BF))
def wide(rng, *shape, cols=0):
    v = rng.standard_normal(shape, dtype=np.float32) * np.exp2(rng.integers(-12, 13, shape)).astype(np.float32)
    if cols: v *= np.repeat(np.exp2(rng.integers(-cols, cols + 1, shape[:-2] + (1, shape[-1] // 4))) * (rng.random(shape[:-2] + (1, shape[-1] // 4)) > 0.0625), 4, axis=-1).astype(np.float32)
    return mx_ref.flush(v.astype(BF))
T, S, O, CAPP = 256, 512, 2, (128, 192, 256)
B = len(CAPP)
def wanters(q, b):
    return sum(1 << e for e in range(N) if (e ^ q ^ (1 << b)) % (2 << b) == 0)
def holders(q, b):
    return (q >> b) << b, ((q >> b) + 1) << b
def limit(rng, m, keep, lo, hi, s, most):
    v = m.reshape(-1)
    e = np.flatnonzero(v[lo * T:hi * T] & s) + lo * T
    e = e[np.argsort(rng.random(len(e)) - ((keep.reshape(-1)[e] & s) != 0))][most:]
    v[e] &= ~s
def masks(rng, keep=None, off=None, share=0.55):
    keep = np.zeros((N, T), int) if keep is None else keep
    off = np.zeros((N, T), bool) if off is None else off
    for r in range(N):
        if not ((keep >> r) & 1).any(): keep[r, rng.choice(np.flatnonzero(~off[r]))] |= 1 << r
    n = rng.integers(1, 4, (N, T)) * (rng.random((N, T)) < share)
    m = ((np.argsort(rng.random((N, T, N)), axis=2) < n[:, :, None]) * (1 << np.arange(N))).sum(axis=2)
    m = np.ascontiguousarray(np.where(off, 0, m) | keep)
    for b in range(B):
        for q in range(N): limit(rng, m, keep, *holders(q, b), wanters(q, b), CAPP[b])
    for r in range(N): limit(rng, m, keep, 0, N, 1 << r, S)
    return {"dm": np.stack([table(v) for v in m])}
def setup_inputs(rng):
    return {"x": f(rng, N, 128, 4 * T), **masks(rng), "w": f(rng, N, 128, 512 * O)}
def setup_inputs_comb(rng):
    k = np.zeros((N, T), int); c = np.arange(T); s = int(rng.integers(0, 16)); p = int(rng.integers(0, N)); g = p ^ (N >> 1)
    for e in range(N): k[:, (c - e - s) % 4 == 0] |= 1 << e
    lo, hi = holders(p, B - 1)
    k[lo:hi] &= ~(1 << g)
    k[p, c % 16 != s] |= 1 << g
    assert not check_inputs({"dm": np.stack([table(v) for v in k])})
    return {**setup_inputs(rng), **masks(rng, k)}
def setup_inputs_turn(rng):
    k = np.zeros((N, T), int); g = int(rng.integers(0, N))
    k[g ^ 1, rng.permutation(T)[:CAPP[0]]] |= 1 << g
    k[g ^ 3, rng.permutation(T)[:CAPP[0]]] |= 1 << g
    h = rng.permutation(T)
    k[g, h[:CAPP[0]]] |= 1 << (g ^ 3)
    k[g, h[CAPP[0]:2 * CAPP[0]]] |= 1 << (g ^ 2)
    if N == 8: k[g ^ 6, rng.permutation(T)[:CAPP[1]]] |= 1 << (g ^ 4)
    return {**setup_inputs(rng), **masks(rng, k)}
def setup_inputs_none(rng):
    z = np.zeros((N, T), bool); k = np.zeros((N, T), int); p = int(rng.integers(0, N))
    for r in range(N): z[r, rng.permutation(T)[:T // 2]] = True
    k[p ^ 1, rng.choice(np.flatnonzero(~z[p ^ 1]))] |= 1 << p
    d = {**setup_inputs(rng), **masks(rng, k, off=z, share=1)}
    d["dm"][p] = 0
    return d
def setup_inputs_full(rng):
    k = np.zeros((N, T), int); g = int(rng.integers(0, N)); s = int(rng.integers(0, T))
    k[g ^ 1, (np.arange(CAPP[0]) + s) % T] |= 1 << (g ^ 2)
    k[g, (np.arange(S - sum(CAPP[1:])) + s) % T] |= 1 << g
    for b in range(1, B):
        for r in range(N):
            if r >> b == (g >> b) ^ 1: k[r, (np.arange(CAPP[b] >> b) + s) % T] |= 1 << g
    assert not check_inputs({"dm": np.stack([table(v) for v in k])})
    return {**setup_inputs(rng), **masks(rng, k, share=1)}
def setup_inputs_spread(rng):
    d = setup_inputs(rng); d["x"] = wide(rng, N, 128, 4 * T, cols=8); return d
def check_inputs(d):
    bad = []
    m = np.stack([entries(v) for v in d["dm"]]).astype(np.int64)
    if m.min() < 0 or m.max() >= 1 << N: bad.append("dm")
    for r in range(N):
        if ((m >> r) & 1).sum() > S: bad.append("arrivals")
    for b in range(B):
        for q in range(N):
            lo, hi = holders(q, b)
            if ((m[lo:hi] & wanters(q, b)) != 0).sum() > CAPP[b]: bad.append("CAPP_" + str(b))
    return bad
def reference(x, dm, w):
    m = np.stack([entries(v) for v in dm])
    every = np.concatenate(list(x), axis=1)
    y = np.zeros((N, 128, O * S), np.float32); ln = np.zeros((N, 1, 2), np.float32)
    for r in range(N):
        e = np.flatnonzero((m.reshape(-1) >> r) & 1); n = len(e)
        k = np.full(S, -1); k[:n] = e
        a = mx_ref.quantize(cols(every, k))
        for o in range(O):
            y[r][:, S * o:S * o + n] = mx_ref.matmul(mx_ref.quantize(np.ascontiguousarray(w[r][:, 512 * o:512 * o + 512])), a)[:, :n]
        ln[r, 0, 0] = n; ln[r, 0, 1] = np.count_nonzero((m[r] >> r) & 1)
    return {"y": y, "ln": ln}

@@ -1,0 +1,442 @@
+from concourse.bass import DstId, RemoteDMATransfer
+from concourse.mybir import dt, AluOpType, AxisListType, ActivationFunctionType
+
+F32, I32, BF, U16, U8, Q8 = "float32", "int32", "bfloat16", "uint16", "uint8", "float8_e4m3fn_x4"
+LB = 4864
+ZERO = 127
+
+
+def _s(n, d):
+    return ("sbuf", [128, n], d)
+
+
+SCRATCH = {
+    "dmx": _s(64, I32), "xt": _s(1032, BF), "wt": _s(1024, BF), "zt": _s(512, BF),
+    "q0": _s(384, Q8), "s0": _s(384, U8), "q1": _s(512, Q8), "s1": _s(512, U8),
+    "q2": _s(704, Q8), "s2": _s(704, U8), "q3": _s(960, Q8), "s3": _s(960, U8),
+    "slq0": _s(128, Q8), "sls0": _s(128, U8), "slq1": _s(192, Q8), "sls1": _s(192, U8),
+    "slq2": _s(256, Q8), "sls2": _s(256, U8),
+    "qa": _s(512, Q8), "sa": _s(512, U8), "wq": _s(256, Q8), "ws": _s(256, U8),
+    "pa": _s(1, I32), "pb": _s(1, I32), "bi": _s(8, I32), "bf": _s(8, F32), "c5": _s(1, F32),
+    "gl": _s(12, U16), "ones": _s(32, F32), "c8": _s(8, F32),
+    "fj": _s(64, F32), "vraw": _s(128, F32), "v1r": _s(128, F32),
+    "ramp": _s(577, F32), "res": _s(104, F32), "uif": _s(32, F32), "ui": _s(32, F32), "ub": _s(32, F32),
+    "zz": _s(200, F32), "and0": _s(8, I32), "sel0": _s(8, F32), "lf0": _s(8, F32), "x0t": _s(32, F32), "bs0": _s(32, F32),
+    "ya0": _s(8, F32), "yc0": _s(8, F32), "p0": _s(8, U16),
+    "and1": _s(104, I32), "sel": _s(136, F32), "lf1": _s(16, F32), "x1t": _s(32, F32), "bs1": _s(32, F32),
+    "ya1": _s(16, F32), "yc1": _s(16, F32), "p1": _s(16, U16), "st1": _s(16, U16), "vr1": _s(64, F32),
+    "tt": _s(96, F32), "st": _s(16, U16), "vr2": _s(128, F32), "lf2": _s(64, F32), "inc2": _s(64, F32), "x2t": _s(64, F32),
+    "bs2": _s(64, F32), "tn": _s(64, F32), "tnt": _s(64, F32), "n2": _s(1, F32),
+    "ya2": _s(64, F32), "yc2": _s(64, F32), "p2": _s(16, U16), "p3": _s(16, U16),
+    "win0": _s(LB + 144, F32), "win1": _s(LB + 192, F32), "win2": _s(LB + 256, F32), "win3": _s(LB + 512, F32),
+    "tr0": _s(288, F32), "tr1": _s(192, F32), "tr2": _s(256, F32), "tr3": _s(512, F32),
+    "m01": _s(32, F32), "z1": _s(48, F32), "h1": _s(24, F32), "z2": _s(64, F32), "h2": _s(32, F32), "m2": _s(16, F32),
+    "z3": _s(128, F32), "h3": _s(64, F32), "m3": _s(32, F32), "tm": _s(32, F32),
+    "off0": _s(16, U16), "off1": _s(16, U16), "off2": _s(16, U16), "off3": _s(32, U16),
+    "lnt": _s(4, F32), "ys": _s(1024, F32),
+    "ps": ("psum", [128, 4096], F32),
+}
+SEMAPHORES = ["ld", "lx", "lw", "v", "s", "t", "gp", "mk", "r0c", "r0s", "r1c", "r1s", "r2c", "r2s", "rn",
+              "c1", "cr", "c3", "d1", "d2", "d3", "lo", "yo", "lnd"]
+
+
+def wanters(q, b):
+    return sum(1 << e for e in range(8) if (e ^ q ^ (1 << b)) % (2 << b) == 0)
+
+
+def rank_program(g, core, T, topo):
+    q = T.rank_of(core)
+    if q is None:
+        return
+    A, X = AluOpType, AxisListType.X
+    CP, ID = ActivationFunctionType.Copy, ActivationFunctionType.Identity
+    S = T.sem
+    p4, half = q & 3, q >> 2
+    own = slice(16 * p4, 16 * p4 + 15)
+    queues = {"v": g.vector, "s": g.scalar, "t": g.tensor, "gp": g, "y": g.sync}
+    n, seen, n_lo, n_yo = {"v": 0, "s": 0, "t": 0, "gp": 0}, {}, [0], [0]
+
+    def need(queue, sem, count):
+        if seen.get((queue, sem), 0) < count:
+            queues[queue].wait_ge(S[sem], int(count))
+            seen[(queue, sem)] = count
+
+    def done(kind, ins):
+        ins.then_inc(S[kind], 1)
+        n[kind] += 1
+        return n[kind]
+
+    def V(ins):
+        return done("v", ins)
+
+    def vv(count=None):
+        need("v", "v", n["v"] if count is None else count)
+
+    ts, tt_, cp = g.vector.tensor_scalar, g.vector.tensor_tensor, g.vector.tensor_copy
+    red, tp, scan = g.vector.tensor_reduce, g.vector.transpose, g.vector.tensor_tensor_scan
+    act = g.scalar.activation
+
+    def to(d):
+        return T.cores[d]
+
+    def send(dst, out, in_, sem):
+        rid, pid, _ = topo.addr(to(dst))
+        g.remote_dma(out, in_, S[sem], S.lo, pid, rid, topo.mask(core, to(dst)))
+        n_lo[0] += len(topo.engines(core, to(dst)))
+
+    def copy(out_q, in_q, out_s, in_s, sem, wq=(), ws=()):
+        for w in wq:
+            need("y", *w)
+        g.sync.dma_start(out_q.bitcast(dt.uint8), in_q.bitcast(dt.uint8)).then_inc(S[sem], 16)
+        for w in ws:
+            need("y", *w)
+        g.sync.dma_start(out_s, in_s).then_inc(S[sem], 16)
+
+    for a in range(4):
+        for h in range(2):
+            e = g.sync if h == 0 else g.scalar
+            e.dma_start(T.dmx[32 * a + 16 * h:32 * a + 16 * h + 16, own], T.dm[:, h:h + 15]).then_inc(S.ld, 16)
+    g.sync.dma_start(T.xt[:, 8:1032], T.x[:]).then_inc(S.lx, 16)
+
+    def iota(out, pat, base, cm=0):
+        return done("gp", g.iota(out, pat, base, cm, allow_small_or_imprecise_dtypes=True))
+
+    k_pa = done("gp", g.iota(T.pa[:], [[0, 1]], 0, 129))
+    k_pb = done("gp", g.iota(T.pb[:], [[0, 1]], 0, 17))
+    k_vraw = iota(T.vraw[:], [[32, 8], [1, 16]], 128)
+    k_fj = iota(T.fj[:], [[0, 2], [1, 32]], 0, 32)
+
+    k_zt = V(g.vector.memset(T.zt[:, 0:208], 0.0))
+    need("s", "v", k_zt)
+    done("s", act(T.ones[:], T.zt[:, 0:32], ID, 1.0))
+    k_zz = done("s", act(T.zz[:], T.zt[:, 0:200], CP))
+    done("s", act(T.win0[:, LB - 16:LB + 144], T.zt[:, 0:160], ID, 128.0))
+    k_m0 = done("s", act(T.m01[:], T.zt[:, 0:32], CP))
+
+    def bits(c, src, shift, mask):
+        need("v", "gp", k_pb if c == 1 else k_pa)
+        if shift:
+            return V(ts(T.bi[:, c:c + 1], src[:], shift, mask, A.logical_shift_right, A.bitwise_and))
+        return V(ts(T.bi[:, c:c + 1], src[:], mask, None, A.bitwise_and))
+
+    bits(0, T.pa, 0, 16)
+    bits(2, T.pa, 1, 7)
+    bits(3, T.pa, 0, 31)
+    bits(4, T.pa, 0, 15)
+    k_bi = bits(1, T.pb, 4, 1)
+    V(g.vector.memset(T.xt[:, 0:8], 0.0))
+    vv(k_bi)
+    k_bf = V(cp(T.bf[:, 0:5], T.bi[:, 0:5]))
+    ei = T.bf[:, 2:3]
+
+    peers = [q ^ 1, q ^ 2, q ^ 3]
+    g.wait_ge(S.ld, 128)
+    m = topo.mask(core, to(peers[0]))
+    ids = []
+    for d in peers:
+        m &= topo.mask(core, to(d))
+        rid, pid, _ = topo.addr(to(d))
+        ids.append(DstId(rid=rid, pnc=pid))
+    g.remote_dma_fused([RemoteDMATransfer(dst_ids=ids, dma_engine_mask=m, remote_sem=S.mk, srcs=[T.dmx[:, own]],
+                                          dsts=[T.dmx[:, own] for d in peers])], local_sem=S.lo)
+    n_lo[0] += bin(m).count("1")
+    k_c8 = iota(T.c8[:], [[32, 8]], 129)
+    k_ramp = iota(T.ramp[:, 129:385], [[1, 256]], 128)
+    if half == 0:
+        k_gp3 = iota(T.uif[:], [[16, 32]], -256)
+    else:
+        k_gp3 = iota(T.win3[:, LB:LB + 256], [[1, 256]], -256)
+
+    def turn(i, count):
+        return V(tp(T["tr%d" % i][:], T["win%d" % i][:, LB:LB + count]))
+
+    def spread(i, count, k):
+        tr, z, nb, sem = T["tr%d" % i], T["z%d" % i], count // 32, "d%d" % i
+        vv(k)
+        k = V(tt_(z[:, 0:nb], tr[:, 0:count:32], tr[:, 16:count:32], A.max))
+        need("y", "v", k)
+        need("s", "v", k)
+        for s in range(1, 8):
+            c, a = slice(nb * s, nb * s + nb), 16 * s
+            g.sync.dma_start(z[0:128 - a, c], z[a:128, 0:nb]).then_inc(S[sem], 16)
+            g.scalar.dma_start(z[128 - a:128, c], z[0:a, 0:nb]).then_inc(S[sem], 16)
+
+    def merge(i, count, out, fill=()):
+        z, h, nb = T["z%d" % i], T["h%d" % i], count // 32
+        need("v", "d%d" % i, 224)
+        k = V(tt_(h[:], z[:, 0:4 * nb], z[:, 4 * nb:8 * nb], A.max))
+        if fill:
+            fill[0]()
+        vv(k)
+        k = V(tt_(out, h[:, 0:2 * nb], h[:, 2 * nb:4 * nb], A.max))
+        if fill:
+            fill[1]()
+        vv(k)
+
+    def pick(qo, so, qi, si, off, k_off, vwaits=(), swaits=()):
+        vv(k_off)
+        for w in vwaits:
+            need("v", *w)
+        a = V(cp(qo.bitcast(dt.uint32), qi.bitcast(dt.uint32).indirect(off)))
+        need("s", "v", k_off)
+        for w in swaits:
+            need("s", *w)
+        return a, done("s", act(so, si.indirect(off), CP))
+
+    def lift(out, sel, k):
+        need("s", "v", k)
+        return done("s", act(out, sel, CP, 0.0, float(LB - 1)))
+
+    def last_gather(c, nb):
+        return V(ts(T.gl[:, c:c + 1], T.bf[:, 1:2], nb, ei, A.mult, A.add))
+
+    need("v", "ld", 128)
+    k = V(ts(T.and0[:], T.dmx[:, 16 * p4:16 * p4 + 15:2], wanters(q, 0), None, A.bitwise_and))
+    bits(5, T.pa, 5, 15)
+    vv(k)
+    k = V(ts(T.sel0[:], T.and0[:], 0.0, None, A.is_gt))
+    kb = lift(T.lf0[:], T.sel0[:], k)
+    k_bi = bits(6, T.pa, 5, 31)
+    need("s", "v", k_bf)
+    need("s", "gp", k_vraw)
+    k_v1 = done("s", act(T.v1r[:], T.vraw[:], ID, T.bf[:, 0:1]))
+    k1 = done("s", act(T.res[:], T.zt[:, 0:104], ID, 1.0))
+    vv(k)
+    need("v", "s", k_zz)
+    k = V(scan(T.zz[:, 0:8], T.ones[:, 0:8], T.sel0[:], 0.0, A.mult, A.add))
+    vv(k_bf)
+    k_c5 = V(ts(T.c5[:], T.bf[:, 0:1], -0.0625, 5.0, A.mult, A.add))
+    vv(k)
+    k = V(tp(T.x0t[:], T.zz[:, 0:32]))
+    need("v", "s", kb)
+    ka = V(tt_(T.ya0[:], T.zz[:, 0:8], T.lf0[:], A.add))
+    vv(k)
+    k = V(scan(T.zz[:, 73:104], T.ones[:, 0:31], T.x0t[:, 0:31], 0.0, A.mult, A.add))
+    vv(ka)
+    need("v", "gp", k_fj)
+    V(tt_(T.yc0[:], T.ya0[:], T.fj[:, 0:8], A.max))
+    vv(k)
+    k = V(tp(T.bs0[:], T.zz[:, 72:104]))
+    V(cp(T.gl[:, 8:12:2], T.bi[:, 5:7]))
+    vv(k)
+    k = V(ts(T.p0[:], T.yc0[:], T.bs0[:, 7:8], None, A.add))
+    V(ts(T.gl[:, 0:1], T.bf[:, 1:2], T.c5[:], ei, A.mult, A.add))
+    need("y", "v", k)
+    g.sync.dma_start(T.wt[:], T.w[:]).then_inc(S.lw, 16)
+    vv(k)
+    need("v", "s", k_v1)
+    k_w0 = V(cp(T.win0[:].indirect(T.p0[:]), T.v1r[:]))
+    need("v", "lx", 16)
+    V(g.vector.quantize_mx(T.q0[:, 126:384], T.s0[:, 126:384], T.xt[:]))
+    need("s", "s", k1)
+    done("s", act(T.res[:, 16:33:16], T.zt[:, 0:2], CP))
+    done("s", act(T.res[:, 72:73], T.zt[:, 0:1], CP))
+    need("s", "gp", k_c8)
+    k_res = done("s", act(T.sel[:, 104 + 8 * p4:112 + 8 * p4], T.c8[:], ID, T.bf[:, 3:4]))
+    need("s", "gp", k_ramp)
+    done("s", act(T.ramp[:, 0:129], T.ramp[:, 129:258], ID, 255.0))
+    k_rs = done("s", act(T.ramp[:, 385:577], T.ramp[:, 129:321], ID, 384.0))
+    k_ui = done("s", act(T.win1[:, LB:LB + 192], T.zt[:, 0:192], ID, 128.0))
+    if half == 0:
+        need("s", "gp", k_gp3)
+        k_ui = done("s", act(T.ui[:], T.uif[:], ID, T.bf[:, 4:5]))
+    vv(k_w0)
+    V(tp(T.tr0[:, 0:128], T.win0[:, LB:LB + 128]))
+    k0 = V(tp(T.tr0[:, 128:288], T.win0[:, LB - 16:LB + 144]))
+    last_gather(2, 6.0)
+    last_gather(4, 8.0)
+    vv(k0)
+    need("v", "s", k_m0)
+    k0 = V(tt_(T.m01[:, 0:9], T.tr0[:, 0:288:32], T.tr0[:, 16:288:32], A.max))
+    last_gather(6, 16.0)
+    vv(k0)
+    k0 = V(cp(T.off0[:], T.m01[:, 0:16].indirect(T.gl[:, 0:1])))
+    V(g.vector.memset(T.zt[:, 208:512], 0.0))
+    k0, ks = pick(T.slq0[:], T.sls0[:], T.q0[:], T.s0[:], T.off0[:, 0:8], k0)
+    need("gp", "v", k0)
+    send(q ^ 1, T.q1[:, 384:512].bitcast(dt.uint8), T.slq0[:].bitcast(dt.uint8), "r0c")
+    need("gp", "s", ks)
+    send(q ^ 1, T.s1[:, 384:512], T.sls0[:], "r0s")
+    copy(T.q1[:, 128:384], T.q0[:, 128:384], T.s1[:, 128:384], T.s0[:, 128:384], "c1", (("v", k0),), (("s", ks),))
+
+    pa, pb, o = 2 * (p4 >> 1), 2 * (1 - (p4 >> 1)), p4 ^ 1
+    share1, share = T.gl[:, 8:9], T.gl[:, 10:11]
+    need("v", "mk", 48)
+    V(ts(T.and1[:, 0:16], T.dmx[:, 16 * pa:16 * pa + 31:2], wanters(q, 1), None, A.bitwise_and))
+    V(ts(T.and1[:, 16:32], T.dmx[:, 16 * pb:16 * pb + 31:2], wanters(q ^ 2, 1), None, A.bitwise_and))
+    k = V(ts(T.and1[:, 32:40], T.dmx[:, 16 * o:16 * o + 15:2], wanters(q ^ 1, 0), None, A.bitwise_and))
+    V(ts(T.and1[:, 40:72], T.dmx[:, 0:63:2], 1 << (q ^ 4), None, A.bitwise_and))
+    vv(k)
+    k = V(ts(T.sel[:, 0:40], T.and1[:, 0:40], 0.0, None, A.is_gt))
+    kb = lift(T.lf1[:], T.sel[:, 0:16], k)
+    kc = V(ts(T.and1[:, 72:104], T.dmx[:, 0:63:2], 1 << q, None, A.bitwise_and))
+    vv(k)
+    need("v", "s", k_res)
+    k = V(scan(T.zz[:, 32:72], T.res[:, 0:40], T.sel[:, 0:40], 0.0, A.mult, A.add))
+    vv(kc)
+    kc = V(ts(T.sel[:, 40:104], T.and1[:, 40:104], 0.0, None, A.is_gt))
+    vv(k)
+    k = V(tp(T.x1t[:], T.zz[:, 40:72]))
+    need("v", "s", kb)
+    ka = V(tt_(T.ya1[:], T.zz[:, 32:48], T.lf1[:], A.add))
+    vv(k)
+    k = V(scan(T.zz[:, 105:136], T.ones[:, 0:31], T.x1t[:, 0:31], 0.0, A.mult, A.add))
+    vv(kc)
+    k_tt = V(tp(T.tt[:, 0:64], T.sel[:, 40:104]))
+    k_lf = lift(T.lf2[:], T.tt[:, 0:64], k_tt)
+    vv(k)
+    k_bs = V(tp(T.bs1[:], T.zz[:, 104:136]))
+    vv(ka)
+    ka = V(tt_(T.yc1[:], T.ya1[:], T.fj[:, 0:16], A.max))
+    vv(k_bs)
+    V(ts(T.sel[:, 104 + 8 * o:112 + 8 * o], T.zz[:, 64:72], T.bs1[:, 31:32], None, A.add))
+    k = V(ts(T.sel[:, 104 + 8 * pb:120 + 8 * pb], T.zz[:, 48:64], T.bs1[:, 23:24], 384.0, A.add, A.add))
+    vv(ka)
+    k_p1 = V(ts(T.p1[:], T.yc1[:].indirect(share1), T.bs1[:, 7:8], None, A.add))
+    vv(k)
+    k = V(cp(T.st1[:], T.sel[:, 104 + 8 * pa:120 + 8 * pa].indirect(share1)))
+    need("s", "v", k)
+    need("s", "s", k_rs)
+    k_vr1 = done("s", act(T.vr1[:], T.ramp[:].indirect(T.st1[:, 0:4]), CP))
+    kt = V(tp(T.tt[:, 64:96], T.sel[:, 104:136]))
+    kc = V(scan(T.inc2[:], T.res[:, 40:104], T.tt[:, 0:64], 0.0, A.mult, A.add))
+    vv(kt)
+    k = V(cp(T.st[:], T.tt[:, 64:96].indirect(share)))
+    need("v", "s", k_vr1)
+    k_w1 = V(cp(T.win1[:].indirect(T.p1[:, 0:4]), T.vr1[:]))
+    need("s", "v", k)
+    k_vr = done("s", act(T.vr2[:], T.ramp[:].indirect(T.st[:, 0:8]), CP))
+    k_f2 = done("s", act(T.win2[:, LB:LB + 256], T.zt[:, 0:256], ID, float(ZERO)))
+    vv(kc)
+    k_x2 = V(tp(T.x2t[:], T.inc2[:]))
+    vv(k_w1)
+    k_t1 = turn(1, 192)
+    need("v", "s", k_lf)
+    ka = V(tt_(T.ya2[:], T.inc2[:], T.lf2[:], A.add))
+    spread(1, 192, k_t1)
+    V(scan(T.zz[:, 137:168], T.ones[:, 0:31], T.x2t[:, 0:31], 0.0, A.mult, A.add))
+    k = V(scan(T.zz[:, 169:200], T.ones[:, 0:31], T.x2t[:, 32:63], 0.0, A.mult, A.add))
+    need("s", "v", k)
+    for c in range(2):
+        b = 32 * c
+        kn = done("s", act(T.tn[:, b:b + 32], T.ones[:], ID, T.x2t[:, b + 31:b + 32], T.zz[:, b + 167:b + 168]))
+    if half == 0:
+        k_fill = done("s", act(T.win3[:, LB:LB + 512], T.zt[:], ID, -1000.0))
+    else:
+        k_fill = done("s", act(T.win3[:, LB + 256:LB + 512], T.zt[:, 0:256], CP))
+    copy(T.q2[:, 126:384], T.q0[:, 126:384], T.s2[:, 126:384], T.s0[:, 126:384], "cr")
+    copy(T.q3[:, 256:258], T.q0[:, 126:128], T.s3[:, 256:258], T.s0[:, 126:128], "c3")
+    vv(ka)
+    ka = V(tt_(T.yc2[:], T.ya2[:], T.fj[:], A.max))
+    vv(k)
+    k = V(tp(T.bs2[:], T.zz[:, 136:200]))
+    vv(k)
+    k_p2 = V(ts(T.p2[:], T.yc2[:, 0:32].indirect(share), T.bs2[:, 31:32], None, A.add))
+    if half == 0:
+        V(ts(T.p3[:], T.yc2[:, 32:64].indirect(share), T.bs2[:, 63:64], None, A.add))
+    vv(k_p2)
+    need("v", "s", k_f2)
+    k_w2 = V(cp(T.win2[:].indirect(T.p2[:, 0:8]), T.vr2[:]))
+    need("v", "s", kn)
+    k_n = V(tp(T.tnt[:], T.tn[:]))
+    nh = T.tnt[:, 63:64]
+    need("gp", "v", k_n)
+    send(q ^ 4, T.n2[:], T.tnt[:, 31:32], "rn")
+    vv(k_w2)
+    k_t2 = turn(2, 256)
+    if half == 0:
+        need("v", "s", k_ui)
+        vv(k_n)
+        V(ts(T.ub[:], T.ui[:], nh, 0.0, A.subtract, A.min))
+    spread(2, 256, k_t2)
+    copy(T.q2[:, 384:512], T.q1[:, 384:512], T.s2[:, 384:512], T.s1[:, 384:512], "cr", (("r0c", 16),), (("r0s", 16),))
+    copy(T.q3[:, 640:768], T.q1[:, 384:512], T.s3[:, 640:768], T.s1[:, 384:512], "c3")
+    merge(1, 192, T.m01[:, 16:28])
+    k_off1 = V(cp(T.off1[:], T.m01[:, 16:32].indirect(T.gl[:, 2:3])))
+    ka, ks = pick(T.slq1[:], T.sls1[:], T.q1[:], T.s1[:], T.off1[:, 0:12], k_off1,
+                  (("c1", 32), ("r0c", 16)), (("c1", 32), ("r0s", 16)))
+    need("gp", "v", ka)
+    send(q ^ 2, T.q2[:, 512:704].bitcast(dt.uint8), T.slq1[:].bitcast(dt.uint8), "r1c")
+    need("gp", "s", ks)
+    send(q ^ 2, T.s2[:, 512:704], T.sls1[:], "r1s")
+    if half:
+        need("v", "rn", 16)
+        vv(V(ts(T.p3[:], T.yc2[:, 32:64].indirect(share), T.bs2[:, 63:64], T.n2[:], A.add, A.add)))
+    need("v", "s", k_fill)
+    need("v", "gp", k_gp3)
+    vv(V(cp(T.win3[:].indirect(T.p3[:, 0:8]), T.vr2[:])))
+    spread(3, 512, turn(3, 512))
+    copy(T.q3[:, 768:960], T.q2[:, 512:704], T.s3[:, 768:960], T.s2[:, 512:704], "c3", (("r1c", 16),), (("r1s", 16),))
+
+    def length_all():
+        need("v", "rn", 16)
+        V(ts(T.lnt[:, 0:1], nh, T.n2[:], None, A.add))
+
+    def length_own():
+        need("y", "v", V(red(T.lnt[:, 1:2], T.x2t[:, 32 + 8 * p4:40 + 8 * p4], X, A.add)))
+        g.sync.dma_start(T.ln[:], T.lnt[31:32, 0:2]).then_inc(S.lnd, 16)
+
+    merge(2, 256, T.m2[:], (length_all, length_own))
+    k_off2 = V(cp(T.off2[:], T.m2[:].indirect(T.gl[:, 4:5])))
+    ka, ks = pick(T.slq2[:], T.sls2[:], T.q2[:], T.s2[:], T.off2[:], k_off2, (("cr", 64), ("r1c", 16)), (("cr", 64), ("r1s", 16)))
+    need("gp", "v", ka)
+    send(q ^ 4, T.q3[:, 0:256].bitcast(dt.uint8), T.slq2[:].bitcast(dt.uint8), "r2c")
+    need("gp", "s", ks)
+    send(q ^ 4, T.s3[:, 0:256], T.sls2[:], "r2s")
+
+    k_wq = []
+
+    def quant_w():
+        need("v", "lw", 16)
+        k_wq.append(V(g.vector.quantize_mx(T.wq[:], T.ws[:], T.wt[:])))
+
+    def quant_x():
+        V(g.vector.quantize_mx(T.q3[:, 384:640], T.s3[:, 384:640], T.xt[:, 8:1032]))
+
+    merge(3, 512, T.m3[:], (quant_x, quant_w))
+    lo3, hi3 = T.m3[:, 0:24].indirect(T.gl[:, 6:7]), T.m3[:, 8:32].indirect(T.gl[:, 6:7])
+    if half == 0:
+        V(tt_(T.tm[:, 0:16], lo3, T.ub[:, 0:16], A.max))
+        vv(V(tt_(T.tm[:, 16:32], hi3, T.ub[:, 16:32], A.max)))
+        k_off3 = V(ts(T.off3[:], T.tm[:], 256.0, None, A.add))
+    else:
+        V(cp(T.off3[:, 16:32], hi3))
+        k_off3 = V(ts(T.off3[:, 0:16], lo3, 256.0, None, A.add))
+
+    def product(i, a, b, lo, vwaits, swaits):
+        w_ = b - a
+        ka, kb = pick(T.qa[:, a:b], T.sa[:, a:b], T.q3[:, lo:960], T.s3[:, lo:960], T.off3[:, a // 16:b // 16], k_off3,
+                      vwaits, swaits)
+        need("t", "v", ka)
+        need("t", "s", kb)
+        for w in range(2):
+            e = 512 * (2 * i + w)
+            done("t", g.tensor.matmul_mx(T.ps[:, e:e + w_], T.wq[:, 128 * w:128 * w + 128],
+                                         T.ws[:, 128 * w:128 * w + 128], T.qa[:, a:b], T.sa[:, a:b], True, True))
+        return n["t"]
+
+    def store(a, b, i, k):
+        e, w_ = 1024 * i, b - a
+        need("v", "t", k - 1)
+        need("s", "t", k)
+        ka = V(cp(T.ys[:, a:b], T.ps[:, e:e + w_]))
+        kb = done("s", act(T.ys[:, 512 + a:512 + b], T.ps[:, e + 512:e + 512 + w_], CP))
+        need("y", "v", ka)
+        g.sync.dma_start(T.y[:, a:b], T.ys[:, a:b]).then_inc(S.yo, 16)
+        need("y", "s", kb)
+        g.sync.dma_start(T.y[:, 512 + a:512 + b], T.ys[:, 512 + a:512 + b]).then_inc(S.yo, 16)
+        n_yo[0] += 32
+
+    need("t", "v", k_wq[0])
+    held, r2 = ("c3", 96), (("r2c", 16), ("r2s", 16))
+    runs = [(0, 128, 0), (128, 384, 0), (384, 512, 0)] if half == 0 else [(256, 512, 256), (0, 128, 0), (128, 256, 0)]
+    ends = [product(i, a, b, lo, [held] + [r2[0]] * (lo == 0), [held] + [r2[1]] * (lo == 0)) for i, (a, b, lo) in enumerate(runs)]
+    for i, (a, b, lo) in enumerate(runs):
+        store(a, b, i, ends[i])
+
+    for kind in ("v", "s", "t"):
+        need("gp", kind, n[kind])
+    g.wait_ge(S.gp, n["gp"])
+    g.wait_ge(S.lo, n_lo[0])
+    g.wait_ge(S.yo, n_yo[0])
+    g.wait_ge(S.lnd, 16)

@@ -1,9 +1,13 @@
 from concourse.bass import DstId, RemoteDMATransfer
-from concourse.mybir import dt, AluOpType, AxisListType, ActivationFunctionType
+from concourse.mybir import dt, AluOpType, ActivationFunctionType
 
 F32, I32, BF, U16, U8, Q8 = "float32", "int32", "bfloat16", "uint16", "uint8", "float8_e4m3fn_x4"
-LB = 4864
-ZERO = 127
+BIG = 4096.0
+TRASH = 528
+WIN = 2352
+ONE, TWO, FOUR = 7, 15, 23
+SETS = 2 ** ONE + (2 ** TWO + 2 ** (TWO + 4)) + sum(2 ** (FOUR + 2 * i) for i in range(4))
+S1, SP = 24, 25
 
 
 def _s(n, d):
@@ -11,432 +15,277 @@ def _s(n, d):
 
 
 SCRATCH = {
-    "dmx": _s(64, I32), "xt": _s(1032, BF), "wt": _s(1024, BF), "zt": _s(512, BF),
-    "q0": _s(384, Q8), "s0": _s(384, U8), "q1": _s(512, Q8), "s1": _s(512, U8),
-    "q2": _s(704, Q8), "s2": _s(704, U8), "q3": _s(960, Q8), "s3": _s(960, U8),
+    "dmx": _s(128, I32), "dmu": _s(16, U16), "xt": _s(1032, BF), "wt": _s(1024, BF),
+    "q0": _s(288, Q8), "s0": _s(288, U8), "q1": _s(386, Q8), "s1": _s(386, U8),
+    "q2": _s(578, Q8), "s2": _s(578, U8), "q3": _s(834, Q8), "s3": _s(834, U8),
     "slq0": _s(128, Q8), "sls0": _s(128, U8), "slq1": _s(192, Q8), "sls1": _s(192, U8),
     "slq2": _s(256, Q8), "sls2": _s(256, U8),
     "qa": _s(512, Q8), "sa": _s(512, U8), "wq": _s(256, Q8), "ws": _s(256, U8),
-    "pa": _s(1, I32), "pb": _s(1, I32), "bi": _s(8, I32), "bf": _s(8, F32), "c5": _s(1, F32),
-    "gl": _s(12, U16), "ones": _s(32, F32), "c8": _s(8, F32),
-    "fj": _s(64, F32), "vraw": _s(128, F32), "v1r": _s(128, F32),
-    "ramp": _s(577, F32), "res": _s(104, F32), "uif": _s(32, F32), "ui": _s(32, F32), "ub": _s(32, F32),
-    "zz": _s(200, F32), "and0": _s(8, I32), "sel0": _s(8, F32), "lf0": _s(8, F32), "x0t": _s(32, F32), "bs0": _s(32, F32),
-    "ya0": _s(8, F32), "yc0": _s(8, F32), "p0": _s(8, U16),
-    "and1": _s(104, I32), "sel": _s(136, F32), "lf1": _s(16, F32), "x1t": _s(32, F32), "bs1": _s(32, F32),
-    "ya1": _s(16, F32), "yc1": _s(16, F32), "p1": _s(16, U16), "st1": _s(16, U16), "vr1": _s(64, F32),
-    "tt": _s(96, F32), "st": _s(16, U16), "vr2": _s(128, F32), "lf2": _s(64, F32), "inc2": _s(64, F32), "x2t": _s(64, F32),
-    "bs2": _s(64, F32), "tn": _s(64, F32), "tnt": _s(64, F32), "n2": _s(1, F32),
-    "ya2": _s(64, F32), "yc2": _s(64, F32), "p2": _s(16, U16), "p3": _s(16, U16),
-    "win0": _s(LB + 144, F32), "win1": _s(LB + 192, F32), "win2": _s(LB + 256, F32), "win3": _s(LB + 512, F32),
-    "tr0": _s(288, F32), "tr1": _s(192, F32), "tr2": _s(256, F32), "tr3": _s(512, F32),
-    "m01": _s(32, F32), "z1": _s(48, F32), "h1": _s(24, F32), "z2": _s(64, F32), "h2": _s(32, F32), "m2": _s(16, F32),
-    "z3": _s(128, F32), "h3": _s(64, F32), "m3": _s(32, F32), "tm": _s(32, F32),
-    "off0": _s(16, U16), "off1": _s(16, U16), "off2": _s(16, U16), "off3": _s(32, U16),
+    "two": _s(24, F32), "pr": _s(56, F32), "pw": _s(32, F32), "ramp": _s(256, F32), "ti": _s(256, I32), "tf": _s(256, BF),
+    "ci": _s(160, BF), "ct": _s(160, BF), "fj": _s(32, F32), "cc": _s(4, F32), "gls": _s(6, U16),
+    "ab": _s(576, F32), "zs": _s(288, BF), "tr": _s(288, BF), "ex": _s(32, F32), "tot": _s(2, F32), "nn": _s(2, F32),
+    "st": _s(8, U16), "vr": _s(128, BF), "yy": _s(32, F32), "n2": _s(1, F32),
+    "p0": _s(8, U16), "p1": _s(8, U16), "p2": _s(8, U16), "p3": _s(8, U16),
+    "win0": _s(WIN, BF), "win1": _s(WIN, BF), "win3": _s(WIN, BF),
+    "tr0": _s(288, BF), "tr1": _s(1056, BF), "tr3": _s(1056, BF),
+    "z0": _s(17, F32), "z1": _s(33, F32), "z3": _s(33, F32), "c1": _s(33, F32), "c3": _s(33, F32),
+    "h1": _s(33, F32), "h3": _s(33, F32), "m1": _s(33, F32), "m3": _s(33, F32),
+    "off0": _s(16, U16), "off1": _s(32, U16), "off3": _s(32, U16),
     "lnt": _s(4, F32), "ys": _s(1024, F32),
     "ps": ("psum", [128, 4096], F32),
 }
 SEMAPHORES = ["ld", "lx", "lw", "v", "s", "t", "gp", "mk", "r0c", "r0s", "r1c", "r1s", "r2c", "r2s", "rn",
-              "c1", "cr", "c3", "d1", "d2", "d3", "lo", "yo", "lnd"]
-
-
-def wanters(q, b):
-    return sum(1 << e for e in range(8) if (e ^ q ^ (1 << b)) % (2 << b) == 0)
+              "c1", "c2", "c3", "l0", "l1", "l2", "lo", "yo", "lnd"]
 
 
 def rank_program(g, core, T, topo):
     q = T.rank_of(core)
     if q is None:
         return
-    A, X = AluOpType, AxisListType.X
-    CP, ID = ActivationFunctionType.Copy, ActivationFunctionType.Identity
+    A = AluOpType
+    CP, ID, RELU = ActivationFunctionType.Copy, ActivationFunctionType.Identity, ActivationFunctionType.Relu
     S = T.sem
-    p4, half = q & 3, q >> 2
-    own = slice(16 * p4, 16 * p4 + 15)
+    p4, half, par = q & 3, q >> 2, q & 1
+    pa, pb, o = p4 & 2, 2 - (p4 & 2), p4 ^ 1
+    s0, s2, s3 = FOUR - 1 + par, ONE - (q ^ 4), ONE - q
+
+    def block(a):
+        return slice(32 * a, 32 * a + 32)
+
+    def side(a):
+        return slice(32 * a, 32 * a + 64)
+
     queues = {"v": g.vector, "s": g.scalar, "t": g.tensor, "gp": g, "y": g.sync}
-    n, seen, n_lo, n_yo = {"v": 0, "s": 0, "t": 0, "gp": 0}, {}, [0], [0]
+    n, seen, left, n_yo = {"v": 0, "s": 0, "t": 0, "gp": 0}, {}, {"l0": 0, "l1": 0, "l2": 0, "lo": 0}, [0]
 
     def need(queue, sem, count):
         if seen.get((queue, sem), 0) < count:
             queues[queue].wait_ge(S[sem], int(count))
             seen[(queue, sem)] = count
 
-    def done(kind, ins):
-        ins.then_inc(S[kind], 1)
-        n[kind] += 1
-        return n[kind]
+    def on(kind, call):
+        def after(*waits):
+            def run(*a, **k):
+                for w in waits:
+                    need(kind, *w)
+                call(*a, **k).then_inc(S[kind], 1)
+                n[kind] += 1
+                return kind, n[kind]
+            return run
+        return after
 
-    def V(ins):
-        return done("v", ins)
-
-    def vv(count=None):
-        need("v", "v", n["v"] if count is None else count)
-
-    ts, tt_, cp = g.vector.tensor_scalar, g.vector.tensor_tensor, g.vector.tensor_copy
-    red, tp, scan = g.vector.tensor_reduce, g.vector.transpose, g.vector.tensor_tensor_scan
-    act = g.scalar.activation
-
-    def to(d):
-        return T.cores[d]
-
-    def send(dst, out, in_, sem):
-        rid, pid, _ = topo.addr(to(dst))
-        g.remote_dma(out, in_, S[sem], S.lo, pid, rid, topo.mask(core, to(dst)))
-        n_lo[0] += len(topo.engines(core, to(dst)))
-
-    def copy(out_q, in_q, out_s, in_s, sem, wq=(), ws=()):
-        for w in wq:
-            need("y", *w)
-        g.sync.dma_start(out_q.bitcast(dt.uint8), in_q.bitcast(dt.uint8)).then_inc(S[sem], 16)
-        for w in ws:
-            need("y", *w)
-        g.sync.dma_start(out_s, in_s).then_inc(S[sem], 16)
-
-    for a in range(4):
-        for h in range(2):
-            e = g.sync if h == 0 else g.scalar
-            e.dma_start(T.dmx[32 * a + 16 * h:32 * a + 16 * h + 16, own], T.dm[:, h:h + 15]).then_inc(S.ld, 16)
-    g.sync.dma_start(T.xt[:, 8:1032], T.x[:]).then_inc(S.lx, 16)
+    v = g.vector
+    ts, tt, cp, tp = on("v", v.tensor_scalar), on("v", v.tensor_tensor), on("v", v.tensor_copy), on("v", v.transpose)
+    scan, fill, quant = on("v", v.tensor_tensor_scan), on("v", v.memset), on("v", v.quantize_mx)
+    act, mm = on("s", g.scalar.activation), on("t", g.tensor.matmul_mx)
 
     def iota(out, pat, base, cm=0):
-        return done("gp", g.iota(out, pat, base, cm, allow_small_or_imprecise_dtypes=True))
+        return on("gp", g.iota)()(out, pat, base, cm, allow_small_or_imprecise_dtypes=True)
 
-    k_pa = done("gp", g.iota(T.pa[:], [[0, 1]], 0, 129))
-    k_pb = done("gp", g.iota(T.pb[:], [[0, 1]], 0, 17))
-    k_vraw = iota(T.vraw[:], [[32, 8], [1, 16]], 128)
-    k_fj = iota(T.fj[:], [[0, 2], [1, 32]], 0, 32)
+    def send(dst, out, in_, sem, local, after):
+        need("gp", *after)
+        rid, pid, _ = topo.addr(T.cores[dst])
+        g.remote_dma(out, in_, S[sem], S[local], pid, rid, topo.mask(core, T.cores[dst]))
+        left[local] += len(topo.engines(core, T.cores[dst]))
 
-    k_zt = V(g.vector.memset(T.zt[:, 0:208], 0.0))
-    need("s", "v", k_zt)
-    done("s", act(T.ones[:], T.zt[:, 0:32], ID, 1.0))
-    k_zz = done("s", act(T.zz[:], T.zt[:, 0:200], CP))
-    done("s", act(T.win0[:, LB - 16:LB + 144], T.zt[:, 0:160], ID, 128.0))
-    k_m0 = done("s", act(T.m01[:], T.zt[:, 0:32], CP))
+    def copy(i, a, j, b, count, sem, *after):
+        for w in after:
+            need("y", *w)
+        g.sync.dma_start(T["q%d" % i][:, a:a + count].bitcast(dt.uint8), T["q%d" % j][:, b:b + count].bitcast(dt.uint8)).then_inc(S[sem], 16)
+        g.sync.dma_start(T["s%d" % i][:, a:a + count], T["s%d" % j][:, b:b + count]).then_inc(S[sem], 16)
 
-    def bits(c, src, shift, mask):
-        need("v", "gp", k_pb if c == 1 else k_pa)
-        if shift:
-            return V(ts(T.bi[:, c:c + 1], src[:], shift, mask, A.logical_shift_right, A.bitwise_and))
-        return V(ts(T.bi[:, c:c + 1], src[:], mask, None, A.bitwise_and))
+    def pick(qo, so, qi, si, off, vwaits, swaits):
+        return cp(*vwaits)(qo.bitcast(dt.uint32), qi.bitcast(dt.uint32).indirect(off)), act(*swaits)(so, si.indirect(off), CP)
 
-    bits(0, T.pa, 0, 16)
-    bits(2, T.pa, 1, 7)
-    bits(3, T.pa, 0, 31)
-    bits(4, T.pa, 0, 15)
-    k_bi = bits(1, T.pb, 4, 1)
-    V(g.vector.memset(T.xt[:, 0:8], 0.0))
-    vv(k_bi)
-    k_bf = V(cp(T.bf[:, 0:5], T.bi[:, 0:5]))
-    ei = T.bf[:, 2:3]
+    def scatter(i, first, places, *after):
+        return cp(*after)(T["win%d" % i][:, 16 + first:WIN].indirect(places), T.vr[:])
 
+    def turn(i, count, back, *after):
+        w, t = T["win%d" % i], T["tr%d" % i]
+        if back:
+            return tp(*after)(t[:, count:2 * count + 32], w[:, 0:count + 32])
+        return tp(*after)(t[:, 0:count], w[:, 16:16 + count])
+
+    def join(i, count, ks, rows=slice(0, 128)):
+        t, z, nb = T["tr%d" % i], T["z%d" % i], count // 32
+        tt(ks[0])(z[rows, 1:2 * nb:2], t[rows, 0:count:32], t[rows, 16:count:32], A.min)
+        return tt(ks[1])(z[rows, 0:2 * nb + 1:2], t[rows, count:2 * count + 32:32], t[rows, count + 16:2 * count + 32:32], A.min)
+
+    def lift(i, *after):
+        return ts(*after)(T["c%d" % i][:], T["z%d" % i][:], T.cc[:, 1:2], None, A.subtract)
+
+    def halve(i, k):
+        c = T["c%d" % i]
+        return tt(k)(T["h%d" % i][0:64, :], c[0:64, :], c[64:128, :], A.min)
+
+    def spread(i, k):
+        h, m = T["h%d" % i], T["m%d" % i]
+        return [tt(k)(m[block(a), :], h[0:32, :], h[32:64, :], A.min) for a in range(4)][-1]
+
+    def blank(w, count, value, *after):
+        for a in range(0, count, 256):
+            b = min(count, a + 256)
+            k = act(*after)(w[:, a:b], T.ramp[:, 0:b - a], ID, value, 0.0)
+        return k
+
+    mine = slice(32 * p4, 32 * p4 + 16)
+    for e, queue in enumerate((g.sync, g.scalar)):
+        queue.dma_start(T.dmx[32 * p4 + 16 * e:32 * p4 + 16 * e + 16, mine], T.dm[:]).then_inc(S.ld, 16)
+    g.sync.dma_start(T.xt[:, 8:1032], T.x[:]).then_inc(S.lx, 16)
+
+    k_ramp = iota(T.ramp[:], [[1, 256]], 0)
+    fill()(T.two[:], 2.0)
+    k = fill()(T.pr[:, 24:56], 0.0)
+    for rows in ((block(1), side(2)), (block(0), side(2)), (side(0), block(3)), (slice(0, 96),))[p4]:
+        k_dm = fill()(T.dmx[rows, mine], 0)
+    scan(k)(T.pr[:, 0:24], T.two[:], T.pr[:, 32:56], 0.5, A.mult, A.add)
+    for rows, s, power in ((side(pa), S1, TWO - (p4 ^ 2)), (side(pb), S1, -2), (block(o), SP, FOUR - par), (side(pb), SP, TWO - p4)):
+        k = fill()(T.pr[rows, s:s + 1], 2.0 ** power)
+    k = tp(k)(T.pw[:], T.pr[:, 0:32])
+    fill()(T.ab[:, 256:257], 1.0 - BIG)
+    k = ts(k, k_ramp)(T.ti[:], T.ramp[:], T.pw[:, 0:1], None, A.mult)
+    fill()(T.ab[:, 257:288], 0.0)
+    k = ts(k)(T.ti[:], T.ti[:], SETS, None, A.bitwise_and)
+    fill()(T.ab[:, 544:576], 0.0)
+    k_tf = ts(k)(T.tf[:], T.ti[:], T.pw[:, 0:1], None, A.is_ge)
+
+    iota(T.ci[:, 128:160], [[0, 2], [1, 16]], 0, 1)
     peers = [q ^ 1, q ^ 2, q ^ 3]
-    g.wait_ge(S.ld, 128)
-    m = topo.mask(core, to(peers[0]))
-    ids = []
+    m, ids = topo.mask(core, T.cores[peers[0]]), []
     for d in peers:
-        m &= topo.mask(core, to(d))
-        rid, pid, _ = topo.addr(to(d))
+        m &= topo.mask(core, T.cores[d])
+        rid, pid, _ = topo.addr(T.cores[d])
         ids.append(DstId(rid=rid, pnc=pid))
-    g.remote_dma_fused([RemoteDMATransfer(dst_ids=ids, dma_engine_mask=m, remote_sem=S.mk, srcs=[T.dmx[:, own]],
-                                          dsts=[T.dmx[:, own] for d in peers])], local_sem=S.lo)
-    n_lo[0] += bin(m).count("1")
-    k_c8 = iota(T.c8[:], [[32, 8]], 129)
-    k_ramp = iota(T.ramp[:, 129:385], [[1, 256]], 128)
-    if half == 0:
-        k_gp3 = iota(T.uif[:], [[16, 32]], -256)
-    else:
-        k_gp3 = iota(T.win3[:, LB:LB + 256], [[1, 256]], -256)
+    need("gp", *k_dm)
+    g.wait_ge(S.ld, 32)
+    g.remote_dma_fused([RemoteDMATransfer(dst_ids=ids, dma_engine_mask=m, remote_sem=S.mk, srcs=[T.dmx[:, mine]],
+                                          dsts=[T.dmx[:, mine] for d in peers])], local_sem=S.l0)
+    left["l0"] += bin(m).count("1")
 
-    def turn(i, count):
-        return V(tp(T["tr%d" % i][:], T["win%d" % i][:, LB:LB + count]))
-
-    def spread(i, count, k):
-        tr, z, nb, sem = T["tr%d" % i], T["z%d" % i], count // 32, "d%d" % i
-        vv(k)
-        k = V(tt_(z[:, 0:nb], tr[:, 0:count:32], tr[:, 16:count:32], A.max))
-        need("y", "v", k)
-        need("s", "v", k)
-        for s in range(1, 8):
-            c, a = slice(nb * s, nb * s + nb), 16 * s
-            g.sync.dma_start(z[0:128 - a, c], z[a:128, 0:nb]).then_inc(S[sem], 16)
-            g.scalar.dma_start(z[128 - a:128, c], z[0:a, 0:nb]).then_inc(S[sem], 16)
-
-    def merge(i, count, out, fill=()):
-        z, h, nb = T["z%d" % i], T["h%d" % i], count // 32
-        need("v", "d%d" % i, 224)
-        k = V(tt_(h[:], z[:, 0:4 * nb], z[:, 4 * nb:8 * nb], A.max))
-        if fill:
-            fill[0]()
-        vv(k)
-        k = V(tt_(out, h[:, 0:2 * nb], h[:, 2 * nb:4 * nb], A.max))
-        if fill:
-            fill[1]()
-        vv(k)
-
-    def pick(qo, so, qi, si, off, k_off, vwaits=(), swaits=()):
-        vv(k_off)
-        for w in vwaits:
-            need("v", *w)
-        a = V(cp(qo.bitcast(dt.uint32), qi.bitcast(dt.uint32).indirect(off)))
-        need("s", "v", k_off)
-        for w in swaits:
-            need("s", *w)
-        return a, done("s", act(so, si.indirect(off), CP))
-
-    def lift(out, sel, k):
-        need("s", "v", k)
-        return done("s", act(out, sel, CP, 0.0, float(LB - 1)))
-
-    def last_gather(c, nb):
-        return V(ts(T.gl[:, c:c + 1], T.bf[:, 1:2], nb, ei, A.mult, A.add))
-
-    need("v", "ld", 128)
-    k = V(ts(T.and0[:], T.dmx[:, 16 * p4:16 * p4 + 15:2], wanters(q, 0), None, A.bitwise_and))
-    bits(5, T.pa, 5, 15)
-    vv(k)
-    k = V(ts(T.sel0[:], T.and0[:], 0.0, None, A.is_gt))
-    kb = lift(T.lf0[:], T.sel0[:], k)
-    k_bi = bits(6, T.pa, 5, 31)
-    need("s", "v", k_bf)
-    need("s", "gp", k_vraw)
-    k_v1 = done("s", act(T.v1r[:], T.vraw[:], ID, T.bf[:, 0:1]))
-    k1 = done("s", act(T.res[:], T.zt[:, 0:104], ID, 1.0))
-    vv(k)
-    need("v", "s", k_zz)
-    k = V(scan(T.zz[:, 0:8], T.ones[:, 0:8], T.sel0[:], 0.0, A.mult, A.add))
-    vv(k_bf)
-    k_c5 = V(ts(T.c5[:], T.bf[:, 0:1], -0.0625, 5.0, A.mult, A.add))
-    vv(k)
-    k = V(tp(T.x0t[:], T.zz[:, 0:32]))
-    need("v", "s", kb)
-    ka = V(tt_(T.ya0[:], T.zz[:, 0:8], T.lf0[:], A.add))
-    vv(k)
-    k = V(scan(T.zz[:, 73:104], T.ones[:, 0:31], T.x0t[:, 0:31], 0.0, A.mult, A.add))
-    vv(ka)
-    need("v", "gp", k_fj)
-    V(tt_(T.yc0[:], T.ya0[:], T.fj[:, 0:8], A.max))
-    vv(k)
-    k = V(tp(T.bs0[:], T.zz[:, 72:104]))
-    V(cp(T.gl[:, 8:12:2], T.bi[:, 5:7]))
-    vv(k)
-    k = V(ts(T.p0[:], T.yc0[:], T.bs0[:, 7:8], None, A.add))
-    V(ts(T.gl[:, 0:1], T.bf[:, 1:2], T.c5[:], ei, A.mult, A.add))
-    need("y", "v", k)
+    iota(T.ci[:, 0:32], [[0, 2], [s2 - s3, 2], [32, 8]], s3)
+    iota(T.ci[:, 32:64], [[0, 2], [s0 - S1, 2], [32, 8]], S1)
+    iota(T.ci[:, 64:96], [[-1, 2], [1, 16]], 1)
+    k_ci = iota(T.ci[:, 96:128], [[-1, 2], [1, 16]], 17)
+    k_fj = iota(T.fj[:], [[0, 4], [1, 8]], TRASH, 8)
+    fill()(T.xt[:, 0:8], 0.0)
+    fill()(T.z0[:, 9:17], 0.0)
+    k_x = fill()(T.ex[0:32, :], 0.0)
+    k = tp(k_ci)(T.ct[:], T.ci[:])
+    k_q = quant(k_x, ("lx", 16))(T.q0[:, 30:288], T.s0[:, 30:288], T.xt[:])
+    k_gl = cp(k)(T.gls[:, 0:5], T.ct[:, 0:160:32])
+    last = T.gls[:, 2:4]
+    copy(1, 0, 0, 31, 257, "c1", k_q, ("l0", left["l0"]))
+    copy(2, 0, 0, 31, 257, "c2")
+    copy(3, 256, 0, 31, 257, "c3")
     g.sync.dma_start(T.wt[:], T.w[:]).then_inc(S.lw, 16)
-    vv(k)
-    need("v", "s", k_v1)
-    k_w0 = V(cp(T.win0[:].indirect(T.p0[:]), T.v1r[:]))
-    need("v", "lx", 16)
-    V(g.vector.quantize_mx(T.q0[:, 126:384], T.s0[:, 126:384], T.xt[:]))
-    need("s", "s", k1)
-    done("s", act(T.res[:, 16:33:16], T.zt[:, 0:2], CP))
-    done("s", act(T.res[:, 72:73], T.zt[:, 0:1], CP))
-    need("s", "gp", k_c8)
-    k_res = done("s", act(T.sel[:, 104 + 8 * p4:112 + 8 * p4], T.c8[:], ID, T.bf[:, 3:4]))
-    need("s", "gp", k_ramp)
-    done("s", act(T.ramp[:, 0:129], T.ramp[:, 129:258], ID, 255.0))
-    k_rs = done("s", act(T.ramp[:, 385:577], T.ramp[:, 129:321], ID, 384.0))
-    k_ui = done("s", act(T.win1[:, LB:LB + 192], T.zt[:, 0:192], ID, 128.0))
-    if half == 0:
-        need("s", "gp", k_gp3)
-        k_ui = done("s", act(T.ui[:], T.uif[:], ID, T.bf[:, 4:5]))
-    vv(k_w0)
-    V(tp(T.tr0[:, 0:128], T.win0[:, LB:LB + 128]))
-    k0 = V(tp(T.tr0[:, 128:288], T.win0[:, LB - 16:LB + 144]))
-    last_gather(2, 6.0)
-    last_gather(4, 8.0)
-    vv(k0)
-    need("v", "s", k_m0)
-    k0 = V(tt_(T.m01[:, 0:9], T.tr0[:, 0:288:32], T.tr0[:, 16:288:32], A.max))
-    last_gather(6, 16.0)
-    vv(k0)
-    k0 = V(cp(T.off0[:], T.m01[:, 0:16].indirect(T.gl[:, 0:1])))
-    V(g.vector.memset(T.zt[:, 208:512], 0.0))
-    k0, ks = pick(T.slq0[:], T.sls0[:], T.q0[:], T.s0[:], T.off0[:, 0:8], k0)
-    need("gp", "v", k0)
-    send(q ^ 1, T.q1[:, 384:512].bitcast(dt.uint8), T.slq0[:].bitcast(dt.uint8), "r0c")
-    need("gp", "s", ks)
-    send(q ^ 1, T.s1[:, 384:512], T.sls0[:], "r0s")
-    copy(T.q1[:, 128:384], T.q0[:, 128:384], T.s1[:, 128:384], T.s0[:, 128:384], "c1", (("v", k0),), (("s", ks),))
+    blank(T.win0, 160, 0.0, k_ramp)
+    for rows, c, value in ((slice(0, 128), 0, -1.0), (block(p4), 1, 0.0), (block(o), 1, 256.0), (side(pb), 1, 384.0)):
+        k_cc = act()(T.cc[rows, c:c + 1], T.ramp[rows, 0:1], ID, value)
+    blank(T.win1, 544, BIG)
 
-    pa, pb, o = 2 * (p4 >> 1), 2 * (1 - (p4 >> 1)), p4 ^ 1
-    share1, share = T.gl[:, 8:9], T.gl[:, 10:11]
-    need("v", "mk", 48)
-    V(ts(T.and1[:, 0:16], T.dmx[:, 16 * pa:16 * pa + 31:2], wanters(q, 1), None, A.bitwise_and))
-    V(ts(T.and1[:, 16:32], T.dmx[:, 16 * pb:16 * pb + 31:2], wanters(q ^ 2, 1), None, A.bitwise_and))
-    k = V(ts(T.and1[:, 32:40], T.dmx[:, 16 * o:16 * o + 15:2], wanters(q ^ 1, 0), None, A.bitwise_and))
-    V(ts(T.and1[:, 40:72], T.dmx[:, 0:63:2], 1 << (q ^ 4), None, A.bitwise_and))
-    vv(k)
-    k = V(ts(T.sel[:, 0:40], T.and1[:, 0:40], 0.0, None, A.is_gt))
-    kb = lift(T.lf1[:], T.sel[:, 0:16], k)
-    kc = V(ts(T.and1[:, 72:104], T.dmx[:, 0:63:2], 1 << q, None, A.bitwise_and))
-    vv(k)
-    need("v", "s", k_res)
-    k = V(scan(T.zz[:, 32:72], T.res[:, 0:40], T.sel[:, 0:40], 0.0, A.mult, A.add))
-    vv(kc)
-    kc = V(ts(T.sel[:, 40:104], T.and1[:, 40:104], 0.0, None, A.is_gt))
-    vv(k)
-    k = V(tp(T.x1t[:], T.zz[:, 40:72]))
-    need("v", "s", kb)
-    ka = V(tt_(T.ya1[:], T.zz[:, 32:48], T.lf1[:], A.add))
-    vv(k)
-    k = V(scan(T.zz[:, 105:136], T.ones[:, 0:31], T.x1t[:, 0:31], 0.0, A.mult, A.add))
-    vv(kc)
-    k_tt = V(tp(T.tt[:, 0:64], T.sel[:, 40:104]))
-    k_lf = lift(T.lf2[:], T.tt[:, 0:64], k_tt)
-    vv(k)
-    k_bs = V(tp(T.bs1[:], T.zz[:, 104:136]))
-    vv(ka)
-    ka = V(tt_(T.yc1[:], T.ya1[:], T.fj[:, 0:16], A.max))
-    vv(k_bs)
-    V(ts(T.sel[:, 104 + 8 * o:112 + 8 * o], T.zz[:, 64:72], T.bs1[:, 31:32], None, A.add))
-    k = V(ts(T.sel[:, 104 + 8 * pb:120 + 8 * pb], T.zz[:, 48:64], T.bs1[:, 23:24], 384.0, A.add, A.add))
-    vv(ka)
-    k_p1 = V(ts(T.p1[:], T.yc1[:].indirect(share1), T.bs1[:, 7:8], None, A.add))
-    vv(k)
-    k = V(cp(T.st1[:], T.sel[:, 104 + 8 * pa:120 + 8 * pa].indirect(share1)))
-    need("s", "v", k)
-    need("s", "s", k_rs)
-    k_vr1 = done("s", act(T.vr1[:], T.ramp[:].indirect(T.st1[:, 0:4]), CP))
-    kt = V(tp(T.tt[:, 64:96], T.sel[:, 104:136]))
-    kc = V(scan(T.inc2[:], T.res[:, 40:104], T.tt[:, 0:64], 0.0, A.mult, A.add))
-    vv(kt)
-    k = V(cp(T.st[:], T.tt[:, 64:96].indirect(share)))
-    need("v", "s", k_vr1)
-    k_w1 = V(cp(T.win1[:].indirect(T.p1[:, 0:4]), T.vr1[:]))
-    need("s", "v", k)
-    k_vr = done("s", act(T.vr2[:], T.ramp[:].indirect(T.st[:, 0:8]), CP))
-    k_f2 = done("s", act(T.win2[:, LB:LB + 256], T.zt[:, 0:256], ID, float(ZERO)))
-    vv(kc)
-    k_x2 = V(tp(T.x2t[:], T.inc2[:]))
-    vv(k_w1)
-    k_t1 = turn(1, 192)
-    need("v", "s", k_lf)
-    ka = V(tt_(T.ya2[:], T.inc2[:], T.lf2[:], A.add))
-    spread(1, 192, k_t1)
-    V(scan(T.zz[:, 137:168], T.ones[:, 0:31], T.x2t[:, 0:31], 0.0, A.mult, A.add))
-    k = V(scan(T.zz[:, 169:200], T.ones[:, 0:31], T.x2t[:, 32:63], 0.0, A.mult, A.add))
-    need("s", "v", k)
-    for c in range(2):
-        b = 32 * c
-        kn = done("s", act(T.tn[:, b:b + 32], T.ones[:], ID, T.x2t[:, b + 31:b + 32], T.zz[:, b + 167:b + 168]))
-    if half == 0:
-        k_fill = done("s", act(T.win3[:, LB:LB + 512], T.zt[:], ID, -1000.0))
-    else:
-        k_fill = done("s", act(T.win3[:, LB + 256:LB + 512], T.zt[:, 0:256], CP))
-    copy(T.q2[:, 126:384], T.q0[:, 126:384], T.s2[:, 126:384], T.s0[:, 126:384], "cr")
-    copy(T.q3[:, 256:258], T.q0[:, 126:128], T.s3[:, 256:258], T.s0[:, 126:128], "c3")
-    vv(ka)
-    ka = V(tt_(T.yc2[:], T.ya2[:], T.fj[:], A.max))
-    vv(k)
-    k = V(tp(T.bs2[:], T.zz[:, 136:200]))
-    vv(k)
-    k_p2 = V(ts(T.p2[:], T.yc2[:, 0:32].indirect(share), T.bs2[:, 31:32], None, A.add))
-    if half == 0:
-        V(ts(T.p3[:], T.yc2[:, 32:64].indirect(share), T.bs2[:, 63:64], None, A.add))
-    vv(k_p2)
-    need("v", "s", k_f2)
-    k_w2 = V(cp(T.win2[:].indirect(T.p2[:, 0:8]), T.vr2[:]))
-    need("v", "s", kn)
-    k_n = V(tp(T.tnt[:], T.tn[:]))
-    nh = T.tnt[:, 63:64]
-    need("gp", "v", k_n)
-    send(q ^ 4, T.n2[:], T.tnt[:, 31:32], "rn")
-    vv(k_w2)
-    k_t2 = turn(2, 256)
-    if half == 0:
-        need("v", "s", k_ui)
-        vv(k_n)
-        V(ts(T.ub[:], T.ui[:], nh, 0.0, A.subtract, A.min))
-    spread(2, 256, k_t2)
-    copy(T.q2[:, 384:512], T.q1[:, 384:512], T.s2[:, 384:512], T.s1[:, 384:512], "cr", (("r0c", 16),), (("r0s", 16),))
-    copy(T.q3[:, 640:768], T.q1[:, 384:512], T.s3[:, 640:768], T.s1[:, 384:512], "c3")
-    merge(1, 192, T.m01[:, 16:28])
-    k_off1 = V(cp(T.off1[:], T.m01[:, 16:32].indirect(T.gl[:, 2:3])))
-    ka, ks = pick(T.slq1[:], T.sls1[:], T.q1[:], T.s1[:], T.off1[:, 0:12], k_off1,
-                  (("c1", 32), ("r0c", 16)), (("c1", 32), ("r0s", 16)))
-    need("gp", "v", ka)
-    send(q ^ 2, T.q2[:, 512:704].bitcast(dt.uint8), T.slq1[:].bitcast(dt.uint8), "r1c")
-    need("gp", "s", ks)
-    send(q ^ 2, T.s2[:, 512:704], T.sls1[:], "r1s")
+    k = cp(k_gl, ("ld", 32), ("mk", 3 * bin(m).count("1")))(T.dmu[:], T.dmx[:].indirect(T.gls[:, 4:5]))
+    ka = ts(k, k_tf)(T.ab[:, 0:256], T.tf[:].indirect(T.dmu[:]), 1.0 - BIG, None, A.mult)
+    kb = act(k)(T.ab[:, 288:544], T.tf[:].indirect(T.dmu[:]), CP, 0.0, BIG)
+    k = scan(ka, kb)(T.zs[:], T.ab[:, 0:288], T.ab[:, 287:575], BIG - 1.0, A.add, A.add)
+    k_tr = tp(k)(T.tr[:], T.zs[:])
+    k_st = ts(k_tr)(T.st[:], T.tr[:, SP:256:32], 255.0, None, A.min)
+    k_y = tt(k_fj)(T.yy[:], T.tr[:].indirect(T.gls[:, 0:2]), T.fj[:], A.min)
+    k = act(k_tr, k_cc)(T.cc[block(pb + 1), 0:1], T.tr[block(pb), 256 + SP:257 + SP], ID, -1.0, -1.0)
+    k_e1 = act()(T.ex[block(1), :], T.tr[block(0), 256:288], CP)
+    k_vr = act(k, k_st)(T.vr[:], T.ramp[:].indirect(T.st[:]), ID, T.cc[:, 0:1], -1.0)
+    k_w3 = blank(T.win3, 544, BIG)
+    k_e = tt()(T.ex[block(2), :], T.tr[block(0), 256:288], T.tr[block(1), 256:288], A.add)
+    k = cp(k_y)(T.p0[:], T.yy[:, 24:32])
+    k_e = tt(k_e)(T.ex[block(3), :], T.ex[block(2), :], T.tr[block(2), 256:288], A.add)
+
+    k_s0 = scatter(0, 0, T.p0[:], k, k_vr)
+    lo = min(s2, s3)
+    k = tt(k_e)(T.tot[block(3), :], T.ex[block(3), lo:lo + 5:4], T.tr[block(3), 256 + lo:261 + lo:4], A.add)
+    k_nn = on("gp", g.partition_broadcast)(k)(T.nn[:], T.tot[96:97, :], 128)
+    c2, c3 = (s2 - lo) // 4, (s3 - lo) // 4
+    nh = T.nn[:, c3:c3 + 1]
+    send(q ^ 4, T.n2[:], T.nn[:, c2:c2 + 1], "rn", "lo", k_nn)
+    ks = turn(0, 128, False, k_s0), turn(0, 128, True)
+    k_p1 = ts(k_e1)(T.p1[:], T.yy[:, 16:24], T.ex[:, S1:S1 + 1], None, A.add)
+    k = join(0, 128, ks, block(p4))
+    k_p2 = ts()(T.p2[:], T.yy[:, 8:16], T.ex[:, s2:s2 + 1], None, A.add)
+    kc = act(k)(T.z0[block(p4 ^ 3), 0:9], T.z0[block(p4), 0:9], CP)
+    cp(k)(T.z0[block(p4 ^ 1), 0:9], T.z0[block(p4), 0:9])
+    k = cp()(T.z0[block(p4 ^ 2), 0:9], T.z0[block(p4), 0:9])
+    k_s1 = scatter(1, 0, T.p1[:], k_p1)
+    k = ts(k, kc)(T.off0[:], T.z0[:].indirect(T.gls[:, 2:3]), -1.0, 31.0, A.mult, A.add)
+    k_s2 = scatter(1, 256, T.p2[:], k_p2, k_s1)
+    ka, kb = pick(T.slq0[:], T.sls0[:], T.q0[:], T.s0[:], T.off0[:, 0:8], [k], [k])
+    send(q ^ 1, T.q1[:, 257:385].bitcast(dt.uint8), T.slq0[:].bitcast(dt.uint8), "r0c", "l1", ka)
+    send(q ^ 1, T.s1[:, 257:385], T.sls0[:], "r0s", "l1", kb)
     if half:
-        need("v", "rn", 16)
-        vv(V(ts(T.p3[:], T.yc2[:, 32:64].indirect(share), T.bs2[:, 63:64], T.n2[:], A.add, A.add)))
-    need("v", "s", k_fill)
-    need("v", "gp", k_gp3)
-    vv(V(cp(T.win3[:].indirect(T.p3[:, 0:8]), T.vr2[:])))
-    spread(3, 512, turn(3, 512))
-    copy(T.q3[:, 768:960], T.q2[:, 512:704], T.s3[:, 768:960], T.s2[:, 512:704], "c3", (("r1c", 16),), (("r1s", 16),))
-
-    def length_all():
-        need("v", "rn", 16)
-        V(ts(T.lnt[:, 0:1], nh, T.n2[:], None, A.add))
-
-    def length_own():
-        need("y", "v", V(red(T.lnt[:, 1:2], T.x2t[:, 32 + 8 * p4:40 + 8 * p4], X, A.add)))
-        g.sync.dma_start(T.ln[:], T.lnt[31:32, 0:2]).then_inc(S.lnd, 16)
-
-    merge(2, 256, T.m2[:], (length_all, length_own))
-    k_off2 = V(cp(T.off2[:], T.m2[:].indirect(T.gl[:, 4:5])))
-    ka, ks = pick(T.slq2[:], T.sls2[:], T.q2[:], T.s2[:], T.off2[:], k_off2, (("cr", 64), ("r1c", 16)), (("cr", 64), ("r1s", 16)))
-    need("gp", "v", ka)
-    send(q ^ 4, T.q3[:, 0:256].bitcast(dt.uint8), T.slq2[:].bitcast(dt.uint8), "r2c")
-    need("gp", "s", ks)
-    send(q ^ 4, T.s3[:, 0:256], T.sls2[:], "r2s")
-
-    k_wq = []
-
-    def quant_w():
-        need("v", "lw", 16)
-        k_wq.append(V(g.vector.quantize_mx(T.wq[:], T.ws[:], T.wt[:])))
-
-    def quant_x():
-        V(g.vector.quantize_mx(T.q3[:, 384:640], T.s3[:, 384:640], T.xt[:, 8:1032]))
-
-    merge(3, 512, T.m3[:], (quant_x, quant_w))
-    lo3, hi3 = T.m3[:, 0:24].indirect(T.gl[:, 6:7]), T.m3[:, 8:32].indirect(T.gl[:, 6:7])
-    if half == 0:
-        V(tt_(T.tm[:, 0:16], lo3, T.ub[:, 0:16], A.max))
-        vv(V(tt_(T.tm[:, 16:32], hi3, T.ub[:, 16:32], A.max)))
-        k_off3 = V(ts(T.off3[:], T.tm[:], 256.0, None, A.add))
+        act(k_w3)(T.win3[block(p4), 16:272], T.ramp[block(p4), :], RELU, 256.0, -1.0)
+        k_w3 = act()(T.win3[block(p4), 272:528], T.ramp[block(p4), :], RELU, 0.0, -1.0)
     else:
-        V(cp(T.off3[:, 16:32], hi3))
-        k_off3 = V(ts(T.off3[:, 0:16], lo3, 256.0, None, A.add))
+        k = act(k_nn)(T.cc[:, 2:3], nh, ID, 256.0)
+        act(k_w3)(T.win3[block(p4), 272:528], T.ramp[block(p4), :], RELU, T.nn[block(p4), c3:c3 + 1], -1.0)
+        k_w3 = act(k)(T.win3[block(p4), 16:272], T.ramp[block(p4), :], RELU, T.cc[block(p4), 2:3], -1.0)
+    act(k_nn, ("rn", 16))(T.lnt[:, 0:1], nh, ID, T.n2[:])
+    need("y", *act()(T.lnt[block(p4), 1:2], T.tr[block(p4), 256 + s3:257 + s3], CP))
+    g.sync.dma_start(T.ln[:], T.lnt[32 * p4:32 * p4 + 1, 0:2]).then_inc(S.lnd, 16)
 
-    def product(i, a, b, lo, vwaits, swaits):
-        w_ = b - a
-        ka, kb = pick(T.qa[:, a:b], T.sa[:, a:b], T.q3[:, lo:960], T.s3[:, lo:960], T.off3[:, a // 16:b // 16], k_off3,
-                      vwaits, swaits)
-        need("t", "v", ka)
-        need("t", "s", kb)
+    ks = turn(1, 512, False, k_s2), turn(1, 512, True)
+    k = join(1, 512, ks)
+    k = spread(1, halve(1, lift(1, k)))
+    k = ts(k)(T.off1[:], T.m1[:].indirect(last), -1.0, None, A.mult)
+    if half:
+        k_p3 = ts(("rn", 16))(T.p3[:], T.yy[:, 0:8], T.ex[:, s3:s3 + 1], T.n2[:], A.add, A.add)
+    else:
+        k_p3 = ts()(T.p3[:], T.yy[:, 0:8], T.ex[:, s3:s3 + 1], None, A.add)
+    ka, kb = pick(T.slq1[:], T.sls1[:], T.q1[:], T.s1[:], T.off1[:, 0:12],
+                  [k, ("c1", 32), ("r0c", 16)], [k, ("c1", 32), ("r0s", 16)])
+    send(q ^ 2, T.q2[:, 385:577].bitcast(dt.uint8), T.slq1[:].bitcast(dt.uint8), "r1c", "l2", ka)
+    send(q ^ 2, T.s2[:, 385:577], T.sls1[:], "r1s", "l2", kb)
+    copy(2, 257, 1, 257, 128, "c2", ("r0c", 16), ("r0s", 16))
+    copy(3, 513, 1, 257, 128, "c3")
+
+    k = scatter(3, 0, T.p3[:], k_p3, k_w3)
+    k_wq = quant(("lw", 16))(T.wq[:], T.ws[:], T.wt[:])
+    ks = turn(3, 512, False, k), turn(3, 512, True)
+    ka, kb = pick(T.slq2[:], T.sls2[:], T.q2[:], T.s2[:], T.off1[:, 16:32], [("c2", 64), ("r1c", 16)], [("c2", 64), ("r1s", 16)])
+    send(q ^ 4, T.q3[:, 0:256].bitcast(dt.uint8), T.slq2[:].bitcast(dt.uint8), "r2c", "lo", ka)
+    send(q ^ 4, T.s3[:, 0:256], T.sls2[:], "r2s", "lo", kb)
+    copy(3, 641, 2, 385, 192, "c3", ("r1c", 16), ("r1s", 16))
+    k = spread(3, halve(3, lift(3, join(3, 512, ks))))
+    if half:
+        ts(k)(T.off3[:, 16:32], T.m3[:, 16:33].indirect(T.gls[:, 2:3]), -1.0, None, A.mult)
+        k_off3 = ts()(T.off3[:, 0:16], T.m3[:].indirect(T.gls[:, 2:3]), -1.0, 256.0, A.mult, A.add)
+    else:
+        k_off3 = ts(k)(T.off3[:], T.m3[:].indirect(last), -1.0, 256.0, A.mult, A.add)
+
+    def product(i, a, b, lo):
+        w_, held = b - a, [k_off3, ("c3", 96)]
+        ka, kb = pick(T.qa[:, a:b], T.sa[:, a:b], T.q3[:, lo:833], T.s3[:, lo:833], T.off3[:, a // 16:b // 16],
+                      held + [("r2c", 16)] * (lo == 0), held + [("r2s", 16)] * (lo == 0))
         for w in range(2):
             e = 512 * (2 * i + w)
-            done("t", g.tensor.matmul_mx(T.ps[:, e:e + w_], T.wq[:, 128 * w:128 * w + 128],
-                                         T.ws[:, 128 * w:128 * w + 128], T.qa[:, a:b], T.sa[:, a:b], True, True))
-        return n["t"]
+            k = mm(k_wq, ka, kb)(T.ps[:, e:e + w_], T.wq[:, 128 * w:128 * w + 128], T.ws[:, 128 * w:128 * w + 128],
+                                 T.qa[:, a:b], T.sa[:, a:b], True, True)
+        return k
 
-    def store(a, b, i, k):
+    def store(i, a, b, k):
         e, w_ = 1024 * i, b - a
-        need("v", "t", k - 1)
-        need("s", "t", k)
-        ka = V(cp(T.ys[:, a:b], T.ps[:, e:e + w_]))
-        kb = done("s", act(T.ys[:, 512 + a:512 + b], T.ps[:, e + 512:e + 512 + w_], CP))
-        need("y", "v", ka)
+        ka = cp(("t", k[1] - 1))(T.ys[:, a:b], T.ps[:, e:e + w_])
+        kb = act(k)(T.ys[:, 512 + a:512 + b], T.ps[:, e + 512:e + 512 + w_], CP)
+        need("y", *ka)
         g.sync.dma_start(T.y[:, a:b], T.ys[:, a:b]).then_inc(S.yo, 16)
-        need("y", "s", kb)
+        need("y", *kb)
         g.sync.dma_start(T.y[:, 512 + a:512 + b], T.ys[:, 512 + a:512 + b]).then_inc(S.yo, 16)
         n_yo[0] += 32
 
-    need("t", "v", k_wq[0])
-    held, r2 = ("c3", 96), (("r2c", 16), ("r2s", 16))
-    runs = [(0, 128, 0), (128, 384, 0), (384, 512, 0)] if half == 0 else [(256, 512, 256), (0, 128, 0), (128, 256, 0)]
-    ends = [product(i, a, b, lo, [held] + [r2[0]] * (lo == 0), [held] + [r2[1]] * (lo == 0)) for i, (a, b, lo) in enumerate(runs)]
+    runs = [(256, 512, 256), (0, 128, 0), (128, 256, 0)] if half else [(0, 128, 0), (128, 384, 0), (384, 512, 0)]
+    ends = [product(i, *r) for i, r in enumerate(runs)]
     for i, (a, b, lo) in enumerate(runs):
-        store(a, b, i, ends[i])
+        store(i, a, b, ends[i])
 
-    for kind in ("v", "s", "t"):
+    for kind in ("v", "s", "t", "gp"):
         need("gp", kind, n[kind])
-    g.wait_ge(S.gp, n["gp"])
-    g.wait_ge(S.lo, n_lo[0])
+    for sem in left:
+        need("gp", sem, left[sem])
     g.wait_ge(S.yo, n_yo[0])
     g.wait_ge(S.lnd, 16)

@@ -4,10 +4,12 @@ from concourse.mybir import dt, AluOpType, ActivationFunctionType
 F32, I32, BF, U16, U8, Q8 = "float32", "int32", "bfloat16", "uint16", "uint8", "float8_e4m3fn_x4"
 BIG = 4096.0
 TRASH = 528
-WIN = 2352
+WIN = 2112
 ONE, TWO, FOUR = 7, 15, 23
 SETS = 2 ** ONE + (2 ** TWO + 2 ** (TWO + 4)) + sum(2 ** (FOUR + 2 * i) for i in range(4))
-S1, SP = 24, 25
+SP, SQ = 24, 25
+FIRST0 = 544
+RUNS = (((0, 128), (128, 256), (256, 384), (384, 512)), ((256, 384), (384, 512), (0, 128), (128, 256)))
 
 
 def _s(n, d):
@@ -24,9 +26,9 @@ SCRATCH = {
     "two": _s(24, F32), "pr": _s(56, F32), "pw": _s(32, F32), "ramp": _s(256, F32), "ti": _s(256, I32), "tf": _s(256, BF),
     "ci": _s(160, BF), "ct": _s(160, BF), "fj": _s(32, F32), "cc": _s(4, F32), "gls": _s(6, U16),
     "ab": _s(576, F32), "zs": _s(288, BF), "tr": _s(288, BF), "ex": _s(32, F32), "tot": _s(2, F32), "nn": _s(2, F32),
-    "st": _s(8, U16), "vr": _s(128, BF), "yy": _s(32, F32), "n2": _s(1, F32),
-    "p0": _s(8, U16), "p1": _s(8, U16), "p2": _s(8, U16), "p3": _s(8, U16),
-    "win0": _s(WIN, BF), "win1": _s(WIN, BF), "win3": _s(WIN, BF),
+    "st": _s(8, U16), "vr": _s(128, BF), "su": _s(8, U16), "vu": _s(128, BF), "yy": _s(32, F32), "n2": _s(1, F32),
+    "p1": _s(8, U16), "p2": _s(8, U16), "p3": _s(8, U16),
+    "win1": _s(WIN, BF), "win3": _s(WIN, BF),
     "tr0": _s(288, BF), "tr1": _s(1056, BF), "tr3": _s(1056, BF),
     "z0": _s(17, F32), "z1": _s(33, F32), "z3": _s(33, F32), "c1": _s(33, F32), "c3": _s(33, F32),
     "h1": _s(33, F32), "h3": _s(33, F32), "m1": _s(33, F32), "m3": _s(33, F32),
@@ -35,7 +37,7 @@ SCRATCH = {
     "ps": ("psum", [128, 4096], F32),
 }
 SEMAPHORES = ["ld", "lx", "lw", "v", "s", "t", "gp", "mk", "r0c", "r0s", "r1c", "r1s", "r2c", "r2s", "rn",
-              "c1", "c2", "c3", "l0", "l1", "l2", "lo", "yo", "lnd"]
+              "c1", "c2", "c3", "l0", "lo", "yo", "lnd"]
 
 
 def rank_program(g, core, T, topo):
@@ -47,7 +49,8 @@ def rank_program(g, core, T, topo):
     S = T.sem
     p4, half, par = q & 3, q >> 2, q & 1
     pa, pb, o = p4 & 2, 2 - (p4 & 2), p4 ^ 1
-    s0, s2, s3 = FOUR - 1 + par, ONE - (q ^ 4), ONE - q
+    s0, s1, s2, s3 = FOUR - 1 + par, TWO - (p4 ^ 2), ONE - (q ^ 4), ONE - q
+    every = slice(0, 128)
 
     def block(a):
         return slice(32 * a, 32 * a + 32)
@@ -56,7 +59,7 @@ def rank_program(g, core, T, topo):
         return slice(32 * a, 32 * a + 64)
 
     queues = {"v": g.vector, "s": g.scalar, "t": g.tensor, "gp": g, "y": g.sync}
-    n, seen, left, n_yo = {"v": 0, "s": 0, "t": 0, "gp": 0}, {}, {"l0": 0, "l1": 0, "l2": 0, "lo": 0}, [0]
+    n, seen, left, n_yo = {"v": 0, "s": 0, "t": 0, "gp": 0}, {}, {"l0": 0, "lo": 0}, [0]
 
     def need(queue, sem, count):
         if seen.get((queue, sem), 0) < count:
@@ -82,11 +85,11 @@ def rank_program(g, core, T, topo):
     def iota(out, pat, base, cm=0):
         return on("gp", g.iota)()(out, pat, base, cm, allow_small_or_imprecise_dtypes=True)
 
-    def send(dst, out, in_, sem, local, after):
+    def send(dst, out, in_, sem, after):
         need("gp", *after)
         rid, pid, _ = topo.addr(T.cores[dst])
-        g.remote_dma(out, in_, S[sem], S[local], pid, rid, topo.mask(core, T.cores[dst]))
-        left[local] += len(topo.engines(core, T.cores[dst]))
+        g.remote_dma(out, in_, S[sem], S.lo, pid, rid, topo.mask(core, T.cores[dst]))
+        left["lo"] += len(topo.engines(core, T.cores[dst]))
 
     def copy(i, a, j, b, count, sem, *after):
         for w in after:
@@ -97,19 +100,20 @@ def rank_program(g, core, T, topo):
     def pick(qo, so, qi, si, off, vwaits, swaits):
         return cp(*vwaits)(qo.bitcast(dt.uint32), qi.bitcast(dt.uint32).indirect(off)), act(*swaits)(so, si.indirect(off), CP)
 
-    def scatter(i, first, places, *after):
-        return cp(*after)(T["win%d" % i][:, 16 + first:WIN].indirect(places), T.vr[:])
+    def scatter(i, first, places, values, *after):
+        return cp(*after)(T["win%d" % i][:, 16 + first:WIN].indirect(places), values)
 
-    def turn(i, count, back, *after):
-        w, t = T["win%d" % i], T["tr%d" % i]
+    def turn(i, count, back, *after, row=None, first=0, rows=every):
+        w, t = T["win%d" % (row or i)], T["tr%d" % i]
         if back:
-            return tp(*after)(t[:, count:2 * count + 32], w[:, 0:count + 32])
-        return tp(*after)(t[:, 0:count], w[:, 16:16 + count])
+            return tp(*after)(t[rows, count:2 * count + 32], w[rows, first:first + count + 32])
+        return tp(*after)(t[rows, 0:count], w[rows, first + 16:first + 16 + count])
 
-    def join(i, count, ks, rows=slice(0, 128)):
+    def join(i, count, back, k, rows=every, to=every):
         t, z, nb = T["tr%d" % i], T["z%d" % i], count // 32
-        tt(ks[0])(z[rows, 1:2 * nb:2], t[rows, 0:count:32], t[rows, 16:count:32], A.min)
-        return tt(ks[1])(z[rows, 0:2 * nb + 1:2], t[rows, count:2 * count + 32:32], t[rows, count + 16:2 * count + 32:32], A.min)
+        if back:
+            return tt(k)(z[to, 0:2 * nb + 1:2], t[rows, count:2 * count + 32:32], t[rows, count + 16:2 * count + 32:32], A.min)
+        return tt(k)(z[to, 1:2 * nb:2], t[rows, 0:count:32], t[rows, 16:count:32], A.min)
 
     def lift(i, *after):
         return ts(*after)(T["c%d" % i][:], T["z%d" % i][:], T.cc[:, 1:2], None, A.subtract)
@@ -122,9 +126,9 @@ def rank_program(g, core, T, topo):
         h, m = T["h%d" % i], T["m%d" % i]
         return [tt(k)(m[block(a), :], h[0:32, :], h[32:64, :], A.min) for a in range(4)][-1]
 
-    def blank(w, count, value, *after):
-        for a in range(0, count, 256):
-            b = min(count, a + 256)
+    def blank(w, first, end, value, *after):
+        for a in range(first, end, 256):
+            b = min(end, a + 256)
             k = act(*after)(w[:, a:b], T.ramp[:, 0:b - a], ID, value, 0.0)
         return k
 
@@ -132,21 +136,23 @@ def rank_program(g, core, T, topo):
     for e, queue in enumerate((g.sync, g.scalar)):
         queue.dma_start(T.dmx[32 * p4 + 16 * e:32 * p4 + 16 * e + 16, mine], T.dm[:]).then_inc(S.ld, 16)
     g.sync.dma_start(T.xt[:, 8:1032], T.x[:]).then_inc(S.lx, 16)
+    g.sync.dma_start(T.wt[:], T.w[:]).then_inc(S.lw, 16)
 
     k_ramp = iota(T.ramp[:], [[1, 256]], 0)
     fill()(T.two[:], 2.0)
     k = fill()(T.pr[:, 24:56], 0.0)
     for rows in ((block(1), side(2)), (block(0), side(2)), (side(0), block(3)), (slice(0, 96),))[p4]:
         k_dm = fill()(T.dmx[rows, mine], 0)
-    scan(k)(T.pr[:, 0:24], T.two[:], T.pr[:, 32:56], 0.5, A.mult, A.add)
-    for rows, s, power in ((side(pa), S1, TWO - (p4 ^ 2)), (side(pb), S1, -2), (block(o), SP, FOUR - par), (side(pb), SP, TWO - p4)):
-        k = fill()(T.pr[rows, s:s + 1], 2.0 ** power)
-    k = tp(k)(T.pw[:], T.pr[:, 0:32])
-    fill()(T.ab[:, 256:257], 1.0 - BIG)
-    k = ts(k, k_ramp)(T.ti[:], T.ramp[:], T.pw[:, 0:1], None, A.mult)
+    ka = scan(k)(T.pr[:, 0:24], T.two[:], T.pr[:, 32:56], 0.5, A.mult, A.add)
+    act(k)(T.pr[block(o), SP:SQ + 1], T.two[block(o), 0:2], CP, 0.0, 2.0 ** (FOUR - par - 1))
+    kb = act()(T.pr[side(pb), SP:SP + 1], T.two[side(pb), 0:1], CP, 0.0, 2.0 ** (TWO - p4 - 1))
+    k_x = fill()(T.xt[:, 0:8], 0.0)
+    k = tp(ka, kb)(T.pw[:], T.pr[:, 0:32])
     fill()(T.ab[:, 257:288], 0.0)
-    k = ts(k)(T.ti[:], T.ti[:], SETS, None, A.bitwise_and)
+    k = ts(k, k_ramp)(T.ti[:], T.ramp[:], T.pw[:, 0:1], None, A.mult)
     fill()(T.ab[:, 544:576], 0.0)
+    k = ts(k)(T.ti[:], T.ti[:], SETS, None, A.bitwise_and)
+    fill()(T.ex[0:32, :], 0.0)
     k_tf = ts(k)(T.tf[:], T.ti[:], T.pw[:, 0:1], None, A.is_ge)
 
     iota(T.ci[:, 128:160], [[0, 2], [1, 16]], 0, 1)
@@ -163,61 +169,63 @@ def rank_program(g, core, T, topo):
     left["l0"] += bin(m).count("1")
 
     iota(T.ci[:, 0:32], [[0, 2], [s2 - s3, 2], [32, 8]], s3)
-    iota(T.ci[:, 32:64], [[0, 2], [s0 - S1, 2], [32, 8]], S1)
+    iota(T.ci[:, 32:64], [[0, 2], [s0 - s1, 2], [32, 8]], s1)
     iota(T.ci[:, 64:96], [[-1, 2], [1, 16]], 1)
     k_ci = iota(T.ci[:, 96:128], [[-1, 2], [1, 16]], 17)
     k_fj = iota(T.fj[:], [[0, 4], [1, 8]], TRASH, 8)
-    fill()(T.xt[:, 0:8], 0.0)
-    fill()(T.z0[:, 9:17], 0.0)
-    k_x = fill()(T.ex[0:32, :], 0.0)
     k = tp(k_ci)(T.ct[:], T.ci[:])
     k_q = quant(k_x, ("lx", 16))(T.q0[:, 30:288], T.s0[:, 30:288], T.xt[:])
     k_gl = cp(k)(T.gls[:, 0:5], T.ct[:, 0:160:32])
-    last = T.gls[:, 2:4]
+    k_wq = quant(("lw", 16))(T.wq[:], T.ws[:], T.wt[:])
+    last, last2 = T.gls[:, 2:3], T.gls[:, 2:4]
     copy(1, 0, 0, 31, 257, "c1", k_q, ("l0", left["l0"]))
     copy(2, 0, 0, 31, 257, "c2")
     copy(3, 256, 0, 31, 257, "c3")
-    g.sync.dma_start(T.wt[:], T.w[:]).then_inc(S.lw, 16)
-    blank(T.win0, 160, 0.0, k_ramp)
-    for rows, c, value in ((slice(0, 128), 0, -1.0), (block(p4), 1, 0.0), (block(o), 1, 256.0), (side(pb), 1, 384.0)):
-        k_cc = act()(T.cc[rows, c:c + 1], T.ramp[rows, 0:1], ID, value)
-    blank(T.win1, 544, BIG)
+    act()(T.ab[:, 256:257], T.two[:, 0:1], ID, 1.0 - BIG, 0.0)
+    act()(T.z0[:, 9:17], T.two[:, 0:8], CP)
+    for rows, c, value in ((every, 0, -1.0), (block(p4), 1, 0.0), (block(o), 1, 256.0), (side(pb), 1, 384.0)):
+        k_cc = act()(T.cc[rows, c:c + 1], T.two[rows, 0:1], ID, value, 0.0)
+    blank(T.win1, 0, FIRST0, BIG, k_ramp)
+    blank(T.win1, FIRST0, FIRST0 + 160, 0.0)
 
     k = cp(k_gl, ("ld", 32), ("mk", 3 * bin(m).count("1")))(T.dmu[:], T.dmx[:].indirect(T.gls[:, 4:5]))
     ka = ts(k, k_tf)(T.ab[:, 0:256], T.tf[:].indirect(T.dmu[:]), 1.0 - BIG, None, A.mult)
     kb = act(k)(T.ab[:, 288:544], T.tf[:].indirect(T.dmu[:]), CP, 0.0, BIG)
     k = scan(ka, kb)(T.zs[:], T.ab[:, 0:288], T.ab[:, 287:575], BIG - 1.0, A.add, A.add)
     k_tr = tp(k)(T.tr[:], T.zs[:])
-    k_st = ts(k_tr)(T.st[:], T.tr[:, SP:256:32], 255.0, None, A.min)
+    k_su = ts(k_tr)(T.su[:], T.tr[:, SQ:256:32], 255.0, None, A.min)
     k_y = tt(k_fj)(T.yy[:], T.tr[:].indirect(T.gls[:, 0:2]), T.fj[:], A.min)
-    k = act(k_tr, k_cc)(T.cc[block(pb + 1), 0:1], T.tr[block(pb), 256 + SP:257 + SP], ID, -1.0, -1.0)
+    k_st = ts()(T.st[:], T.tr[:, SP:256:32], 255.0, None, A.min)
+    k_vu = act(k_su)(T.vu[:], T.ramp[:].indirect(T.su[:]), ID, -1.0, -1.0)
+    k = act(k_cc)(T.cc[block(pb + 1), 0:1], T.tr[block(pb), 256 + SP:257 + SP], ID, -1.0, -1.0)
     k_e1 = act()(T.ex[block(1), :], T.tr[block(0), 256:288], CP)
     k_vr = act(k, k_st)(T.vr[:], T.ramp[:].indirect(T.st[:]), ID, T.cc[:, 0:1], -1.0)
-    k_w3 = blank(T.win3, 544, BIG)
-    k_e = tt()(T.ex[block(2), :], T.tr[block(0), 256:288], T.tr[block(1), 256:288], A.add)
-    k = cp(k_y)(T.p0[:], T.yy[:, 24:32])
-    k_e = tt(k_e)(T.ex[block(3), :], T.ex[block(2), :], T.tr[block(2), 256:288], A.add)
+    k_w3 = blank(T.win3, 0, 544, BIG)
 
-    k_s0 = scatter(0, 0, T.p0[:], k, k_vr)
+    for a in (pb, pb + 1):
+        ts(k_y)(T.p1[block(a), :], T.yy[block(p4), 24:32], float(FIRST0), None, A.add)
+    ts()(T.p1[block(pa + 1), :], T.yy[block(pa + 1), 16:24], T.tr[block(pa), 256 + s1:257 + s1], None, A.add)
+    k_e = tt()(T.ex[block(2), :], T.tr[block(0), 256:288], T.tr[block(1), 256:288], A.add)
+    k = cp()(T.p1[block(pa), :], T.yy[block(pa), 16:24])
+    k_e = tt(k_e)(T.ex[block(3), :], T.ex[block(2), :], T.tr[block(2), 256:288], A.add)
+    k_s1 = scatter(1, 0, T.p1[:], T.vu[:], k, k_vu)
+    k_p2 = ts(k_e, k_e1)(T.p2[:], T.yy[:, 8:16], T.ex[:, s2:s2 + 1], None, A.add)
     lo = min(s2, s3)
-    k = tt(k_e)(T.tot[block(3), :], T.ex[block(3), lo:lo + 5:4], T.tr[block(3), 256 + lo:261 + lo:4], A.add)
+    k = tt()(T.tot[block(3), :], T.ex[block(3), lo:lo + 5:4], T.tr[block(3), 256 + lo:261 + lo:4], A.add)
     k_nn = on("gp", g.partition_broadcast)(k)(T.nn[:], T.tot[96:97, :], 128)
     c2, c3 = (s2 - lo) // 4, (s3 - lo) // 4
     nh = T.nn[:, c3:c3 + 1]
-    send(q ^ 4, T.n2[:], T.nn[:, c2:c2 + 1], "rn", "lo", k_nn)
-    ks = turn(0, 128, False, k_s0), turn(0, 128, True)
-    k_p1 = ts(k_e1)(T.p1[:], T.yy[:, 16:24], T.ex[:, S1:S1 + 1], None, A.add)
-    k = join(0, 128, ks, block(p4))
-    k_p2 = ts()(T.p2[:], T.yy[:, 8:16], T.ex[:, s2:s2 + 1], None, A.add)
-    kc = act(k)(T.z0[block(p4 ^ 3), 0:9], T.z0[block(p4), 0:9], CP)
-    cp(k)(T.z0[block(p4 ^ 1), 0:9], T.z0[block(p4), 0:9])
-    k = cp()(T.z0[block(p4 ^ 2), 0:9], T.z0[block(p4), 0:9])
-    k_s1 = scatter(1, 0, T.p1[:], k_p1)
-    k = ts(k, kc)(T.off0[:], T.z0[:].indirect(T.gls[:, 2:3]), -1.0, 31.0, A.mult, A.add)
-    k_s2 = scatter(1, 256, T.p2[:], k_p2, k_s1)
+    send(q ^ 4, T.n2[:], T.nn[:, c2:c2 + 1], "rn", k_nn)
+    ks = [turn(0, 128, back, k_s1, row=1, first=FIRST0, rows=side(pb)) for back in (False, True)]
+    for back in (False, True):
+        for to in (pa, pb):
+            k = join(0, 128, back, ks[back], side(pb), side(to))
+    k_s2 = scatter(1, 256, T.p2[:], T.vr[:], k_p2, k_vr)
+    k = ts(k)(T.off0[:], T.z0[:].indirect(last), -1.0, 31.0, A.mult, A.add)
+    k1 = turn(1, 512, False, k_s2)
     ka, kb = pick(T.slq0[:], T.sls0[:], T.q0[:], T.s0[:], T.off0[:, 0:8], [k], [k])
-    send(q ^ 1, T.q1[:, 257:385].bitcast(dt.uint8), T.slq0[:].bitcast(dt.uint8), "r0c", "l1", ka)
-    send(q ^ 1, T.s1[:, 257:385], T.sls0[:], "r0s", "l1", kb)
+    send(q ^ 1, T.q1[:, 257:385].bitcast(dt.uint8), T.slq0[:].bitcast(dt.uint8), "r0c", ka)
+    send(q ^ 1, T.s1[:, 257:385], T.sls0[:], "r0s", kb)
     if half:
         act(k_w3)(T.win3[block(p4), 16:272], T.ramp[block(p4), :], RELU, 256.0, -1.0)
         k_w3 = act()(T.win3[block(p4), 272:528], T.ramp[block(p4), :], RELU, 0.0, -1.0)
@@ -229,59 +237,61 @@ def rank_program(g, core, T, topo):
     need("y", *act()(T.lnt[block(p4), 1:2], T.tr[block(p4), 256 + s3:257 + s3], CP))
     g.sync.dma_start(T.ln[:], T.lnt[32 * p4:32 * p4 + 1, 0:2]).then_inc(S.lnd, 16)
 
-    ks = turn(1, 512, False, k_s2), turn(1, 512, True)
-    k = join(1, 512, ks)
-    k = spread(1, halve(1, lift(1, k)))
-    k = ts(k)(T.off1[:], T.m1[:].indirect(last), -1.0, None, A.mult)
+    k = turn(1, 512, True)
+    join(1, 512, False, k1)
+    k = lift(1, join(1, 512, True, k))
     if half:
         k_p3 = ts(("rn", 16))(T.p3[:], T.yy[:, 0:8], T.ex[:, s3:s3 + 1], T.n2[:], A.add, A.add)
     else:
         k_p3 = ts()(T.p3[:], T.yy[:, 0:8], T.ex[:, s3:s3 + 1], None, A.add)
+    k = spread(1, halve(1, k))
+    k = ts(k)(T.off1[:], T.m1[:].indirect(last2), -1.0, None, A.mult)
     ka, kb = pick(T.slq1[:], T.sls1[:], T.q1[:], T.s1[:], T.off1[:, 0:12],
                   [k, ("c1", 32), ("r0c", 16)], [k, ("c1", 32), ("r0s", 16)])
-    send(q ^ 2, T.q2[:, 385:577].bitcast(dt.uint8), T.slq1[:].bitcast(dt.uint8), "r1c", "l2", ka)
-    send(q ^ 2, T.s2[:, 385:577], T.sls1[:], "r1s", "l2", kb)
+    send(q ^ 2, T.q2[:, 385:577].bitcast(dt.uint8), T.slq1[:].bitcast(dt.uint8), "r1c", ka)
+    send(q ^ 2, T.s2[:, 385:577], T.sls1[:], "r1s", kb)
     copy(2, 257, 1, 257, 128, "c2", ("r0c", 16), ("r0s", 16))
     copy(3, 513, 1, 257, 128, "c3")
 
-    k = scatter(3, 0, T.p3[:], k_p3, k_w3)
-    k_wq = quant(("lw", 16))(T.wq[:], T.ws[:], T.wt[:])
+    k = scatter(3, 0, T.p3[:], T.vr[:], k_p3, k_w3)
     ks = turn(3, 512, False, k), turn(3, 512, True)
+    join(3, 512, False, ks[0])
+    k3 = join(3, 512, True, ks[1])
     ka, kb = pick(T.slq2[:], T.sls2[:], T.q2[:], T.s2[:], T.off1[:, 16:32], [("c2", 64), ("r1c", 16)], [("c2", 64), ("r1s", 16)])
-    send(q ^ 4, T.q3[:, 0:256].bitcast(dt.uint8), T.slq2[:].bitcast(dt.uint8), "r2c", "lo", ka)
-    send(q ^ 4, T.s3[:, 0:256], T.sls2[:], "r2s", "lo", kb)
+    send(q ^ 4, T.q3[:, 0:256].bitcast(dt.uint8), T.slq2[:].bitcast(dt.uint8), "r2c", ka)
+    send(q ^ 4, T.s3[:, 0:256], T.sls2[:], "r2s", kb)
     copy(3, 641, 2, 385, 192, "c3", ("r1c", 16), ("r1s", 16))
-    k = spread(3, halve(3, lift(3, join(3, 512, ks))))
+    k = spread(3, halve(3, lift(3, k3)))
     if half:
-        ts(k)(T.off3[:, 16:32], T.m3[:, 16:33].indirect(T.gls[:, 2:3]), -1.0, None, A.mult)
-        k_off3 = ts()(T.off3[:, 0:16], T.m3[:].indirect(T.gls[:, 2:3]), -1.0, 256.0, A.mult, A.add)
+        k_off3 = [ts(k)(T.off3[:, 16:32], T.m3[:, 16:33].indirect(last), -1.0, None, A.mult)] * 2
+        k_off3 += [ts()(T.off3[:, 0:16], T.m3[:].indirect(last), -1.0, 256.0, A.mult, A.add)] * 2
     else:
-        k_off3 = ts(k)(T.off3[:], T.m3[:].indirect(last), -1.0, 256.0, A.mult, A.add)
+        k_off3 = [ts(k)(T.off3[:], T.m3[:].indirect(last2), -1.0, 256.0, A.mult, A.add)] * 4
 
-    def product(i, a, b, lo):
-        w_, held = b - a, [k_off3, ("c3", 96)]
+    def product(i):
+        a, b = RUNS[half][i]
+        lo = 256 if half and a >= 256 else 0
+        held = [k_off3[i], ("c3", 96)]
         ka, kb = pick(T.qa[:, a:b], T.sa[:, a:b], T.q3[:, lo:833], T.s3[:, lo:833], T.off3[:, a // 16:b // 16],
                       held + [("r2c", 16)] * (lo == 0), held + [("r2s", 16)] * (lo == 0))
-        for w in range(2):
-            e = 512 * (2 * i + w)
-            k = mm(k_wq, ka, kb)(T.ps[:, e:e + w_], T.wq[:, 128 * w:128 * w + 128], T.ws[:, 128 * w:128 * w + 128],
-                                 T.qa[:, a:b], T.sa[:, a:b], True, True)
-        return k
+        return [mm(k_wq, ka, kb)(T.ps[:, 512 * (2 * i + w):512 * (2 * i + w) + b - a], T.wq[:, 128 * w:128 * w + 128],
+                                 T.ws[:, 128 * w:128 * w + 128], T.qa[:, a:b], T.sa[:, a:b], True, True) for w in range(2)]
 
-    def store(i, a, b, k):
-        e, w_ = 1024 * i, b - a
-        ka = cp(("t", k[1] - 1))(T.ys[:, a:b], T.ps[:, e:e + w_])
-        kb = act(k)(T.ys[:, 512 + a:512 + b], T.ps[:, e + 512:e + 512 + w_], CP)
-        need("y", *ka)
-        g.sync.dma_start(T.y[:, a:b], T.ys[:, a:b]).then_inc(S.yo, 16)
-        need("y", *kb)
-        g.sync.dma_start(T.y[:, 512 + a:512 + b], T.ys[:, 512 + a:512 + b]).then_inc(S.yo, 16)
-        n_yo[0] += 32
+    def store(i, ks):
+        a, b = RUNS[half][i]
+        ka = cp(ks[0])(T.ys[:, a:b], T.ps[:, 1024 * i:1024 * i + b - a])
+        kb = act(ks[1])(T.ys[:, 512 + a:512 + b], T.ps[:, 1024 * i + 512:1024 * i + 512 + b - a], CP)
+        for k, c in ((ka, a), (kb, 512 + a)):
+            need("y", *k)
+            g.sync.dma_start(T.y[:, c:c + b - a], T.ys[:, c:c + b - a]).then_inc(S.yo, 16)
+            n_yo[0] += 16
 
-    runs = [(256, 512, 256), (0, 128, 0), (128, 256, 0)] if half else [(0, 128, 0), (128, 384, 0), (384, 512, 0)]
-    ends = [product(i, *r) for i, r in enumerate(runs)]
-    for i, (a, b, lo) in enumerate(runs):
-        store(i, a, b, ends[i])
+    ends = []
+    for i in range(6):
+        if i < 4:
+            ends.append(product(i))
+        if i >= 2:
+            store(i - 2, ends[i - 2])
 
     for kind in ("v", "s", "t", "gp"):
         need("gp", kind, n[kind])

@@ -8,8 +8,12 @@ WIN = 2112
 ONE, TWO, FOUR = 7, 15, 23
 SETS = 2 ** ONE + (2 ** TWO + 2 ** (TWO + 4)) + sum(2 ** (FOUR + 2 * i) for i in range(4))
 SP, SQ = 24, 25
-FIRST0 = 544
+LENGTH = {1: 192, 2: 256, 3: 512}
+MID = 192.0
 RUNS = (((0, 128), (128, 256), (256, 384), (384, 512)), ((256, 384), (384, 512), (0, 128), (128, 256)))
+PEERS = ((1, 2, 3),)
+ORDER = ("e2 s1 e3 ta1 tb1 tot ja1 jb1 st off0 p2 side0 x0 w3 s2 spread1 off1 ta2 tb2 ja2 jb2 p3 x1 "
+         "lift2 s3 halve2 spread2 off2 ta3 x2 tb3 ja3 jb3 lift3 halve3 spread3 off3").split()
 
 
 def _s(n, d):
@@ -18,7 +22,7 @@ def _s(n, d):
 
 SCRATCH = {
     "dmx": _s(128, I32), "dmu": _s(16, U16), "xt": _s(1032, BF), "wt": _s(1024, BF),
-    "q0": _s(288, Q8), "s0": _s(288, U8), "q1": _s(386, Q8), "s1": _s(386, U8),
+    "q0": _s(258, Q8), "s0": _s(258, U8), "q1": _s(386, Q8), "s1": _s(386, U8),
     "q2": _s(578, Q8), "s2": _s(578, U8), "q3": _s(834, Q8), "s3": _s(834, U8),
     "slq0": _s(128, Q8), "sls0": _s(128, U8), "slq1": _s(192, Q8), "sls1": _s(192, U8),
     "slq2": _s(256, Q8), "sls2": _s(256, U8),
@@ -28,11 +32,10 @@ SCRATCH = {
     "ab": _s(576, F32), "zs": _s(288, BF), "tr": _s(288, BF), "ex": _s(32, F32), "tot": _s(2, F32), "nn": _s(2, F32),
     "st": _s(8, U16), "vr": _s(128, BF), "su": _s(8, U16), "vu": _s(128, BF), "yy": _s(32, F32), "n2": _s(1, F32),
     "p1": _s(8, U16), "p2": _s(8, U16), "p3": _s(8, U16),
-    "win1": _s(WIN, BF), "win3": _s(WIN, BF),
-    "tr0": _s(288, BF), "tr1": _s(1056, BF), "tr3": _s(1056, BF),
-    "z0": _s(17, F32), "z1": _s(33, F32), "z3": _s(33, F32), "c1": _s(33, F32), "c3": _s(33, F32),
-    "h1": _s(33, F32), "h3": _s(33, F32), "m1": _s(33, F32), "m3": _s(33, F32),
-    "off0": _s(16, U16), "off1": _s(32, U16), "off3": _s(32, U16),
+    "win1": _s(WIN, BF), "win2": _s(WIN, BF), "win3": _s(WIN, BF), "tr1": _s(416, BF), "tr2": _s(544, BF), "tr3": _s(1056, BF),
+    "z1": _s(17, F32), "z2": _s(17, F32), "z3": _s(33, F32), "c2": _s(17, F32), "c3": _s(33, F32),
+    "h2": _s(17, F32), "h3": _s(33, F32), "m1": _s(17, F32), "m2": _s(17, F32), "m3": _s(33, F32),
+    "off0": _s(16, U16), "off1": _s(16, U16), "off2": _s(16, U16), "off3": _s(32, U16),
     "lnt": _s(4, F32), "ys": _s(1024, F32),
     "ps": ("psum", [128, 4096], F32),
 }
@@ -92,44 +95,43 @@ def rank_program(g, core, T, topo):
         left["lo"] += len(topo.engines(core, T.cores[dst]))
 
     def copy(i, a, j, b, count, sem, *after):
-        for w in after:
+        for w in after[:-1]:
             need("y", *w)
         g.sync.dma_start(T["q%d" % i][:, a:a + count].bitcast(dt.uint8), T["q%d" % j][:, b:b + count].bitcast(dt.uint8)).then_inc(S[sem], 16)
+        for w in after[-1:]:
+            need("y", *w)
         g.sync.dma_start(T["s%d" % i][:, a:a + count], T["s%d" % j][:, b:b + count]).then_inc(S[sem], 16)
 
     def pick(qo, so, qi, si, off, vwaits, swaits):
         return cp(*vwaits)(qo.bitcast(dt.uint32), qi.bitcast(dt.uint32).indirect(off)), act(*swaits)(so, si.indirect(off), CP)
 
-    def scatter(i, first, places, values, *after):
-        return cp(*after)(T["win%d" % i][:, 16 + first:WIN].indirect(places), values)
+    def scatter(i, values, *after):
+        return cp(*after)(T["win%d" % i][:, 16:WIN].indirect(T["p%d" % i][:]), values)
 
-    def turn(i, count, back, *after, row=None, first=0, rows=every):
-        w, t = T["win%d" % (row or i)], T["tr%d" % i]
+    def turn(i, back, k):
+        w, t, c = T["win%d" % i], T["tr%d" % i], LENGTH[i]
+        return tp(k)(t[:, c:2 * c + 32], w[:, 0:c + 32]) if back else tp(k)(t[:, 0:c], w[:, 16:c + 16])
+
+    def join(i, back, k):
+        t, z, c = T["tr%d" % i], T["z%d" % i], LENGTH[i]
         if back:
-            return tp(*after)(t[rows, count:2 * count + 32], w[rows, first:first + count + 32])
-        return tp(*after)(t[rows, 0:count], w[rows, first + 16:first + 16 + count])
+            return tt(k)(z[:, 0:c // 16 + 1:2], t[:, c:2 * c + 32:32], t[:, c + 16:2 * c + 32:32], A.min)
+        return tt(k)(z[:, 1:c // 16:2], t[:, 0:c:32], t[:, 16:c:32], A.min)
 
-    def join(i, count, back, k, rows=every, to=every):
-        t, z, nb = T["tr%d" % i], T["z%d" % i], count // 32
-        if back:
-            return tt(k)(z[to, 0:2 * nb + 1:2], t[rows, count:2 * count + 32:32], t[rows, count + 16:2 * count + 32:32], A.min)
-        return tt(k)(z[to, 1:2 * nb:2], t[rows, 0:count:32], t[rows, 16:count:32], A.min)
-
-    def lift(i, *after):
-        return ts(*after)(T["c%d" % i][:], T["z%d" % i][:], T.cc[:, 1:2], None, A.subtract)
+    def lift(i, k):
+        return ts(k)(T["c%d" % i][:], T["z%d" % i][:], T.cc[:, 1:2], None, A.subtract)
 
     def halve(i, k):
         c = T["c%d" % i]
         return tt(k)(T["h%d" % i][0:64, :], c[0:64, :], c[64:128, :], A.min)
 
-    def spread(i, k):
-        h, m = T["h%d" % i], T["m%d" % i]
-        return [tt(k)(m[block(a), :], h[0:32, :], h[32:64, :], A.min) for a in range(4)][-1]
+    def spread(i, h, a, k):
+        return [tt(k)(T["m%d" % i][block(b), :], h[block(a), :], h[block(a + 1), :], A.min) for b in range(4)][-1]
 
-    def blank(w, first, end, value, *after):
-        for a in range(first, end, 256):
-            b = min(end, a + 256)
-            k = act(*after)(w[:, a:b], T.ramp[:, 0:b - a], ID, value, 0.0)
+    def blank(i, *after):
+        for a in range(0, LENGTH[i] + 32, 256):
+            b = min(LENGTH[i] + 32, a + 256)
+            k = act(*after)(T["win%d" % i][:, a:b], T.ramp[:, 0:b - a], ID, BIG, 0.0)
         return k
 
     mine = slice(32 * p4, 32 * p4 + 16)
@@ -156,122 +158,143 @@ def rank_program(g, core, T, topo):
     k_tf = ts(k)(T.tf[:], T.ti[:], T.pw[:, 0:1], None, A.is_ge)
 
     iota(T.ci[:, 128:160], [[0, 2], [1, 16]], 0, 1)
-    peers = [q ^ 1, q ^ 2, q ^ 3]
-    m, ids = topo.mask(core, T.cores[peers[0]]), []
-    for d in peers:
-        m &= topo.mask(core, T.cores[d])
-        rid, pid, _ = topo.addr(T.cores[d])
-        ids.append(DstId(rid=rid, pnc=pid))
     need("gp", *k_dm)
     g.wait_ge(S.ld, 32)
-    g.remote_dma_fused([RemoteDMATransfer(dst_ids=ids, dma_engine_mask=m, remote_sem=S.mk, srcs=[T.dmx[:, mine]],
-                                          dsts=[T.dmx[:, mine] for d in peers])], local_sem=S.l0)
-    left["l0"] += bin(m).count("1")
+    masks = 0
+    for i, peers in enumerate(PEERS):
+        es = [e for e in topo.engines(core, T.cores[q ^ 1])[i::2] if all(e in topo.engines(core, T.cores[q ^ d]) for d in peers)]
+        ids = [DstId(rid=topo.addr(T.cores[q ^ d])[0], pnc=topo.addr(T.cores[q ^ d])[1]) for d in peers]
+        g.remote_dma_fused([RemoteDMATransfer(dst_ids=ids, dma_engine_mask=sum(1 << e for e in es), remote_sem=S.mk,
+                                              srcs=[T.dmx[:, mine]], dsts=[T.dmx[:, mine] for d in peers])], local_sem=S.l0)
+        left["l0"] += len(es)
+        masks += len(es) * len(peers)
 
     iota(T.ci[:, 0:32], [[0, 2], [s2 - s3, 2], [32, 8]], s3)
     iota(T.ci[:, 32:64], [[0, 2], [s0 - s1, 2], [32, 8]], s1)
-    iota(T.ci[:, 64:96], [[-1, 2], [1, 16]], 1)
-    k_ci = iota(T.ci[:, 96:128], [[-1, 2], [1, 16]], 17)
+    k_ci = iota(T.ci[:, 64:128], [[16, 2], [-1, 2], [1, 16]], 1)
     k_fj = iota(T.fj[:], [[0, 4], [1, 8]], TRASH, 8)
     k = tp(k_ci)(T.ct[:], T.ci[:])
-    k_q = quant(k_x, ("lx", 16))(T.q0[:, 30:288], T.s0[:, 30:288], T.xt[:])
+    k_q = quant(k_x, ("lx", 16))(T.q0[:], T.s0[:], T.xt[:])
     k_gl = cp(k)(T.gls[:, 0:5], T.ct[:, 0:160:32])
     k_wq = quant(("lw", 16))(T.wq[:], T.ws[:], T.wt[:])
     last, last2 = T.gls[:, 2:3], T.gls[:, 2:4]
-    copy(1, 0, 0, 31, 257, "c1", k_q, ("l0", left["l0"]))
-    copy(2, 0, 0, 31, 257, "c2")
-    copy(3, 256, 0, 31, 257, "c3")
+    copy(1, 0, 0, 1, 257, "c1", ("l0", left["l0"]), k_q, k_q)
+    copy(2, 0, 0, 1, 257, "c2")
+    copy(3, 256, 0, 1, 257, "c3")
     act()(T.ab[:, 256:257], T.two[:, 0:1], ID, 1.0 - BIG, 0.0)
-    act()(T.z0[:, 9:17], T.two[:, 0:8], CP)
-    for rows, c, value in ((every, 0, -1.0), (block(p4), 1, 0.0), (block(o), 1, 256.0), (side(pb), 1, 384.0)):
+    act()(T.z1[:, 13:17], T.two[:, 0:4], CP)
+    for rows, c, value in ((every, 0, -1.0), (block(p4), 1, 0.0), (block(o), 1, 256.0), (side(pb), 1, 384.0),
+                           (block(p4), 2, MID - 1.0), (block(o), 2, MID - 257.0), (side(pb), 2, MID - 1.0)):
         k_cc = act()(T.cc[rows, c:c + 1], T.two[rows, 0:1], ID, value, 0.0)
-    blank(T.win1, 0, FIRST0, BIG, k_ramp)
-    blank(T.win1, FIRST0, FIRST0 + 160, 0.0)
+    blank(1, k_ramp)
+    blank(2)
 
-    k = cp(k_gl, ("ld", 32), ("mk", 3 * bin(m).count("1")))(T.dmu[:], T.dmx[:].indirect(T.gls[:, 4:5]))
+    k = cp(k_gl, ("ld", 32), ("mk", masks))(T.dmu[:], T.dmx[:].indirect(T.gls[:, 4:5]))
     ka = ts(k, k_tf)(T.ab[:, 0:256], T.tf[:].indirect(T.dmu[:]), 1.0 - BIG, None, A.mult)
     kb = act(k)(T.ab[:, 288:544], T.tf[:].indirect(T.dmu[:]), CP, 0.0, BIG)
     k = scan(ka, kb)(T.zs[:], T.ab[:, 0:288], T.ab[:, 287:575], BIG - 1.0, A.add, A.add)
     k_tr = tp(k)(T.tr[:], T.zs[:])
     k_su = ts(k_tr)(T.su[:], T.tr[:, SQ:256:32], 255.0, None, A.min)
     k_y = tt(k_fj)(T.yy[:], T.tr[:].indirect(T.gls[:, 0:2]), T.fj[:], A.min)
-    k_st = ts()(T.st[:], T.tr[:, SP:256:32], 255.0, None, A.min)
-    k_vu = act(k_su)(T.vu[:], T.ramp[:].indirect(T.su[:]), ID, -1.0, -1.0)
-    k = act(k_cc)(T.cc[block(pb + 1), 0:1], T.tr[block(pb), 256 + SP:257 + SP], ID, -1.0, -1.0)
-    k_e1 = act()(T.ex[block(1), :], T.tr[block(0), 256:288], CP)
-    k_vr = act(k, k_st)(T.vr[:], T.ramp[:].indirect(T.st[:]), ID, T.cc[:, 0:1], -1.0)
-    k_w3 = blank(T.win3, 0, 544, BIG)
+    k_e1 = act(k_tr)(T.ex[block(1), :], T.tr[block(0), 256:288], CP)
+    k_vu = act(k_su, k_cc)(T.vu[:], T.ramp[:].indirect(T.su[:]), ID, T.cc[:, 2:3], -1.0)
+    k_cv = act()(T.cc[block(pb + 1), 0:1], T.tr[block(pb), 256 + SP:257 + SP], ID, -1.0, -1.0)
+    k_w3 = blank(3)
 
+    ts(k_y)(T.p1[block(pa + 1), :], T.yy[block(pa + 1), 16:24], T.tr[block(pa), 256 + s1:257 + s1], None, A.add)
+    cp()(T.p1[block(pa), :], T.yy[block(pa), 16:24])
     for a in (pb, pb + 1):
-        ts(k_y)(T.p1[block(a), :], T.yy[block(p4), 24:32], float(FIRST0), None, A.add)
-    ts()(T.p1[block(pa + 1), :], T.yy[block(pa + 1), 16:24], T.tr[block(pa), 256 + s1:257 + s1], None, A.add)
-    k_e = tt()(T.ex[block(2), :], T.tr[block(0), 256:288], T.tr[block(1), 256:288], A.add)
-    k = cp()(T.p1[block(pa), :], T.yy[block(pa), 16:24])
-    k_e = tt(k_e)(T.ex[block(3), :], T.ex[block(2), :], T.tr[block(2), 256:288], A.add)
-    k_s1 = scatter(1, 0, T.p1[:], T.vu[:], k, k_vu)
-    k_p2 = ts(k_e, k_e1)(T.p2[:], T.yy[:, 8:16], T.ex[:, s2:s2 + 1], None, A.add)
+        k = cp()(T.p1[block(a), :], T.yy[block(p4), 24:32])
+    H = {"p1": k, "e1": k_e1}
     lo = min(s2, s3)
-    k = tt()(T.tot[block(3), :], T.ex[block(3), lo:lo + 5:4], T.tr[block(3), 256 + lo:261 + lo:4], A.add)
-    k_nn = on("gp", g.partition_broadcast)(k)(T.nn[:], T.tot[96:97, :], 128)
     c2, c3 = (s2 - lo) // 4, (s3 - lo) // 4
     nh = T.nn[:, c3:c3 + 1]
-    send(q ^ 4, T.n2[:], T.nn[:, c2:c2 + 1], "rn", k_nn)
-    ks = [turn(0, 128, back, k_s1, row=1, first=FIRST0, rows=side(pb)) for back in (False, True)]
-    for back in (False, True):
-        for to in (pa, pb):
-            k = join(0, 128, back, ks[back], side(pb), side(to))
-    k_s2 = scatter(1, 256, T.p2[:], T.vr[:], k_p2, k_vr)
-    k = ts(k)(T.off0[:], T.z0[:].indirect(last), -1.0, 31.0, A.mult, A.add)
-    k1 = turn(1, 512, False, k_s2)
-    ka, kb = pick(T.slq0[:], T.sls0[:], T.q0[:], T.s0[:], T.off0[:, 0:8], [k], [k])
-    send(q ^ 1, T.q1[:, 257:385].bitcast(dt.uint8), T.slq0[:].bitcast(dt.uint8), "r0c", ka)
-    send(q ^ 1, T.s1[:, 257:385], T.sls0[:], "r0s", kb)
-    if half:
-        act(k_w3)(T.win3[block(p4), 16:272], T.ramp[block(p4), :], RELU, 256.0, -1.0)
-        k_w3 = act()(T.win3[block(p4), 272:528], T.ramp[block(p4), :], RELU, 0.0, -1.0)
-    else:
-        k = act(k_nn)(T.cc[:, 2:3], nh, ID, 256.0)
+
+    def earlier(a):
+        return tt(H["e%d" % (a - 1)])(T.ex[block(a), :], T.ex[block(a - 1), :], T.tr[block(a - 1), 256:288], A.add)
+
+    def values():
+        k = ts()(T.st[:], T.tr[:, SP:256:32], 255.0, None, A.min)
+        return act(k, k_cv)(T.vr[:], T.ramp[:].indirect(T.st[:]), ID, T.cc[:, 0:1], -1.0)
+
+    def lengths():
+        k = tt(H["e3"])(T.tot[block(3), :], T.ex[block(3), lo:lo + 5:4], T.tr[block(3), 256 + lo:261 + lo:4], A.add)
+        k = on("gp", g.partition_broadcast)(k)(T.nn[:], T.tot[96:97, :], 128)
+        send(q ^ 4, T.n2[:], T.nn[:, c2:c2 + 1], "rn", k)
+        return k
+
+    def rows3():
+        if half:
+            act(k_w3)(T.win3[block(p4), 16:272], T.ramp[block(p4), :], RELU, 256.0, -1.0)
+            return act()(T.win3[block(p4), 272:528], T.ramp[block(p4), :], RELU, 0.0, -1.0)
+        k = act(H["tot"])(T.cc[:, 3:4], nh, ID, 256.0)
         act(k_w3)(T.win3[block(p4), 272:528], T.ramp[block(p4), :], RELU, T.nn[block(p4), c3:c3 + 1], -1.0)
-        k_w3 = act(k)(T.win3[block(p4), 16:272], T.ramp[block(p4), :], RELU, T.cc[block(p4), 2:3], -1.0)
-    act(k_nn, ("rn", 16))(T.lnt[:, 0:1], nh, ID, T.n2[:])
-    need("y", *act()(T.lnt[block(p4), 1:2], T.tr[block(p4), 256 + s3:257 + s3], CP))
-    g.sync.dma_start(T.ln[:], T.lnt[32 * p4:32 * p4 + 1, 0:2]).then_inc(S.lnd, 16)
+        return act(k)(T.win3[block(p4), 16:272], T.ramp[block(p4), :], RELU, T.cc[block(p4), 3:4], -1.0)
 
-    k = turn(1, 512, True)
-    join(1, 512, False, k1)
-    k = lift(1, join(1, 512, True, k))
-    if half:
-        k_p3 = ts(("rn", 16))(T.p3[:], T.yy[:, 0:8], T.ex[:, s3:s3 + 1], T.n2[:], A.add, A.add)
-    else:
-        k_p3 = ts()(T.p3[:], T.yy[:, 0:8], T.ex[:, s3:s3 + 1], None, A.add)
-    k = spread(1, halve(1, k))
-    k = ts(k)(T.off1[:], T.m1[:].indirect(last2), -1.0, None, A.mult)
-    ka, kb = pick(T.slq1[:], T.sls1[:], T.q1[:], T.s1[:], T.off1[:, 0:12],
-                  [k, ("c1", 32), ("r0c", 16)], [k, ("c1", 32), ("r0s", 16)])
-    send(q ^ 2, T.q2[:, 385:577].bitcast(dt.uint8), T.slq1[:].bitcast(dt.uint8), "r1c", ka)
-    send(q ^ 2, T.s2[:, 385:577], T.sls1[:], "r1s", kb)
-    copy(2, 257, 1, 257, 128, "c2", ("r0c", 16), ("r0s", 16))
-    copy(3, 513, 1, 257, 128, "c3")
+    def places3():
+        if half:
+            return ts(H["e3"], ("rn", 16))(T.p3[:], T.yy[:, 0:8], T.ex[:, s3:s3 + 1], T.n2[:], A.add, A.add)
+        return ts(H["e3"])(T.p3[:], T.yy[:, 0:8], T.ex[:, s3:s3 + 1], None, A.add)
 
-    k = scatter(3, 0, T.p3[:], T.vr[:], k_p3, k_w3)
-    ks = turn(3, 512, False, k), turn(3, 512, True)
-    join(3, 512, False, ks[0])
-    k3 = join(3, 512, True, ks[1])
-    ka, kb = pick(T.slq2[:], T.sls2[:], T.q2[:], T.s2[:], T.off1[:, 16:32], [("c2", 64), ("r1c", 16)], [("c2", 64), ("r1s", 16)])
-    send(q ^ 4, T.q3[:, 0:256].bitcast(dt.uint8), T.slq2[:].bitcast(dt.uint8), "r2c", ka)
-    send(q ^ 4, T.s3[:, 0:256], T.sls2[:], "r2s", kb)
-    copy(3, 641, 2, 385, 192, "c3", ("r1c", 16), ("r1s", 16))
-    k = spread(3, halve(3, lift(3, k3)))
-    if half:
-        k_off3 = [ts(k)(T.off3[:, 16:32], T.m3[:, 16:33].indirect(last), -1.0, None, A.mult)] * 2
-        k_off3 += [ts()(T.off3[:, 0:16], T.m3[:].indirect(last), -1.0, 256.0, A.mult, A.add)] * 2
-    else:
-        k_off3 = [ts(k)(T.off3[:], T.m3[:].indirect(last2), -1.0, 256.0, A.mult, A.add)] * 4
+    def exchange0():
+        k = H["side0"]
+        ka, kb = pick(T.slq0[:], T.sls0[:], T.q0[:], T.s0[:], T.off0[:, 0:8], [k], [k])
+        send(q ^ 1, T.q1[:, 257:385].bitcast(dt.uint8), T.slq0[:].bitcast(dt.uint8), "r0c", ka)
+        send(q ^ 1, T.s1[:, 257:385], T.sls0[:], "r0s", kb)
+        copy(2, 257, 1, 257, 128, "c2", ("r0c", 16), ("r0s", 16))
+
+    def exchange1():
+        k = H["off1"]
+        ka, kb = pick(T.slq1[:], T.sls1[:], T.q1[:], T.s1[:], T.off1[:, 0:12],
+                      [k, ("c1", 32), ("r0c", 16)], [k, ("c1", 32), ("r0s", 16)])
+        send(q ^ 2, T.q2[:, 385:577].bitcast(dt.uint8), T.slq1[:].bitcast(dt.uint8), "r1c", ka)
+        send(q ^ 2, T.s2[:, 385:577], T.sls1[:], "r1s", kb)
+        act(H["tot"], ("rn", 16))(T.lnt[:, 0:1], nh, ID, T.n2[:])
+        need("y", *act()(T.lnt[block(p4), 1:2], T.tr[block(p4), 256 + s3:257 + s3], CP))
+        g.sync.dma_start(T.ln[:], T.lnt[32 * p4:32 * p4 + 1, 0:2]).then_inc(S.lnd, 16)
+        copy(3, 513, 2, 257, 320, "c3", ("c2", 64), ("r1c", 16), ("r1s", 16))
+
+    def exchange2():
+        k = H["off2"]
+        ka, kb = pick(T.slq2[:], T.sls2[:], T.q2[:], T.s2[:], T.off2[:], [k, ("c2", 64), ("r1c", 16)], [k, ("c2", 64), ("r1s", 16)])
+        send(q ^ 4, T.q3[:, 0:256].bitcast(dt.uint8), T.slq2[:].bitcast(dt.uint8), "r2c", ka)
+        send(q ^ 4, T.s3[:, 0:256], T.sls2[:], "r2s", kb)
+
+    def offsets3():
+        k = H["spread3"]
+        if half:
+            return ([ts(k)(T.off3[:, 16:32], T.m3[:, 16:33].indirect(last), -1.0, None, A.mult)] * 2
+                    + [ts()(T.off3[:, 0:16], T.m3[:].indirect(last), -1.0, 256.0, A.mult, A.add)] * 2)
+        return [ts(k)(T.off3[:], T.m3[:].indirect(last2), -1.0, 256.0, A.mult, A.add)] * 4
+
+    steps = {
+        "tot": lengths, "w3": rows3, "p3": places3,
+        "e2": lambda: earlier(2), "e3": lambda: earlier(3), "s1": lambda: scatter(1, T.vu[:], H["p1"], k_vu),
+        "p2": lambda: ts(H["e3"])(T.p2[:], T.yy[:, 8:16], T.ex[:, s2:s2 + 1], None, A.add),
+        "st": values, "s2": lambda: scatter(2, T.vr[:], H["p2"], H["st"]),
+        "s3": lambda: scatter(3, T.vr[:], H["p3"], H["w3"], H["st"]),
+        "off0": lambda: ts(H["jb1"])(T.off0[:], T.z1[:].indirect(last), -1.0, MID + 1.0, A.mult, A.add),
+        "side0": lambda: cp(H["off0"])(T.off0[side(pa), :], T.off0[side(pb), :]),
+        "spread1": lambda: spread(1, T.z1, pa, H["jb1"]),
+        "off1": lambda: ts(H["spread1"])(T.off1[:], T.m1[:].indirect(last), -1.0, MID, A.mult, A.add),
+        "off2": lambda: ts(H["spread2"])(T.off2[:], T.m2[:].indirect(last), -1.0, None, A.mult),
+        "off3": offsets3, "x0": exchange0, "x1": exchange1, "x2": exchange2,
+    }
+    for i in (1, 2, 3):
+        steps.update({
+            "ta%d" % i: lambda i=i: turn(i, False, H["s%d" % i]), "tb%d" % i: lambda i=i: turn(i, True, H["s%d" % i]),
+            "ja%d" % i: lambda i=i: join(i, False, H["ta%d" % i]), "jb%d" % i: lambda i=i: join(i, True, H["tb%d" % i])})
+    for i in (2, 3):
+        steps.update({
+            "lift%d" % i: lambda i=i: lift(i, H["jb%d" % i]), "halve%d" % i: lambda i=i: halve(i, H["lift%d" % i]),
+            "spread%d" % i: lambda i=i: spread(i, T["h%d" % i], 0, H["halve%d" % i])})
+    for name in ORDER:
+        H[name] = steps[name]()
 
     def product(i):
         a, b = RUNS[half][i]
         lo = 256 if half and a >= 256 else 0
-        held = [k_off3[i], ("c3", 96)]
+        held = [H["off3"][i], ("c3", 64)]
         ka, kb = pick(T.qa[:, a:b], T.sa[:, a:b], T.q3[:, lo:833], T.s3[:, lo:833], T.off3[:, a // 16:b // 16],
                       held + [("r2c", 16)] * (lo == 0), held + [("r2s", 16)] * (lo == 0))
         return [mm(k_wq, ka, kb)(T.ps[:, 512 * (2 * i + w):512 * (2 * i + w) + b - a], T.wq[:, 128 * w:128 * w + 128],

@@ -4,16 +4,19 @@ from concourse.mybir import dt, AluOpType, ActivationFunctionType
 F32, I32, BF, U16, U8, Q8 = "float32", "int32", "bfloat16", "uint16", "uint8", "float8_e4m3fn_x4"
 BIG = 4096.0
 TRASH = 528
-WIN = 2112
+BACK = 592
+BACK2 = 800
+EMPTY = 2.0 * (256 + 384 + 384)
+WIN = 1392
 ONE, TWO, FOUR = 7, 15, 23
 SETS = 2 ** ONE + (2 ** TWO + 2 ** (TWO + 4)) + sum(2 ** (FOUR + 2 * i) for i in range(4))
-SP, SQ = 24, 25
+SQ, SP, S0, S1, S2, S3 = 0, 8, 4, 3, 18, 2
 LENGTH = {1: 192, 2: 256, 3: 512}
+WIDE = {1: 17, 2: 17, 3: 33}
 MID = 192.0
 RUNS = (((0, 128), (128, 256), (256, 384), (384, 512)), ((256, 384), (384, 512), (0, 128), (128, 256)))
-PEERS = ((1, 2, 3),)
-ORDER = ("e2 s1 e3 ta1 tb1 tot ja1 jb1 st off0 p2 side0 x0 w3 s2 spread1 off1 ta2 tb2 ja2 jb2 p3 x1 "
-         "lift2 s3 halve2 spread2 off2 ta3 x2 tb3 ja3 jb3 lift3 halve3 spread3 off3").split()
+ORDER = ("wq masks turn2 sets lists2 scan counts y1 y p1 e2 s1 e3 ta1 tb1 p2 tot j0 j1 off0 s2:0:2 x0 s2:2:8 spread1 off1 ta2 tb2 "
+         "w3 p3 j2 x1 s3:0:8 halve2 spread2 off2 ta3 x2 tb3 j3 halve3 spread3 off3").split()
 
 
 def _s(n, d):
@@ -27,20 +30,20 @@ SCRATCH = {
     "slq0": _s(128, Q8), "sls0": _s(128, U8), "slq1": _s(192, Q8), "sls1": _s(192, U8),
     "slq2": _s(256, Q8), "sls2": _s(256, U8),
     "qa": _s(512, Q8), "sa": _s(512, U8), "wq": _s(256, Q8), "ws": _s(256, U8),
-    "two": _s(24, F32), "pr": _s(56, F32), "pw": _s(32, F32), "ramp": _s(256, F32), "ti": _s(256, I32), "tf": _s(256, BF),
-    "ci": _s(160, BF), "ct": _s(160, BF), "fj": _s(32, F32), "cc": _s(4, F32), "gls": _s(6, U16),
+    "pr": _s(64, F32), "pw": _s(32, F32), "ramp": _s(288, BF), "ct": _s(288, BF), "ti": _s(256, I32), "tf": _s(256, BF),
+    "ci": _s(96, BF), "cu": _s(96, BF), "fj": _s(16, F32), "cc": _s(10, F32), "gls": _s(10, U16), "gl2": _s(4, U16),
     "ab": _s(576, F32), "zs": _s(288, BF), "tr": _s(288, BF), "ex": _s(32, F32), "tot": _s(2, F32), "nn": _s(2, F32),
-    "st": _s(8, U16), "vr": _s(128, BF), "su": _s(8, U16), "vu": _s(128, BF), "yy": _s(32, F32), "n2": _s(1, F32),
+    "vr": _s(128, BF), "vu": _s(128, BF), "yo": _s(8, F32), "yy": _s(16, F32), "n2": _s(1, F32),
     "p1": _s(8, U16), "p2": _s(8, U16), "p3": _s(8, U16),
-    "win1": _s(WIN, BF), "win2": _s(WIN, BF), "win3": _s(WIN, BF), "tr1": _s(416, BF), "tr2": _s(544, BF), "tr3": _s(1056, BF),
-    "z1": _s(17, F32), "z2": _s(17, F32), "z3": _s(33, F32), "c2": _s(17, F32), "c3": _s(33, F32),
-    "h2": _s(17, F32), "h3": _s(33, F32), "m1": _s(17, F32), "m2": _s(17, F32), "m3": _s(33, F32),
+    "win1": _s(WIN, BF), "win2": _s(WIN, BF), "win3": _s(WIN, BF), "tr1": _s(544, BF), "tr2": _s(544, BF), "tr3": _s(1056, BF),
+    "z0": _s(17, F32), "z1": _s(34, F32), "z2": _s(34, F32), "z3": _s(66, F32),
+    "h2": _s(34, F32), "h3": _s(66, F32), "m1": _s(17, F32), "m2": _s(17, F32), "m3": _s(33, F32),
     "off0": _s(16, U16), "off1": _s(16, U16), "off2": _s(16, U16), "off3": _s(32, U16),
     "lnt": _s(4, F32), "ys": _s(1024, F32),
     "ps": ("psum", [128, 4096], F32),
 }
 SEMAPHORES = ["ld", "lx", "lw", "v", "s", "t", "gp", "mk", "r0c", "r0s", "r1c", "r1s", "r2c", "r2s", "rn",
-              "c1", "c2", "c3", "l0", "lo", "yo", "lnd"]
+              "c1", "c2", "c3", "l0", "l1", "lo", "yo", "lnd"]
 
 
 def rank_program(g, core, T, topo):
@@ -52,8 +55,9 @@ def rank_program(g, core, T, topo):
     S = T.sem
     p4, half, par = q & 3, q >> 2, q & 1
     pa, pb, o = p4 & 2, 2 - (p4 & 2), p4 ^ 1
-    s0, s1, s2, s3 = FOUR - 1 + par, TWO - (p4 ^ 2), ONE - (q ^ 4), ONE - q
     every = slice(0, 128)
+    start, merge = {1: BACK, 2: BACK2 * half, 3: 0}, {1: A.min, 2: A.add, 3: A.add}
+    turned = BACK2 + 255.0
 
     def block(a):
         return slice(32 * a, 32 * a + 32)
@@ -62,7 +66,7 @@ def rank_program(g, core, T, topo):
         return slice(32 * a, 32 * a + 64)
 
     queues = {"v": g.vector, "s": g.scalar, "t": g.tensor, "gp": g, "y": g.sync}
-    n, seen, left, n_yo = {"v": 0, "s": 0, "t": 0, "gp": 0}, {}, {"l0": 0, "lo": 0}, [0]
+    n, seen, left, n_yo = {"v": 0, "s": 0, "t": 0, "gp": 0}, {}, {"l0": 0, "l1": 0, "lo": 0}, [0]
 
     def need(queue, sem, count):
         if seen.get((queue, sem), 0) < count:
@@ -88,11 +92,11 @@ def rank_program(g, core, T, topo):
     def iota(out, pat, base, cm=0):
         return on("gp", g.iota)()(out, pat, base, cm, allow_small_or_imprecise_dtypes=True)
 
-    def send(dst, out, in_, sem, after):
+    def send(dst, out, in_, sem, after, gone="lo"):
         need("gp", *after)
         rid, pid, _ = topo.addr(T.cores[dst])
-        g.remote_dma(out, in_, S[sem], S.lo, pid, rid, topo.mask(core, T.cores[dst]))
-        left["lo"] += len(topo.engines(core, T.cores[dst]))
+        g.remote_dma(out, in_, S[sem], S[gone], pid, rid, topo.mask(core, T.cores[dst]))
+        left[gone] += len(topo.engines(core, T.cores[dst]))
 
     def copy(i, a, j, b, count, sem, *after):
         for w in after[:-1]:
@@ -105,34 +109,32 @@ def rank_program(g, core, T, topo):
     def pick(qo, so, qi, si, off, vwaits, swaits):
         return cp(*vwaits)(qo.bitcast(dt.uint32), qi.bitcast(dt.uint32).indirect(off)), act(*swaits)(so, si.indirect(off), CP)
 
-    def scatter(i, values, *after):
-        return cp(*after)(T["win%d" % i][:, 16:WIN].indirect(T["p%d" % i][:]), values)
+    def scatter(i, a, b, values, *after):
+        return cp(*after)(T["win%d" % i][:, 16:WIN].indirect(T["p%d" % i][:, a:b]), values[:, 16 * a:16 * b])
 
     def turn(i, back, k):
-        w, t, c = T["win%d" % i], T["tr%d" % i], LENGTH[i]
-        return tp(k)(t[:, c:2 * c + 32], w[:, 0:c + 32]) if back else tp(k)(t[:, 0:c], w[:, 16:c + 16])
+        w, t, c, a, b = T["win%d" % i], T["tr%d" % i], LENGTH[i], start[i], 16 * (WIDE[i] - 1)
+        return tp(k)(t[:, b:b + c + 32], w[:, a:a + c + 32]) if back else tp(k)(t[:, 0:c], w[:, a + 16:a + c + 16])
 
-    def join(i, back, k):
-        t, z, c = T["tr%d" % i], T["z%d" % i], LENGTH[i]
-        if back:
-            return tt(k)(z[:, 0:c // 16 + 1:2], t[:, c:2 * c + 32:32], t[:, c + 16:2 * c + 32:32], A.min)
-        return tt(k)(z[:, 1:c // 16:2], t[:, 0:c:32], t[:, 16:c:32], A.min)
-
-    def lift(i, k):
-        return ts(k)(T["c%d" % i][:], T["z%d" % i][:], T.cc[:, 1:2], None, A.subtract)
+    def join(i, out, rows, *after):
+        t, r = T["tr%d" % i], SQ if i == 1 else SP
+        return tt(*after)(out, t[rows, r::32], t[rows, r + 16::32], merge[i])
 
     def halve(i, k):
-        c = T["c%d" % i]
-        return tt(k)(T["h%d" % i][0:64, :], c[0:64, :], c[64:128, :], A.min)
+        z, c = T["z%d" % i], WIDE[i]
+        return tt(k)(T["h%d" % i][0:64, 0:c], z[0:64, 0:c], z[64:128, 0:c], A.add)
 
-    def spread(i, h, a, k):
-        return [tt(k)(T["m%d" % i][block(b), :], h[block(a), :], h[block(a + 1), :], A.min) for b in range(4)][-1]
+    def spread(i, ha, hb, *k):
+        return [tt(*k)(T["m%d" % i][block(b), :], ha, hb, merge[i]) for b in range(4)][-1]
 
     def blank(i, *after):
-        for a in range(0, LENGTH[i] + 32, 256):
-            b = min(LENGTH[i] + 32, a + 256)
-            k = act(*after)(T["win%d" % i][:, a:b], T.ramp[:, 0:b - a], ID, BIG, 0.0)
+        for a in range(0, LENGTH[i] + 32, 288):
+            b, c = min(LENGTH[i] + 32, a + 288), start[i]
+            k = act(*after)(T["win%d" % i][:, c + a:c + b], T.ramp[:, 0:b - a], ID, BIG if i == 1 else T.cc[:, 3:4], 0.0)
         return k
+
+    def pair(rows, c, a, b, *after):
+        return act(*after)(T.cc[rows, c:c + 2], T.ramp[rows, 0:2], ID, a, b - a)
 
     mine = slice(32 * p4, 32 * p4 + 16)
     for e, queue in enumerate((g.sync, g.scalar)):
@@ -140,104 +142,106 @@ def rank_program(g, core, T, topo):
     g.sync.dma_start(T.xt[:, 8:1032], T.x[:]).then_inc(S.lx, 16)
     g.sync.dma_start(T.wt[:], T.w[:]).then_inc(S.lw, 16)
 
-    k_ramp = iota(T.ramp[:], [[1, 256]], 0)
-    fill()(T.two[:], 2.0)
-    k = fill()(T.pr[:, 24:56], 0.0)
+    k_low = iota(T.ramp[:, 0:128], [[1, 128]], 0)
+    iota(T.ramp[:, 128:256], [[1, 128]], 128)
+    k = fill()(T.pr[:], 0.0)
     for rows in ((block(1), side(2)), (block(0), side(2)), (side(0), block(3)), (slice(0, 96),))[p4]:
         k_dm = fill()(T.dmx[rows, mine], 0)
-    ka = scan(k)(T.pr[:, 0:24], T.two[:], T.pr[:, 32:56], 0.5, A.mult, A.add)
-    act(k)(T.pr[block(o), SP:SQ + 1], T.two[block(o), 0:2], CP, 0.0, 2.0 ** (FOUR - par - 1))
-    kb = act()(T.pr[side(pb), SP:SP + 1], T.two[side(pb), 0:1], CP, 0.0, 2.0 ** (TWO - p4 - 1))
+    for rows, c, s in ((every, slice(S3, S3 + 1), ONE - q), (every, slice(S2, S2 + 1), ONE - (q ^ 4)),
+                       (block(o), slice(SQ, 32, 8), FOUR - par)):
+        ka = fill(k)(T.pr[rows, c], 2.0 ** s)
+    for rows, c, s in ((side(pb), slice(SP, 32, 16), TWO - p4), (side(pa), slice(S1, S1 + 1), TWO - (p4 ^ 2)),
+                       (block(p4), slice(S0, S0 + 1), FOUR - 1 + par)):
+        kb = act(k)(T.pr[rows, c], T.pr[rows, slice(c.start + 32, c.stop + 32, c.step)], ID, 2.0 ** s, 0.0)
     k_x = fill()(T.xt[:, 0:8], 0.0)
     k = tp(ka, kb)(T.pw[:], T.pr[:, 0:32])
     fill()(T.ab[:, 257:288], 0.0)
-    k = ts(k, k_ramp)(T.ti[:], T.ramp[:], T.pw[:, 0:1], None, A.mult)
     fill()(T.ab[:, 544:576], 0.0)
-    k = ts(k)(T.ti[:], T.ti[:], SETS, None, A.bitwise_and)
-    fill()(T.ex[0:32, :], 0.0)
-    k_tf = ts(k)(T.tf[:], T.ti[:], T.pw[:, 0:1], None, A.is_ge)
+    ks = [ts(k, k_low)(T.ti[:, a:a + 128], T.ramp[:, 0:128], float(a), T.pw[:, 0:1], A.add, A.mult) for a in (0, 128)]
+    ks = [ts(k)(T.ti[:, a:a + 128], T.ti[:, a:a + 128], SETS, None, A.bitwise_and) for k, a in zip(ks, (0, 128))]
+    ks = [ts(k)(T.tf[:, a:a + 128], T.ti[:, a:a + 128], T.pw[:, 0:1], None, A.is_ge) for k, a in zip(ks, (0, 128))]
 
-    iota(T.ci[:, 128:160], [[0, 2], [1, 16]], 0, 1)
     need("gp", *k_dm)
     g.wait_ge(S.ld, 32)
-    masks = 0
-    for i, peers in enumerate(PEERS):
-        es = [e for e in topo.engines(core, T.cores[q ^ 1])[i::2] if all(e in topo.engines(core, T.cores[q ^ d]) for d in peers)]
-        ids = [DstId(rid=topo.addr(T.cores[q ^ d])[0], pnc=topo.addr(T.cores[q ^ d])[1]) for d in peers]
-        g.remote_dma_fused([RemoteDMATransfer(dst_ids=ids, dma_engine_mask=sum(1 << e for e in es), remote_sem=S.mk,
-                                              srcs=[T.dmx[:, mine]], dsts=[T.dmx[:, mine] for d in peers])], local_sem=S.l0)
-        left["l0"] += len(es)
-        masks += len(es) * len(peers)
+    peers = [T.cores[q ^ d] for d in (1, 2, 3)]
+    es = [e for e in topo.engines(core, peers[0])[::2] if all(e in topo.engines(core, d) for d in peers)]
+    ids = [DstId(rid=topo.addr(d)[0], pnc=topo.addr(d)[1]) for d in peers]
+    g.remote_dma_fused([RemoteDMATransfer(dst_ids=ids, dma_engine_mask=sum(1 << e for e in es), remote_sem=S.mk,
+                                          srcs=[T.dmx[:, mine]], dsts=[T.dmx[:, mine] for d in peers])], local_sem=S.l0)
+    left["l0"] += len(es)
 
-    iota(T.ci[:, 0:32], [[0, 2], [s2 - s3, 2], [32, 8]], s3)
-    iota(T.ci[:, 32:64], [[0, 2], [s0 - s1, 2], [32, 8]], s1)
-    k_ci = iota(T.ci[:, 64:128], [[16, 2], [-1, 2], [1, 16]], 1)
-    k_fj = iota(T.fj[:], [[0, 4], [1, 8]], TRASH, 8)
-    k = tp(k_ci)(T.ct[:], T.ci[:])
+    k_ramp = iota(T.ramp[:, 256:288], [[0, 2], [1, 16]], 0, 1)
+    for a, c, b in ((0, 16, 0), (32, 16, 8), (64, 8, 0)):
+        iota(T.ci[:, a:a + 16], [[1, 8], [c + 1, 2]], b)
+        k_ci = iota(T.ci[:, a + 16:a + 32], [[1, 8], [-c, 2]], b + c)
+    k = tp(k_ramp)(T.ct[:], T.ramp[:])
     k_q = quant(k_x, ("lx", 16))(T.q0[:], T.s0[:], T.xt[:])
-    k_gl = cp(k)(T.gls[:, 0:5], T.ct[:, 0:160:32])
-    k_wq = quant(("lw", 16))(T.wq[:], T.ws[:], T.wt[:])
-    last, last2 = T.gls[:, 2:3], T.gls[:, 2:4]
+    k_gl = cp(k)(T.gls[:, 0:9], T.ct[:, 0:288:32])
+    k_fj = ts()(T.fj[:], T.ct[:, 0:256:16], float(TRASH), None, A.add)
+    fill()(T.ex[0:32, :], -turned * half)
+    held, diagonal, last2, last = T.gls[:, 0:8], T.gls[:, 8:9], T.gl2[:, 0:2], T.gl2[:, 2:3]
     copy(1, 0, 0, 1, 257, "c1", ("l0", left["l0"]), k_q, k_q)
     copy(2, 0, 0, 1, 257, "c2")
-    copy(3, 256, 0, 1, 257, "c3")
-    act()(T.ab[:, 256:257], T.two[:, 0:1], ID, 1.0 - BIG, 0.0)
-    act()(T.z1[:, 13:17], T.two[:, 0:4], CP)
-    for rows, c, value in ((every, 0, -1.0), (block(p4), 1, 0.0), (block(o), 1, 256.0), (side(pb), 1, 384.0),
-                           (block(p4), 2, MID - 1.0), (block(o), 2, MID - 257.0), (side(pb), 2, MID - 1.0)):
-        k_cc = act()(T.cc[rows, c:c + 1], T.two[rows, 0:1], ID, value, 0.0)
+    if not half:
+        copy(3, 257, 0, 2, 256, "c3")
+        copy(3, 0, 0, 0, 1, "c3")
+    for rows, a, b in ((block(p4), 1.0, BACK), (block(o), -1.0, BACK + 191.0), (side(pb), 1.0, BACK)):
+        pair(rows, 0, a, b, k_low)
+    for rows, a, b in ((block(p4), MID - 1.0, 0.0), (block(o), MID - 257.0, 256.0), (side(pb), MID - 1.0, 384.0)):
+        k_cc = pair(rows, 2, a, b)
+    for rows, a, b in ((side(pa), -1.0, -1.0), (block(p4 ^ 2), -1.0, -1.0), (block(p4 ^ 3), -192.0, 1.0)):
+        pair(rows, 4, a, b)
+    act()(T.ab[:, 256:257], T.ramp[:, 0:1], ID, 1.0 - BIG, 0.0)
+    for a in (192, 480):
+        act()(T.tr1[:, a:a + 64], T.ramp[:, 0:64], CP)
     blank(1, k_ramp)
-    blank(2)
+    k_w2 = blank(2, k_cc)
 
-    k = cp(k_gl, ("ld", 32), ("mk", masks))(T.dmu[:], T.dmx[:].indirect(T.gls[:, 4:5]))
-    ka = ts(k, k_tf)(T.ab[:, 0:256], T.tf[:].indirect(T.dmu[:]), 1.0 - BIG, None, A.mult)
-    kb = act(k)(T.ab[:, 288:544], T.tf[:].indirect(T.dmu[:]), CP, 0.0, BIG)
-    k = scan(ka, kb)(T.zs[:], T.ab[:, 0:288], T.ab[:, 287:575], BIG - 1.0, A.add, A.add)
-    k_tr = tp(k)(T.tr[:], T.zs[:])
-    k_su = ts(k_tr)(T.su[:], T.tr[:, SQ:256:32], 255.0, None, A.min)
-    k_y = tt(k_fj)(T.yy[:], T.tr[:].indirect(T.gls[:, 0:2]), T.fj[:], A.min)
-    k_e1 = act(k_tr)(T.ex[block(1), :], T.tr[block(0), 256:288], CP)
-    k_vu = act(k_su, k_cc)(T.vu[:], T.ramp[:].indirect(T.su[:]), ID, T.cc[:, 2:3], -1.0)
-    k_cv = act()(T.cc[block(pb + 1), 0:1], T.tr[block(pb), 256 + SP:257 + SP], ID, -1.0, -1.0)
-    k_w3 = blank(3)
+    H = {}
+    nh = T.nn[:, 0:1]
 
-    ts(k_y)(T.p1[block(pa + 1), :], T.yy[block(pa + 1), 16:24], T.tr[block(pa), 256 + s1:257 + s1], None, A.add)
-    cp()(T.p1[block(pa), :], T.yy[block(pa), 16:24])
-    for a in (pb, pb + 1):
-        k = cp()(T.p1[block(a), :], T.yy[block(p4), 24:32])
-    H = {"p1": k, "e1": k_e1}
-    lo = min(s2, s3)
-    c2, c3 = (s2 - lo) // 4, (s3 - lo) // 4
-    nh = T.nn[:, c3:c3 + 1]
+    def sets():
+        k = H["masks"]
+        return (ts(k, ks[1])(T.ab[:, 0:256], T.tf[:].indirect(T.dmu[:]), 1.0 - BIG, None, A.mult),
+                act(k)(T.ab[:, 288:544], T.tf[:].indirect(T.dmu[:]), CP, 0.0, BIG))
+
+    def counts():
+        k = tp(H["scan"])(T.tr[:], T.zs[:])
+        H["v1"] = act(H["scan"])(T.vu[:], T.zs[:].indirect(held), ID, T.cc[:, 2:3], -1.0)
+        H["e1"] = act(k)(T.ex[block(1), :], T.tr[block(0), 256:288], ID, -turned * half)
+        H["v2"] = H["v3"] = act()(T.vr[:], T.zs[:].indirect(held), ID, T.cc[:, 4:5], T.cc[:, 5:6])
+        H["blank3"] = blank(3)
+        return k
+
+    def places01():
+        tt(H["counts"], k_fj)(T.yo[side(pa), :], T.tr[side(pa), S1:256:32], T.fj[side(pa), 0:16:2], A.min)
+        return [tt()(T.yo[block(a), :], T.tr[block(p4), S0:256:32], T.fj[block(p4), 0:16:2], A.min) for a in (pb, pb + 1)][1]
 
     def earlier(a):
         return tt(H["e%d" % (a - 1)])(T.ex[block(a), :], T.ex[block(a - 1), :], T.tr[block(a - 1), 256:288], A.add)
 
-    def values():
-        k = ts()(T.st[:], T.tr[:, SP:256:32], 255.0, None, A.min)
-        return act(k, k_cv)(T.vr[:], T.ramp[:].indirect(T.st[:]), ID, T.cc[:, 0:1], -1.0)
-
     def lengths():
-        k = tt(H["e3"])(T.tot[block(3), :], T.ex[block(3), lo:lo + 5:4], T.tr[block(3), 256 + lo:261 + lo:4], A.add)
+        k = tt(H["e3"])(T.tot[block(3), :], T.ex[block(3), S3:32:16], T.tr[block(3), 256 + S3:288:16], A.add)
         k = on("gp", g.partition_broadcast)(k)(T.nn[:], T.tot[96:97, :], 128)
-        send(q ^ 4, T.n2[:], T.nn[:, c2:c2 + 1], "rn", k)
+        send(q ^ 4, T.n2[:], T.nn[:, 1:2], "rn", k)
         return k
 
     def rows3():
         if half:
-            act(k_w3)(T.win3[block(p4), 16:272], T.ramp[block(p4), :], RELU, 256.0, -1.0)
-            return act()(T.win3[block(p4), 272:528], T.ramp[block(p4), :], RELU, 0.0, -1.0)
-        k = act(H["tot"])(T.cc[:, 3:4], nh, ID, 256.0)
-        act(k_w3)(T.win3[block(p4), 272:528], T.ramp[block(p4), :], RELU, T.nn[block(p4), c3:c3 + 1], -1.0)
-        return act(k)(T.win3[block(p4), 16:272], T.ramp[block(p4), :], RELU, T.cc[block(p4), 3:4], -1.0)
+            H["n2"] = act(("rn", 16))(T.cc[:, 8:9], T.n2[:], ID, turned)
+            return H["blank3"]
+        act(H["tot"])(T.cc[:, 6:7], nh, ID, 0.0, -0.5)
+        k = act()(T.cc[:, 7:8], nh, ID, 128.0, -0.5)
+        return [act(k)(T.win3[block(p4), 16 + 256 * h:272 + 256 * h], T.ramp[block(p4), 0:256], RELU,
+                       T.cc[block(p4), 6 + h:7 + h], 0.5) for h in range(2)][1]
 
     def places3():
         if half:
-            return ts(H["e3"], ("rn", 16))(T.p3[:], T.yy[:, 0:8], T.ex[:, s3:s3 + 1], T.n2[:], A.add, A.add)
-        return ts(H["e3"])(T.p3[:], T.yy[:, 0:8], T.ex[:, s3:s3 + 1], None, A.add)
+            return ts(H["e3"], H["n2"])(T.p3[:], T.yy[:, 0:16:2], T.ex[:, S3:S3 + 1], T.cc[:, 8:9], A.add, A.add)
+        return ts(H["e3"])(T.p3[:], T.yy[:, 0:16:2], T.ex[:, S3:S3 + 1], None, A.add)
 
     def exchange0():
-        k = H["side0"]
+        k = H["off0"]
         ka, kb = pick(T.slq0[:], T.sls0[:], T.q0[:], T.s0[:], T.off0[:, 0:8], [k], [k])
         send(q ^ 1, T.q1[:, 257:385].bitcast(dt.uint8), T.slq0[:].bitcast(dt.uint8), "r0c", ka)
         send(q ^ 1, T.s1[:, 257:385], T.sls0[:], "r0s", kb)
@@ -249,56 +253,68 @@ def rank_program(g, core, T, topo):
                       [k, ("c1", 32), ("r0c", 16)], [k, ("c1", 32), ("r0s", 16)])
         send(q ^ 2, T.q2[:, 385:577].bitcast(dt.uint8), T.slq1[:].bitcast(dt.uint8), "r1c", ka)
         send(q ^ 2, T.s2[:, 385:577], T.sls1[:], "r1s", kb)
-        act(H["tot"], ("rn", 16))(T.lnt[:, 0:1], nh, ID, T.n2[:])
-        need("y", *act()(T.lnt[block(p4), 1:2], T.tr[block(p4), 256 + s3:257 + s3], CP))
+        if not half:
+            H["n2"] = act(("rn", 16))(T.cc[:, 8:9], T.n2[:], ID, turned)
+        act()(T.lnt[block(p4), 1:2], T.tr[block(p4), 256 + S3:257 + S3], CP)
+        need("y", *act(H["tot"], H["n2"])(T.lnt[:, 0:1], nh, ID, T.cc[:, 8:9]))
         g.sync.dma_start(T.ln[:], T.lnt[32 * p4:32 * p4 + 1, 0:2]).then_inc(S.lnd, 16)
-        copy(3, 513, 2, 257, 320, "c3", ("c2", 64), ("r1c", 16), ("r1s", 16))
+        if not half:
+            copy(3, 513, 2, 257, 320, "c3", ("c2", 64), ("r1c", 16), ("r1s", 16))
 
     def exchange2():
         k = H["off2"]
         ka, kb = pick(T.slq2[:], T.sls2[:], T.q2[:], T.s2[:], T.off2[:], [k, ("c2", 64), ("r1c", 16)], [k, ("c2", 64), ("r1s", 16)])
-        send(q ^ 4, T.q3[:, 0:256].bitcast(dt.uint8), T.slq2[:].bitcast(dt.uint8), "r2c", ka)
-        send(q ^ 4, T.s3[:, 0:256], T.sls2[:], "r2s", kb)
+        send(q ^ 4, T.q3[:, half:256 + half].bitcast(dt.uint8), T.slq2[:].bitcast(dt.uint8), "r2c", ka)
+        send(q ^ 4, T.s3[:, half:256 + half], T.sls2[:], "r2s", kb)
 
-    def offsets3():
-        k = H["spread3"]
-        if half:
-            return ([ts(k)(T.off3[:, 16:32], T.m3[:, 16:33].indirect(last), -1.0, None, A.mult)] * 2
-                    + [ts()(T.off3[:, 0:16], T.m3[:].indirect(last), -1.0, 256.0, A.mult, A.add)] * 2)
-        return [ts(k)(T.off3[:], T.m3[:].indirect(last2), -1.0, 256.0, A.mult, A.add)] * 4
+    def piece(i, a, b):
+        ready = {1: ["p1", "v1"], 2: ["p2", "v2"], 3: ["p3", "v3", "w3"]}[i] + ["s%d" % i] * (a > 0)
+        H["s%d" % i] = scatter(i, a, b, T.vu if i == 1 else T.vr, *[H[r] for r in ready])
 
     steps = {
-        "tot": lengths, "w3": rows3, "p3": places3,
-        "e2": lambda: earlier(2), "e3": lambda: earlier(3), "s1": lambda: scatter(1, T.vu[:], H["p1"], k_vu),
-        "p2": lambda: ts(H["e3"])(T.p2[:], T.yy[:, 8:16], T.ex[:, s2:s2 + 1], None, A.add),
-        "st": values, "s2": lambda: scatter(2, T.vr[:], H["p2"], H["st"]),
-        "s3": lambda: scatter(3, T.vr[:], H["p3"], H["w3"], H["st"]),
-        "off0": lambda: ts(H["jb1"])(T.off0[:], T.z1[:].indirect(last), -1.0, MID + 1.0, A.mult, A.add),
-        "side0": lambda: cp(H["off0"])(T.off0[side(pa), :], T.off0[side(pb), :]),
-        "spread1": lambda: spread(1, T.z1, pa, H["jb1"]),
+        "tot": lengths, "w3": rows3, "p3": places3, "counts": counts, "sets": sets, "y1": places01,
+        "masks": lambda: cp(k_gl, ("ld", 32), ("mk", 3 * len(es)))(T.dmu[:], T.dmx[:].indirect(diagonal)),
+        "turn2": lambda: tp(k_ci)(T.cu[:], T.ci[:]),
+        "lists2": lambda: cp(H["turn2"])(T.gl2[:, 0:3], T.cu[:, 0:96:32]),
+        "scan": lambda: scan(*H["sets"])(T.zs[:], T.ab[:, 0:288], T.ab[:, 287:575], BIG - 1.0, A.add, A.add),
+        "y": lambda: tt(H["counts"])(T.yy[:], T.tr[:, S3:256:16], T.fj[:], A.min),
+        "wq": lambda: quant(("lw", 16))(T.wq[:], T.ws[:], T.wt[:]),
+        "p1": lambda: ts(H["y1"])(T.p1[:], T.yo[:], T.cc[:, 0:1], T.cc[:, 1:2], A.mult, A.add),
+        "e2": lambda: earlier(2), "e3": lambda: earlier(3), "s1": lambda: scatter(1, 0, 8, T.vu, H["p1"], H["v1"]),
+        "p2": lambda: ts(H["e3"])(T.p2[:], T.yy[:, 1:16:2], T.ex[:, S2:S2 + 1], 1.0 - 2 * half, A.add, A.mult),
+        "j0": lambda: [join(1, T.z0[side(a), :], side(pb), H["tb1"]) for a in (pa, pb)][1],
+        "j1": lambda: [join(1, T.z1[block(pa), 17 * a:17 * a + 17], block(pa + a), H["tb1"]) for a in range(2)][1],
+        "off0": lambda: ts(H["j0"], H["lists2"])(T.off0[:], T.z0[:].indirect(last), -1.0, MID + 1.0, A.mult, A.add),
+        "spread1": lambda: spread(1, T.z1[block(pa), 0:17], T.z1[block(pa), 17:34], H["j1"]),
         "off1": lambda: ts(H["spread1"])(T.off1[:], T.m1[:].indirect(last), -1.0, MID, A.mult, A.add),
-        "off2": lambda: ts(H["spread2"])(T.off2[:], T.m2[:].indirect(last), -1.0, None, A.mult),
-        "off3": offsets3, "x0": exchange0, "x1": exchange1, "x2": exchange2,
+        "off2": lambda: ts(H["spread2"])(T.off2[:], T.m2[:].indirect(last), -1.0, EMPTY, A.mult, A.add),
+        "off3": lambda: ts(H["spread3"])(T.off3[:], T.m3[:].indirect(last2), -1.0, EMPTY + 256.0 * (1 - half), A.mult, A.add),
+        "x0": exchange0, "x1": exchange1, "x2": exchange2,
     }
     for i in (1, 2, 3):
-        steps.update({
-            "ta%d" % i: lambda i=i: turn(i, False, H["s%d" % i]), "tb%d" % i: lambda i=i: turn(i, True, H["s%d" % i]),
-            "ja%d" % i: lambda i=i: join(i, False, H["ta%d" % i]), "jb%d" % i: lambda i=i: join(i, True, H["tb%d" % i])})
+        steps.update({"ta%d" % i: lambda i=i: turn(i, False, H["s%d" % i]), "tb%d" % i: lambda i=i: turn(i, True, H["s%d" % i])})
     for i in (2, 3):
         steps.update({
-            "lift%d" % i: lambda i=i: lift(i, H["jb%d" % i]), "halve%d" % i: lambda i=i: halve(i, H["lift%d" % i]),
-            "spread%d" % i: lambda i=i: spread(i, T["h%d" % i], 0, H["halve%d" % i])})
+            "j%d" % i: lambda i=i: join(i, T["z%d" % i][:, 0:WIDE[i]], every, H["tb%d" % i]),
+            "halve%d" % i: lambda i=i: halve(i, H["j%d" % i]),
+            "spread%d" % i: lambda i=i: spread(i, T["h%d" % i][block(0), 0:WIDE[i]], T["h%d" % i][block(1), 0:WIDE[i]], H["halve%d" % i])})
     for name in ORDER:
-        H[name] = steps[name]()
+        if ":" in name:
+            piece(*[int(c) for c in name[1:].split(":")])
+        else:
+            H[name] = steps[name]()
 
     def product(i):
         a, b = RUNS[half][i]
-        lo = 256 if half and a >= 256 else 0
-        held = [H["off3"][i], ("c3", 64)]
-        ka, kb = pick(T.qa[:, a:b], T.sa[:, a:b], T.q3[:, lo:833], T.s3[:, lo:833], T.off3[:, a // 16:b // 16],
-                      held + [("r2c", 16)] * (lo == 0), held + [("r2s", 16)] * (lo == 0))
-        return [mm(k_wq, ka, kb)(T.ps[:, 512 * (2 * i + w):512 * (2 * i + w) + b - a], T.wq[:, 128 * w:128 * w + 128],
-                                 T.ws[:, 128 * w:128 * w + 128], T.qa[:, a:b], T.sa[:, a:b], True, True) for w in range(2)]
+        qi, si, landed = (T.q2, T.s2, []) if half else (T.q3, T.s3, [("c3", 96)])
+        ka, kb = pick(T.qa[:, a:b], T.sa[:, a:b], qi[:], si[:], T.off3[:, a // 16:b // 16],
+                      [H["off3"]] + landed + [("r2c", 16)] * (1 - half), [H["off3"]] + landed + [("r2s", 16)] * (1 - half))
+        terms = [(T.qa, T.sa, (ka, kb))] + [(T.q3, T.s3, (("r2c", 16), ("r2s", 16)))] * (half and a < 256)
+        for j, (qm, sm, waits) in enumerate(terms):
+            ks = [mm(H["wq"], *waits)(T.ps[:, 512 * (2 * i + w):512 * (2 * i + w) + b - a], T.wq[:, 128 * w:128 * w + 128],
+                                      T.ws[:, 128 * w:128 * w + 128], qm[:, a:b], sm[:, a:b], j == 0, j == len(terms) - 1)
+                  for w in range(2)]
+        return ks
 
     def store(i, ks):
         a, b = RUNS[half][i]

@@ -3,20 +3,22 @@ from concourse.mybir import dt, AluOpType, ActivationFunctionType
 
 F32, I32, BF, U16, U8, Q8 = "float32", "int32", "bfloat16", "uint16", "uint8", "float8_e4m3fn_x4"
 BIG = 4096.0
-TRASH = 528
-BACK = 592
-BACK2 = 800
+BACK = 1856
+LAST = 576
 EMPTY = 2.0 * (256 + 384 + 384)
-WIN = 1392
+WIN = 3936
 ONE, TWO, FOUR = 7, 15, 23
 SETS = 2 ** ONE + (2 ** TWO + 2 ** (TWO + 4)) + sum(2 ** (FOUR + 2 * i) for i in range(4))
-SQ, SP, S0, S1, S2, S3 = 0, 8, 4, 3, 18, 2
+SQ, SP, S3, S1, S2, S0, SPARE = 0, 8, 6, 14, 22, 30, 2
 LENGTH = {1: 192, 2: 256, 3: 512}
 WIDE = {1: 17, 2: 17, 3: 33}
 MID = 192.0
 RUNS = (((0, 128), (128, 256), (256, 384), (384, 512)), ((256, 384), (384, 512), (0, 128), (128, 256)))
-ORDER = ("wq masks turn2 sets lists2 scan counts y1 y p1 e2 s1 e3 ta1 tb1 p2 tot j0 j1 off0 s2:0:2 x0 s2:2:8 spread1 off1 ta2 tb2 "
-         "w3 p3 j2 x1 s3:0:8 halve2 spread2 off2 ta3 x2 tb3 j3 halve3 spread3 off3").split()
+ORDER = [("masks xq0 sets xq1 scan unwanted counts turn2 y e1 p1 lists2 e2 s1 e3 ta1 tb1 tot p2 j0 j1 off0 spread1 from3 x0 wide1 "
+          "s2:0:8 w3 off1 ta2 tb2 early1 J2 p3 x1 H2 s3:0:2 S2 wide2 s3:2:8 off2 ta3 tb3 x2 j3 x3 ln halve3 spread3 off3 wq0 wq1").split()] * 2
+END = ["p0 p1 p2 v00 s01 p3 v10 v11 v20 s21 v30 s31".split()] * 2
+BY = {1: 2, 2: 2, 3: 4}
+PARTS = ((0, 128), (128, 256))
 
 
 def _s(n, d):
@@ -24,16 +26,17 @@ def _s(n, d):
 
 
 SCRATCH = {
-    "dmx": _s(128, I32), "dmu": _s(16, U16), "xt": _s(1032, BF), "wt": _s(1024, BF),
-    "q0": _s(258, Q8), "s0": _s(258, U8), "q1": _s(386, Q8), "s1": _s(386, U8),
+    "dmx": _s(128, I32), "dmu": _s(16, U16), "xt": _s(1040, BF), "wt": _s(1024, BF),
+    "q0": _s(260, Q8), "s0": _s(260, U8), "q1": _s(386, Q8), "s1": _s(386, U8),
     "q2": _s(578, Q8), "s2": _s(578, U8), "q3": _s(834, Q8), "s3": _s(834, U8),
     "slq0": _s(128, Q8), "sls0": _s(128, U8), "slq1": _s(192, Q8), "sls1": _s(192, U8),
     "slq2": _s(256, Q8), "sls2": _s(256, U8),
     "qa": _s(512, Q8), "sa": _s(512, U8), "wq": _s(256, Q8), "ws": _s(256, U8),
-    "pr": _s(64, F32), "pw": _s(32, F32), "ramp": _s(288, BF), "ct": _s(288, BF), "ti": _s(256, I32), "tf": _s(256, BF),
-    "ci": _s(96, BF), "cu": _s(96, BF), "fj": _s(16, F32), "cc": _s(10, F32), "gls": _s(10, U16), "gl2": _s(4, U16),
-    "ab": _s(576, F32), "zs": _s(288, BF), "tr": _s(288, BF), "ex": _s(32, F32), "tot": _s(2, F32), "nn": _s(2, F32),
-    "vr": _s(128, BF), "vu": _s(128, BF), "yo": _s(8, F32), "yy": _s(16, F32), "n2": _s(1, F32),
+    "pr": _s(96, F32), "pw": _s(64, F32), "ramp": _s(288, BF), "ct": _s(288, BF), "ti": _s(256, I32), "tf": _s(256, BF),
+    "ci": _s(96, BF), "cu": _s(96, BF), "cc": _s(12, F32), "first": _s(1, BF), "gls": _s(10, U16), "gl2": _s(4, U16),
+    "one": _s(288, BF), "un": _s(288, BF), "ut": _s(256, BF),
+    "zs": _s(288, BF), "tr": _s(288, BF), "ex": _s(32, F32), "tot": _s(2, F32), "nn": _s(2, F32),
+    "vr": _s(128, BF), "vu": _s(128, BF), "yy": _s(64, F32), "n2": _s(1, F32),
     "p1": _s(8, U16), "p2": _s(8, U16), "p3": _s(8, U16),
     "win1": _s(WIN, BF), "win2": _s(WIN, BF), "win3": _s(WIN, BF), "tr1": _s(544, BF), "tr2": _s(544, BF), "tr3": _s(1056, BF),
     "z0": _s(17, F32), "z1": _s(34, F32), "z2": _s(34, F32), "z3": _s(66, F32),
@@ -42,8 +45,8 @@ SCRATCH = {
     "lnt": _s(4, F32), "ys": _s(1024, F32),
     "ps": ("psum", [128, 4096], F32),
 }
-SEMAPHORES = ["ld", "lx", "lw", "v", "s", "t", "gp", "mk", "r0c", "r0s", "r1c", "r1s", "r2c", "r2s", "rn",
-              "c1", "c2", "c3", "l0", "l1", "lo", "yo", "lnd"]
+SEMAPHORES = ["ld", "lx", "lw", "v", "s", "t", "gp", "mk", "r0c", "r0s", "r1c", "r1s", "r2c", "r2s", "r3c", "r3s", "rn",
+              "c1", "c2", "c3", "l0", "lo", "yo", "lnd"]
 
 
 def rank_program(g, core, T, topo):
@@ -56,8 +59,7 @@ def rank_program(g, core, T, topo):
     p4, half, par = q & 3, q >> 2, q & 1
     pa, pb, o = p4 & 2, 2 - (p4 & 2), p4 ^ 1
     every = slice(0, 128)
-    start, merge = {1: BACK, 2: BACK2 * half, 3: 0}, {1: A.min, 2: A.add, 3: A.add}
-    turned = BACK2 + 255.0
+    start, merge = {1: BACK, 2: 0, 3: 0}, {1: A.min, 2: A.add, 3: A.add}
 
     def block(a):
         return slice(32 * a, 32 * a + 32)
@@ -66,7 +68,7 @@ def rank_program(g, core, T, topo):
         return slice(32 * a, 32 * a + 64)
 
     queues = {"v": g.vector, "s": g.scalar, "t": g.tensor, "gp": g, "y": g.sync}
-    n, seen, left, n_yo = {"v": 0, "s": 0, "t": 0, "gp": 0}, {}, {"l0": 0, "l1": 0, "lo": 0}, [0]
+    n, seen, left, n_yo = {"v": 0, "s": 0, "t": 0, "gp": 0}, {}, {"l0": 0, "lo": 0}, [0]
 
     def need(queue, sem, count):
         if seen.get((queue, sem), 0) < count:
@@ -92,11 +94,11 @@ def rank_program(g, core, T, topo):
     def iota(out, pat, base, cm=0):
         return on("gp", g.iota)()(out, pat, base, cm, allow_small_or_imprecise_dtypes=True)
 
-    def send(dst, out, in_, sem, after, gone="lo"):
+    def send(dst, out, in_, sem, after):
         need("gp", *after)
         rid, pid, _ = topo.addr(T.cores[dst])
-        g.remote_dma(out, in_, S[sem], S[gone], pid, rid, topo.mask(core, T.cores[dst]))
-        left[gone] += len(topo.engines(core, T.cores[dst]))
+        g.remote_dma(out, in_, S[sem], S.lo, pid, rid, topo.mask(core, T.cores[dst]))
+        left["lo"] += len(topo.engines(core, T.cores[dst]))
 
     def copy(i, a, j, b, count, sem, *after):
         for w in after[:-1]:
@@ -125,7 +127,19 @@ def rank_program(g, core, T, topo):
         return tt(k)(T["h%d" % i][0:64, 0:c], z[0:64, 0:c], z[64:128, 0:c], A.add)
 
     def spread(i, ha, hb, *k):
-        return [tt(*k)(T["m%d" % i][block(b), :], ha, hb, merge[i]) for b in range(4)][-1]
+        return [tt(*k)(T["m%d" % i][block(b), :], ha, hb, merge[i]) for b in range(BY[i])][-1]
+
+    def widen(i):
+        m, k = T["m%d" % i], H["spread%d" % i]
+        if BY[i] == 2:
+            k = act(k)(m[64:128, :], m[0:64, :], CP)
+        if BY[i] == 1:
+            k = [act(k)(m[block(b), :], m[block(0), :], CP) for b in (1, 2, 3)][2]
+        H["spread%d" % i] = k
+
+    def both(i, a, b, c, sem, ka, kb):
+        send(q ^ (1 << i), T["q%d" % (i + 1)][:, c:c + b - a].bitcast(dt.uint8), T["slq%d" % i][:, a:b].bitcast(dt.uint8), sem + "c", ka)
+        send(q ^ (1 << i), T["s%d" % (i + 1)][:, c:c + b - a], T["sls%d" % i][:, a:b], sem + "s", kb)
 
     def blank(i, *after):
         for a in range(0, LENGTH[i] + 32, 288):
@@ -140,26 +154,26 @@ def rank_program(g, core, T, topo):
     for e, queue in enumerate((g.sync, g.scalar)):
         queue.dma_start(T.dmx[32 * p4 + 16 * e:32 * p4 + 16 * e + 16, mine], T.dm[:]).then_inc(S.ld, 16)
     g.sync.dma_start(T.xt[:, 8:1032], T.x[:]).then_inc(S.lx, 16)
-    g.sync.dma_start(T.wt[:], T.w[:]).then_inc(S.lw, 16)
 
     k_low = iota(T.ramp[:, 0:128], [[1, 128]], 0)
     iota(T.ramp[:, 128:256], [[1, 128]], 128)
+    k_ramp = iota(T.ramp[:, 256:288], [[0, 2], [1, 16]], 0, 1)
     k = fill()(T.pr[:], 0.0)
     for rows in ((block(1), side(2)), (block(0), side(2)), (side(0), block(3)), (slice(0, 96),))[p4]:
         k_dm = fill()(T.dmx[rows, mine], 0)
     for rows, c, s in ((every, slice(S3, S3 + 1), ONE - q), (every, slice(S2, S2 + 1), ONE - (q ^ 4)),
-                       (block(o), slice(SQ, 32, 8), FOUR - par)):
+                       (block(o), slice(SQ, 32, 8), FOUR - par), (every, slice(32 + SPARE, 64, 8), 0)):
         ka = fill(k)(T.pr[rows, c], 2.0 ** s)
     for rows, c, s in ((side(pb), slice(SP, 32, 16), TWO - p4), (side(pa), slice(S1, S1 + 1), TWO - (p4 ^ 2)),
                        (block(p4), slice(S0, S0 + 1), FOUR - 1 + par)):
-        kb = act(k)(T.pr[rows, c], T.pr[rows, slice(c.start + 32, c.stop + 32, c.step)], ID, 2.0 ** s, 0.0)
-    k_x = fill()(T.xt[:, 0:8], 0.0)
-    k = tp(ka, kb)(T.pw[:], T.pr[:, 0:32])
-    fill()(T.ab[:, 257:288], 0.0)
-    fill()(T.ab[:, 544:576], 0.0)
+        kb = act(k)(T.pr[rows, c], T.pr[rows, slice(c.start + 64, c.stop + 64, c.step)], ID, 2.0 ** s, 0.0)
+    fill()(T.xt[:, 0:8], 0.0)
+    k = tp(ka, kb)(T.pw[:], T.pr[:, 0:64])
+    fill()(T.un[:, 256:288], 1.0)
+    k_x = fill()(T.xt[:, 1032:1040], 0.0)
     ks = [ts(k, k_low)(T.ti[:, a:a + 128], T.ramp[:, 0:128], float(a), T.pw[:, 0:1], A.add, A.mult) for a in (0, 128)]
     ks = [ts(k)(T.ti[:, a:a + 128], T.ti[:, a:a + 128], SETS, None, A.bitwise_and) for k, a in zip(ks, (0, 128))]
-    ks = [ts(k)(T.tf[:, a:a + 128], T.ti[:, a:a + 128], T.pw[:, 0:1], None, A.is_ge) for k, a in zip(ks, (0, 128))]
+    ks = [ts(k)(T.tf[:, a:a + 128], T.ti[:, a:a + 128], T.pw[:, 0:1], None, A.is_lt) for k, a in zip(ks, (0, 128))]
 
     need("gp", *k_dm)
     g.wait_ge(S.ld, 32)
@@ -170,55 +184,60 @@ def rank_program(g, core, T, topo):
                                           srcs=[T.dmx[:, mine]], dsts=[T.dmx[:, mine] for d in peers])], local_sem=S.l0)
     left["l0"] += len(es)
 
-    k_ramp = iota(T.ramp[:, 256:288], [[0, 2], [1, 16]], 0, 1)
     for a, c, b in ((0, 16, 0), (32, 16, 8), (64, 8, 0)):
         iota(T.ci[:, a:a + 16], [[1, 8], [c + 1, 2]], b)
         k_ci = iota(T.ci[:, a + 16:a + 32], [[1, 8], [-c, 2]], b + c)
+    ts()(T.cc[:, 10:12], T.ramp[:, 3:8:4], T.pw[:, 32:33], None, A.mult)
+    ts()(T.first[:], T.pw[:, 32:33], 512.0, None, A.mult)
     k = tp(k_ramp)(T.ct[:], T.ramp[:])
-    k_q = quant(k_x, ("lx", 16))(T.q0[:], T.s0[:], T.xt[:])
+    fill()(T.ex[0:32, 0:16], half - 1.0)
+    fill()(T.ex[0:32, 16:32], -1.0)
     k_gl = cp(k)(T.gls[:, 0:9], T.ct[:, 0:288:32])
-    k_fj = ts()(T.fj[:], T.ct[:, 0:256:16], float(TRASH), None, A.add)
-    fill()(T.ex[0:32, :], -turned * half)
     held, diagonal, last2, last = T.gls[:, 0:8], T.gls[:, 8:9], T.gl2[:, 0:2], T.gl2[:, 2:3]
-    copy(1, 0, 0, 1, 257, "c1", ("l0", left["l0"]), k_q, k_q)
-    copy(2, 0, 0, 1, 257, "c2")
-    if not half:
-        copy(3, 257, 0, 2, 256, "c3")
-        copy(3, 0, 0, 0, 1, "c3")
-    for rows, a, b in ((block(p4), 1.0, BACK), (block(o), -1.0, BACK + 191.0), (side(pb), 1.0, BACK)):
-        pair(rows, 0, a, b, k_low)
-    for rows, a, b in ((block(p4), MID - 1.0, 0.0), (block(o), MID - 257.0, 256.0), (side(pb), MID - 1.0, 384.0)):
-        k_cc = pair(rows, 2, a, b)
-    for rows, a, b in ((side(pa), -1.0, -1.0), (block(p4 ^ 2), -1.0, -1.0), (block(p4 ^ 3), -192.0, 1.0)):
-        pair(rows, 4, a, b)
-    act()(T.ab[:, 256:257], T.ramp[:, 0:1], ID, 1.0 - BIG, 0.0)
+    for rows, a, b in ((block(p4), MID, 0.0), (block(o), MID - 256.0, 256.0), (side(pb), MID, 384.0)):
+        k_cc = pair(rows, 2, a, b, k_low)
+    for b, a, c in ((p4, -257.0, 1.0), (o, -129.0, 1.0), (p4 ^ 2, -193.0, 1.0), (p4 ^ 3, 0.0, -1.0)):
+        pair(block(b), 4, a, c)
     for a in (192, 480):
         act()(T.tr1[:, a:a + 64], T.ramp[:, 0:64], CP)
+    for rows, a, b in ((block(p4), 1.0, BACK - 1.0), (block(o), -1.0, BACK + 192.0)):
+        pair(rows, 0, a, b)
     blank(1, k_ramp)
-    k_w2 = blank(2, k_cc)
+    for a, b, c in ((0, 128, 10), (128, 288, 11)):
+        ts()(T.one[:, a:b], T.ramp[:, a:b], 0.0, T.cc[:, c:c + 1], A.is_ge, A.add)
 
     H = {}
     nh = T.nn[:, 0:1]
 
+    def own():
+        k = quant()(T.q0[:, 130:260], T.s0[:, 130:260], T.xt[:, 520:1040])
+        copy(1, 0, 0, 1, 257, "c1", ("l0", left["l0"]), k, k)
+        copy(2, 320, 0, 2, 257, "c2")
+        if not half:
+            copy(3, 320, 0, 2, 256, "c3")
+            copy(3, LAST + 256, 0, 0, 1, "c3")
+        g.sync.dma_start(T.wt[:], T.w[:]).then_inc(S.lw, 16)
+        return k
+
     def sets():
         k = H["masks"]
-        return (ts(k, ks[1])(T.ab[:, 0:256], T.tf[:].indirect(T.dmu[:]), 1.0 - BIG, None, A.mult),
-                act(k)(T.ab[:, 288:544], T.tf[:].indirect(T.dmu[:]), CP, 0.0, BIG))
+        return (cp(k, ks[1])(T.un[:, 0:128], T.tf[:].indirect(T.dmu[:, 0:8])),
+                act(k)(T.un[:, 128:256], T.tf[:].indirect(T.dmu[:, 8:16]), CP))
 
     def counts():
         k = tp(H["scan"])(T.tr[:], T.zs[:])
         H["v1"] = act(H["scan"])(T.vu[:], T.zs[:].indirect(held), ID, T.cc[:, 2:3], -1.0)
-        H["e1"] = act(k)(T.ex[block(1), :], T.tr[block(0), 256:288], ID, -turned * half)
-        H["v2"] = H["v3"] = act()(T.vr[:], T.zs[:].indirect(held), ID, T.cc[:, 4:5], T.cc[:, 5:6])
+        act()(T.vr[:], T.zs[:].indirect(held), ID, T.cc[:, 4:5], T.cc[:, 5:6])
+        H["v2"] = blank(2)
         H["blank3"] = blank(3)
         return k
 
     def places01():
-        tt(H["counts"], k_fj)(T.yo[side(pa), :], T.tr[side(pa), S1:256:32], T.fj[side(pa), 0:16:2], A.min)
-        return [tt()(T.yo[block(a), :], T.tr[block(p4), S0:256:32], T.fj[block(p4), 0:16:2], A.min) for a in (pb, pb + 1)][1]
+        ts(H["y"])(T.p1[side(pa), :], T.yy[side(pa), 3::8], T.cc[side(pa), 0:1], T.cc[side(pa), 1:2], A.mult, A.add)
+        return [ts()(T.p1[block(a), :], T.yy[block(p4), 7::8], BACK - 1.0, None, A.add) for a in (pb, pb + 1)][1]
 
     def earlier(a):
-        return tt(H["e%d" % (a - 1)])(T.ex[block(a), :], T.ex[block(a - 1), :], T.tr[block(a - 1), 256:288], A.add)
+        return tt(H["e%d" % (a - 1) if a > 1 else "counts"])(T.ex[block(a), :], T.ex[block(a - 1), :], T.tr[block(a - 1), 256:288], A.add)
 
     def lengths():
         k = tt(H["e3"])(T.tot[block(3), :], T.ex[block(3), S3:32:16], T.tr[block(3), 256 + S3:288:16], A.add)
@@ -228,68 +247,71 @@ def rank_program(g, core, T, topo):
 
     def rows3():
         if half:
-            H["n2"] = act(("rn", 16))(T.cc[:, 8:9], T.n2[:], ID, turned)
             return H["blank3"]
-        act(H["tot"])(T.cc[:, 6:7], nh, ID, 0.0, -0.5)
-        k = act()(T.cc[:, 7:8], nh, ID, 128.0, -0.5)
-        return [act(k)(T.win3[block(p4), 16 + 256 * h:272 + 256 * h], T.ramp[block(p4), 0:256], RELU,
-                       T.cc[block(p4), 6 + h:7 + h], 0.5) for h in range(2)][1]
+        return [act(H["from3"])(T.win3[block(p4), 16 + 256 * h:272 + 256 * h], T.ramp[block(p4), 0:256], RELU,
+                                T.cc[block(p4), 6 + h:7 + h], 0.5) for h in range(2)][1]
 
     def places3():
         if half:
-            return ts(H["e3"], H["n2"])(T.p3[:], T.yy[:, 0:16:2], T.ex[:, S3:S3 + 1], T.cc[:, 8:9], A.add, A.add)
-        return ts(H["e3"])(T.p3[:], T.yy[:, 0:16:2], T.ex[:, S3:S3 + 1], None, A.add)
+            return ts(H["e3"], ("rn", 16))(T.p3[:], T.yy[:, 1::8], T.ex[:, S3:S3 + 1], T.n2[:], A.add, A.add)
+        return ts(H["e3"])(T.p3[:], T.yy[:, 1::8], T.ex[:, S3:S3 + 1], None, A.add)
 
     def exchange0():
         k = H["off0"]
         ka, kb = pick(T.slq0[:], T.sls0[:], T.q0[:], T.s0[:], T.off0[:, 0:8], [k], [k])
-        send(q ^ 1, T.q1[:, 257:385].bitcast(dt.uint8), T.slq0[:].bitcast(dt.uint8), "r0c", ka)
-        send(q ^ 1, T.s1[:, 257:385], T.sls0[:], "r0s", kb)
-        copy(2, 257, 1, 257, 128, "c2", ("r0c", 16), ("r0s", 16))
+        both(0, 0, 128, 257, "r0", ka, kb)
+        copy(2, 192, 1, 257, 128, "c2", ("r0c", 16), ("r0s", 16))
 
     def exchange1():
         k = H["off1"]
-        ka, kb = pick(T.slq1[:], T.sls1[:], T.q1[:], T.s1[:], T.off1[:, 0:12],
+        ka, kb = pick(T.slq1[:, 64:192], T.sls1[:, 64:192], T.q1[:], T.s1[:], T.off1[:, 4:12],
                       [k, ("c1", 32), ("r0c", 16)], [k, ("c1", 32), ("r0s", 16)])
-        send(q ^ 2, T.q2[:, 385:577].bitcast(dt.uint8), T.slq1[:].bitcast(dt.uint8), "r1c", ka)
-        send(q ^ 2, T.s2[:, 385:577], T.sls1[:], "r1s", kb)
+        both(1, 0, 192, 0, "r1", ka, kb)
         if not half:
-            H["n2"] = act(("rn", 16))(T.cc[:, 8:9], T.n2[:], ID, turned)
-        act()(T.lnt[block(p4), 1:2], T.tr[block(p4), 256 + S3:257 + S3], CP)
-        need("y", *act(H["tot"], H["n2"])(T.lnt[:, 0:1], nh, ID, T.cc[:, 8:9]))
-        g.sync.dma_start(T.ln[:], T.lnt[32 * p4:32 * p4 + 1, 0:2]).then_inc(S.lnd, 16)
-        if not half:
-            copy(3, 513, 2, 257, 320, "c3", ("c2", 64), ("r1c", 16), ("r1s", 16))
+            copy(3, 0, 2, 0, 320, "c3", ("c2", 64), ("r1c", 16), ("r1s", 16))
 
-    def exchange2():
-        k = H["off2"]
-        ka, kb = pick(T.slq2[:], T.sls2[:], T.q2[:], T.s2[:], T.off2[:], [k, ("c2", 64), ("r1c", 16)], [k, ("c2", 64), ("r1s", 16)])
-        send(q ^ 4, T.q3[:, half:256 + half].bitcast(dt.uint8), T.slq2[:].bitcast(dt.uint8), "r2c", ka)
-        send(q ^ 4, T.s3[:, half:256 + half], T.sls2[:], "r2s", kb)
+    def exchange2(i):
+        k, (a, b) = H["off2"], PARTS[i]
+        ka, kb = pick(T.slq2[:, a:b], T.sls2[:, a:b], T.q2[:], T.s2[:], T.off2[:, a // 16:b // 16],
+                      [k, ("c2", 64), ("r1c", 16)], [k, ("c2", 64), ("r1s", 16)])
+        both(2, a, b, LAST + a, "r%d" % (2 + i), ka, kb)
+
+    def numbers():
+        k = act(("rn", 16))(T.cc[:, 9:10], T.n2[:], ID, 2.0 - half)
+        act()(T.lnt[block(p4), 1:2], T.tr[block(p4), 256 + S3:257 + S3], CP)
+        need("y", *act(H["tot"], k)(T.lnt[:, 0:1], nh, ID, T.cc[:, 9:10]))
+        g.sync.dma_start(T.ln[:], T.lnt[32 * p4:32 * p4 + 1, 0:2]).then_inc(S.lnd, 16)
 
     def piece(i, a, b):
-        ready = {1: ["p1", "v1"], 2: ["p2", "v2"], 3: ["p3", "v3", "w3"]}[i] + ["s%d" % i] * (a > 0)
-        H["s%d" % i] = scatter(i, a, b, T.vu if i == 1 else T.vr, *[H[r] for r in ready])
+        ready = {2: ["p2", "v2"], 3: ["p3", "v2", "w3"]}[i] + ["s%d" % i] * (a > 0)
+        H["s%d" % i] = scatter(i, a, b, T.vr, *[H[r] for r in ready])
 
     steps = {
-        "tot": lengths, "w3": rows3, "p3": places3, "counts": counts, "sets": sets, "y1": places01,
+        "tot": lengths, "w3": rows3, "p3": places3, "counts": counts, "sets": sets, "p1": places01, "ln": numbers,
         "masks": lambda: cp(k_gl, ("ld", 32), ("mk", 3 * len(es)))(T.dmu[:], T.dmx[:].indirect(diagonal)),
         "turn2": lambda: tp(k_ci)(T.cu[:], T.ci[:]),
         "lists2": lambda: cp(H["turn2"])(T.gl2[:, 0:3], T.cu[:, 0:96:32]),
-        "scan": lambda: scan(*H["sets"])(T.zs[:], T.ab[:, 0:288], T.ab[:, 287:575], BIG - 1.0, A.add, A.add),
-        "y": lambda: tt(H["counts"])(T.yy[:], T.tr[:, S3:256:16], T.fj[:], A.min),
-        "wq": lambda: quant(("lw", 16))(T.wq[:], T.ws[:], T.wt[:]),
-        "p1": lambda: ts(H["y1"])(T.p1[:], T.yo[:], T.cc[:, 0:1], T.cc[:, 1:2], A.mult, A.add),
-        "e2": lambda: earlier(2), "e3": lambda: earlier(3), "s1": lambda: scatter(1, 0, 8, T.vu, H["p1"], H["v1"]),
-        "p2": lambda: ts(H["e3"])(T.p2[:], T.yy[:, 1:16:2], T.ex[:, S2:S2 + 1], 1.0 - 2 * half, A.add, A.mult),
+        "scan": lambda: scan(*H["sets"])(T.zs[:], T.one[:], T.un[:], T.first[:], A.add, A.subtract),
+        "unwanted": lambda: tp(*H["sets"])(T.ut[:], T.un[:, 0:256]),
+        "y": lambda: scan(H["counts"], H["unwanted"])(T.yy[:], T.ut[:, SPARE::4], T.tr[:, SPARE:256:4], 0.0, A.mult, A.max),
+        "xq0": lambda: quant(k_x, ("lx", 16))(T.q0[:, 0:130], T.s0[:, 0:130], T.xt[:, 0:520]), "xq1": own,
+        "wq0": lambda: quant(("lw", 16))(T.wq[:, 0:128], T.ws[:, 0:128], T.wt[:, 0:512]),
+        "wq1": lambda: quant()(T.wq[:, 128:256], T.ws[:, 128:256], T.wt[:, 512:1024]),
+        "e1": lambda: earlier(1), "e2": lambda: earlier(2), "e3": lambda: earlier(3),
+        "s1": lambda: scatter(1, 0, 8, T.vu, H["p1"], H["v1"]),
+        "p2": lambda: ts(H["e3"], H["y"])(T.p2[:], T.yy[:, 5::8], T.ex[:, S2:S2 + 1], None, A.add),
         "j0": lambda: [join(1, T.z0[side(a), :], side(pb), H["tb1"]) for a in (pa, pb)][1],
         "j1": lambda: [join(1, T.z1[block(pa), 17 * a:17 * a + 17], block(pa + a), H["tb1"]) for a in range(2)][1],
         "off0": lambda: ts(H["j0"], H["lists2"])(T.off0[:], T.z0[:].indirect(last), -1.0, MID + 1.0, A.mult, A.add),
         "spread1": lambda: spread(1, T.z1[block(pa), 0:17], T.z1[block(pa), 17:34], H["j1"]),
         "off1": lambda: ts(H["spread1"])(T.off1[:], T.m1[:].indirect(last), -1.0, MID, A.mult, A.add),
-        "off2": lambda: ts(H["spread2"])(T.off2[:], T.m2[:].indirect(last), -1.0, EMPTY, A.mult, A.add),
-        "off3": lambda: ts(H["spread3"])(T.off3[:], T.m3[:].indirect(last2), -1.0, EMPTY + 256.0 * (1 - half), A.mult, A.add),
-        "x0": exchange0, "x1": exchange1, "x2": exchange2,
+        "off2": lambda: ts(H["spread2"])(T.off2[:], T.m2[:].indirect(last), LAST - EMPTY, None, A.add),
+        "off3": lambda: ts(H["spread3"])(T.off3[:], T.m3[:].indirect(last2), LAST - EMPTY, LAST + 256.0, A.add, A.min),
+        "early1": lambda: pick(T.slq1[:, 0:64], T.sls1[:, 0:64], T.q1[:, 0:257], T.s1[:, 0:257], T.off1[:, 0:4],
+                               [H["off1"], ("c1", 32)], [H["off1"], ("c1", 32)]),
+        "from3": lambda: half or [act(H["tot"])(T.cc[:, 6 + h:7 + h], nh, ID, 128.0 * h - 0.5, -0.5) for h in range(2)][1],
+        "wide1": lambda: widen(1), "wide2": lambda: widen(2), "wide3": lambda: widen(3),
+        "x0": exchange0, "x1": exchange1, "x2": lambda: exchange2(0), "x3": lambda: exchange2(1),
     }
     for i in (1, 2, 3):
         steps.update({"ta%d" % i: lambda i=i: turn(i, False, H["s%d" % i]), "tb%d" % i: lambda i=i: turn(i, True, H["s%d" % i])})
@@ -297,8 +319,12 @@ def rank_program(g, core, T, topo):
         steps.update({
             "j%d" % i: lambda i=i: join(i, T["z%d" % i][:, 0:WIDE[i]], every, H["tb%d" % i]),
             "halve%d" % i: lambda i=i: halve(i, H["j%d" % i]),
+            "J%d" % i: lambda i=i: [join(i, T["z%d" % i][0:64, a * WIDE[i]:(a + 1) * WIDE[i]], side(2 * a), H["tb%d" % i]) for a in range(2)][1],
+            "H%d" % i: lambda i=i: [tt(H["J%d" % i])(T["h%d" % i][block(0), a * WIDE[i]:(a + 1) * WIDE[i]], T["z%d" % i][block(a), 0:WIDE[i]],
+                                                   T["z%d" % i][block(a), WIDE[i]:2 * WIDE[i]], A.add) for a in range(2)][1],
+            "S%d" % i: lambda i=i: H.update({"spread%d" % i: spread(i, T["h%d" % i][block(0), 0:WIDE[i]], T["h%d" % i][block(0), WIDE[i]:2 * WIDE[i]], H["H%d" % i])}),
             "spread%d" % i: lambda i=i: spread(i, T["h%d" % i][block(0), 0:WIDE[i]], T["h%d" % i][block(1), 0:WIDE[i]], H["halve%d" % i])})
-    for name in ORDER:
+    for name in ORDER[half]:
         if ":" in name:
             piece(*[int(c) for c in name[1:].split(":")])
         else:
@@ -306,31 +332,34 @@ def rank_program(g, core, T, topo):
 
     def product(i):
         a, b = RUNS[half][i]
-        qi, si, landed = (T.q2, T.s2, []) if half else (T.q3, T.s3, [("c3", 96)])
-        ka, kb = pick(T.qa[:, a:b], T.sa[:, a:b], qi[:], si[:], T.off3[:, a // 16:b // 16],
-                      [H["off3"]] + landed + [("r2c", 16)] * (1 - half), [H["off3"]] + landed + [("r2s", 16)] * (1 - half))
-        terms = [(T.qa, T.sa, (ka, kb))] + [(T.q3, T.s3, (("r2c", 16), ("r2s", 16)))] * (half and a < 256)
-        for j, (qm, sm, waits) in enumerate(terms):
-            ks = [mm(H["wq"], *waits)(T.ps[:, 512 * (2 * i + w):512 * (2 * i + w) + b - a], T.wq[:, 128 * w:128 * w + 128],
-                                      T.ws[:, 128 * w:128 * w + 128], qm[:, a:b], sm[:, a:b], j == 0, j == len(terms) - 1)
+        parts = [(j, d) for j, (c, d) in enumerate(PARTS) if c < b]
+        codes, scales = [[("r%d%s" % (2 + j, kind), 16) for j, d in parts] for kind in "cs"]
+        if half:
+            ka, kb = pick(T.qa[:, a:b], T.sa[:, a:b], T.q2[:], T.s2[:], T.off3[:, a // 16:b // 16], [H["off3"]], [H["off3"]])
+        else:
+            end = LAST + parts[-1][1] + (b > 256)
+            ka, kb = pick(T.qa[:, a:b], T.sa[:, a:b], T.q3[:, 0:end], T.s3[:, 0:end], T.off3[:, a // 16:b // 16],
+                          [H["off3"], ("c3", 96)] + codes, [H["off3"], ("c3", 96)] + scales)
+        terms = [(T.q3, T.s3, LAST, codes + scales)] * (half and a < 256) + [(T.qa, T.sa, 0, (ka, kb))]
+        for j, (qm, sm, c, waits) in enumerate(terms):
+            ks = [mm(H["wq1"], *waits)(T.ps[:, 512 * (2 * i + w):512 * (2 * i + w) + b - a], T.wq[:, 128 * w:128 * w + 128],
+                                       T.ws[:, 128 * w:128 * w + 128], qm[:, c + a:c + b], sm[:, c + a:c + b], j == 0, j == len(terms) - 1)
                   for w in range(2)]
         return ks
 
-    def store(i, ks):
+    def store(by, i, w):
         a, b = RUNS[half][i]
-        ka = cp(ks[0])(T.ys[:, a:b], T.ps[:, 1024 * i:1024 * i + b - a])
-        kb = act(ks[1])(T.ys[:, 512 + a:512 + b], T.ps[:, 1024 * i + 512:1024 * i + 512 + b - a], CP)
-        for k, c in ((ka, a), (kb, 512 + a)):
-            need("y", *k)
-            g.sync.dma_start(T.y[:, c:c + b - a], T.ys[:, c:c + b - a]).then_inc(S.yo, 16)
-            n_yo[0] += 16
+        out, got = T.ys[:, 512 * w + a:512 * w + b], T.ps[:, 512 * (2 * i + w):512 * (2 * i + w) + b - a]
+        need("y", *(cp(ends[i][w])(out, got) if by == "v" else act(ends[i][w])(out, got, CP)))
+        g.sync.dma_start(T.y[:, 512 * w + a:512 * w + b], out).then_inc(S.yo, 16)
+        n_yo[0] += 16
 
-    ends = []
-    for i in range(6):
-        if i < 4:
-            ends.append(product(i))
-        if i >= 2:
-            store(i - 2, ends[i - 2])
+    ends = {}
+    for name in END[half]:
+        if name[0] == "p":
+            ends[int(name[1])] = product(int(name[1]))
+        else:
+            store(name[0], int(name[1]), int(name[2]))
 
     for kind in ("v", "s", "t", "gp"):
         need("gp", kind, n[kind])

from concourse.bass import DstId, RemoteDMATransfer
from concourse.mybir import dt, AluOpType, ActivationFunctionType

F32, I32, BF, U16, U8, Q8 = "float32", "int32", "bfloat16", "uint16", "uint8", "float8_e4m3fn_x4"
BIG = 4096.0
BACK = 1856
LAST = 576
EMPTY = 2.0 * (256 + 384 + 384)
WIN = 3936
ONE, TWO, FOUR = 7, 15, 23
SETS = 2 ** ONE + (2 ** TWO + 2 ** (TWO + 4)) + sum(2 ** (FOUR + 2 * i) for i in range(4))
SQ, SP, S3, S1, S2, S0, SPARE = 0, 8, 6, 14, 22, 30, 2
LENGTH = {1: 192, 2: 256, 3: 512}
WIDE = {1: 17, 2: 17, 3: 33}
MID = 192.0
RUNS = (((0, 128), (128, 256), (256, 384), (384, 512)), ((256, 384), (384, 512), (0, 128), (128, 256)))
ORDER = [("masks xq0 sets xq1 scan unwanted counts turn2 y e1 p1 lists2 e2 s1 e3 ta1 tb1 tot p2 j0 j1 off0 spread1 from3 x0 wide1 "
          "s2:0:8 w3 off1 ta2 tb2 early1 J2 p3 x1 H2 s3:0:2 S2 wide2 s3:2:8 off2 ta3 tb3 x2 j3 x3 ln halve3 spread3 off3 wq0 wq1").split()] * 2
END = ["p0 p1 p2 v00 s01 p3 v10 v11 v20 s21 v30 s31".split()] * 2
BY = {1: 2, 2: 2, 3: 4}
PARTS = ((0, 128), (128, 256))


def _s(n, d):
    return ("sbuf", [128, n], d)


SCRATCH = {
    "dmx": _s(128, I32), "dmu": _s(16, U16), "xt": _s(1040, BF), "wt": _s(1024, BF),
    "q0": _s(260, Q8), "s0": _s(260, U8), "q1": _s(386, Q8), "s1": _s(386, U8),
    "q2": _s(578, Q8), "s2": _s(578, U8), "q3": _s(834, Q8), "s3": _s(834, U8),
    "slq0": _s(128, Q8), "sls0": _s(128, U8), "slq1": _s(192, Q8), "sls1": _s(192, U8),
    "slq2": _s(256, Q8), "sls2": _s(256, U8),
    "qa": _s(512, Q8), "sa": _s(512, U8), "wq": _s(256, Q8), "ws": _s(256, U8),
    "pr": _s(96, F32), "pw": _s(64, F32), "ramp": _s(288, BF), "ct": _s(288, BF), "ti": _s(256, I32), "tf": _s(256, BF),
    "ci": _s(96, BF), "cu": _s(96, BF), "cc": _s(12, F32), "first": _s(1, BF), "gls": _s(10, U16), "gl2": _s(4, U16),
    "one": _s(288, BF), "un": _s(288, BF), "ut": _s(256, BF),
    "zs": _s(288, BF), "tr": _s(288, BF), "ex": _s(32, F32), "tot": _s(2, F32), "nn": _s(2, F32),
    "vr": _s(128, BF), "vu": _s(128, BF), "yy": _s(64, F32), "n2": _s(1, F32),
    "p1": _s(8, U16), "p2": _s(8, U16), "p3": _s(8, U16),
    "win1": _s(WIN, BF), "win2": _s(WIN, BF), "win3": _s(WIN, BF), "tr1": _s(544, BF), "tr2": _s(544, BF), "tr3": _s(1056, BF),
    "z0": _s(17, F32), "z1": _s(34, F32), "z2": _s(34, F32), "z3": _s(66, F32),
    "h2": _s(34, F32), "h3": _s(66, F32), "m1": _s(17, F32), "m2": _s(17, F32), "m3": _s(33, F32),
    "off0": _s(16, U16), "off1": _s(16, U16), "off2": _s(16, U16), "off3": _s(32, U16),
    "lnt": _s(4, F32), "ys": _s(1024, F32),
    "ps": ("psum", [128, 4096], F32),
}
SEMAPHORES = ["ld", "lx", "lw", "v", "s", "t", "gp", "mk", "r0c", "r0s", "r1c", "r1s", "r2c", "r2s", "r3c", "r3s", "rn",
              "c1", "c2", "c3", "l0", "lo", "yo", "lnd"]


def rank_program(g, core, T, topo):
    q = T.rank_of(core)
    if q is None:
        return
    A = AluOpType
    CP, ID, RELU = ActivationFunctionType.Copy, ActivationFunctionType.Identity, ActivationFunctionType.Relu
    S = T.sem
    p4, half, par = q & 3, q >> 2, q & 1
    pa, pb, o = p4 & 2, 2 - (p4 & 2), p4 ^ 1
    every = slice(0, 128)
    start, merge = {1: BACK, 2: 0, 3: 0}, {1: A.min, 2: A.add, 3: A.add}

    def block(a):
        return slice(32 * a, 32 * a + 32)

    def side(a):
        return slice(32 * a, 32 * a + 64)

    queues = {"v": g.vector, "s": g.scalar, "t": g.tensor, "gp": g, "y": g.sync}
    n, seen, left, n_yo = {"v": 0, "s": 0, "t": 0, "gp": 0}, {}, {"l0": 0, "lo": 0}, [0]

    def need(queue, sem, count):
        if seen.get((queue, sem), 0) < count:
            queues[queue].wait_ge(S[sem], int(count))
            seen[(queue, sem)] = count

    def on(kind, call):
        def after(*waits):
            def run(*a, **k):
                for w in waits:
                    need(kind, *w)
                call(*a, **k).then_inc(S[kind], 1)
                n[kind] += 1
                return kind, n[kind]
            return run
        return after

    v = g.vector
    ts, tt, cp, tp = on("v", v.tensor_scalar), on("v", v.tensor_tensor), on("v", v.tensor_copy), on("v", v.transpose)
    scan, fill, quant = on("v", v.tensor_tensor_scan), on("v", v.memset), on("v", v.quantize_mx)
    act, mm = on("s", g.scalar.activation), on("t", g.tensor.matmul_mx)

    def iota(out, pat, base, cm=0):
        return on("gp", g.iota)()(out, pat, base, cm, allow_small_or_imprecise_dtypes=True)

    def send(dst, out, in_, sem, after):
        need("gp", *after)
        rid, pid, _ = topo.addr(T.cores[dst])
        g.remote_dma(out, in_, S[sem], S.lo, pid, rid, topo.mask(core, T.cores[dst]))
        left["lo"] += len(topo.engines(core, T.cores[dst]))

    def copy(i, a, j, b, count, sem, *after):
        for w in after[:-1]:
            need("y", *w)
        g.sync.dma_start(T["q%d" % i][:, a:a + count].bitcast(dt.uint8), T["q%d" % j][:, b:b + count].bitcast(dt.uint8)).then_inc(S[sem], 16)
        for w in after[-1:]:
            need("y", *w)
        g.sync.dma_start(T["s%d" % i][:, a:a + count], T["s%d" % j][:, b:b + count]).then_inc(S[sem], 16)

    def pick(qo, so, qi, si, off, vwaits, swaits):
        return cp(*vwaits)(qo.bitcast(dt.uint32), qi.bitcast(dt.uint32).indirect(off)), act(*swaits)(so, si.indirect(off), CP)

    def scatter(i, a, b, values, *after):
        return cp(*after)(T["win%d" % i][:, 16:WIN].indirect(T["p%d" % i][:, a:b]), values[:, 16 * a:16 * b])

    def turn(i, back, k):
        w, t, c, a, b = T["win%d" % i], T["tr%d" % i], LENGTH[i], start[i], 16 * (WIDE[i] - 1)
        return tp(k)(t[:, b:b + c + 32], w[:, a:a + c + 32]) if back else tp(k)(t[:, 0:c], w[:, a + 16:a + c + 16])

    def join(i, out, rows, *after):
        t, r = T["tr%d" % i], SQ if i == 1 else SP
        return tt(*after)(out, t[rows, r::32], t[rows, r + 16::32], merge[i])

    def halve(i, k):
        z, c = T["z%d" % i], WIDE[i]
        return tt(k)(T["h%d" % i][0:64, 0:c], z[0:64, 0:c], z[64:128, 0:c], A.add)

    def spread(i, ha, hb, *k):
        return [tt(*k)(T["m%d" % i][block(b), :], ha, hb, merge[i]) for b in range(BY[i])][-1]

    def widen(i):
        m, k = T["m%d" % i], H["spread%d" % i]
        if BY[i] == 2:
            k = act(k)(m[64:128, :], m[0:64, :], CP)
        if BY[i] == 1:
            k = [act(k)(m[block(b), :], m[block(0), :], CP) for b in (1, 2, 3)][2]
        H["spread%d" % i] = k

    def both(i, a, b, c, sem, ka, kb):
        send(q ^ (1 << i), T["q%d" % (i + 1)][:, c:c + b - a].bitcast(dt.uint8), T["slq%d" % i][:, a:b].bitcast(dt.uint8), sem + "c", ka)
        send(q ^ (1 << i), T["s%d" % (i + 1)][:, c:c + b - a], T["sls%d" % i][:, a:b], sem + "s", kb)

    def blank(i, *after):
        for a in range(0, LENGTH[i] + 32, 288):
            b, c = min(LENGTH[i] + 32, a + 288), start[i]
            k = act(*after)(T["win%d" % i][:, c + a:c + b], T.ramp[:, 0:b - a], ID, BIG if i == 1 else T.cc[:, 3:4], 0.0)
        return k

    def pair(rows, c, a, b, *after):
        return act(*after)(T.cc[rows, c:c + 2], T.ramp[rows, 0:2], ID, a, b - a)

    mine = slice(32 * p4, 32 * p4 + 16)
    for e, queue in enumerate((g.sync, g.scalar)):
        queue.dma_start(T.dmx[32 * p4 + 16 * e:32 * p4 + 16 * e + 16, mine], T.dm[:]).then_inc(S.ld, 16)
    g.sync.dma_start(T.xt[:, 8:1032], T.x[:]).then_inc(S.lx, 16)

    k_low = iota(T.ramp[:, 0:128], [[1, 128]], 0)
    iota(T.ramp[:, 128:256], [[1, 128]], 128)
    k_ramp = iota(T.ramp[:, 256:288], [[0, 2], [1, 16]], 0, 1)
    k = fill()(T.pr[:], 0.0)
    for rows in ((block(1), side(2)), (block(0), side(2)), (side(0), block(3)), (slice(0, 96),))[p4]:
        k_dm = fill()(T.dmx[rows, mine], 0)
    for rows, c, s in ((every, slice(S3, S3 + 1), ONE - q), (every, slice(S2, S2 + 1), ONE - (q ^ 4)),
                       (block(o), slice(SQ, 32, 8), FOUR - par), (every, slice(32 + SPARE, 64, 8), 0)):
        ka = fill(k)(T.pr[rows, c], 2.0 ** s)
    for rows, c, s in ((side(pb), slice(SP, 32, 16), TWO - p4), (side(pa), slice(S1, S1 + 1), TWO - (p4 ^ 2)),
                       (block(p4), slice(S0, S0 + 1), FOUR - 1 + par)):
        kb = act(k)(T.pr[rows, c], T.pr[rows, slice(c.start + 64, c.stop + 64, c.step)], ID, 2.0 ** s, 0.0)
    fill()(T.xt[:, 0:8], 0.0)
    k = tp(ka, kb)(T.pw[:], T.pr[:, 0:64])
    fill()(T.un[:, 256:288], 1.0)
    k_x = fill()(T.xt[:, 1032:1040], 0.0)
    ks = [ts(k, k_low)(T.ti[:, a:a + 128], T.ramp[:, 0:128], float(a), T.pw[:, 0:1], A.add, A.mult) for a in (0, 128)]
    ks = [ts(k)(T.ti[:, a:a + 128], T.ti[:, a:a + 128], SETS, None, A.bitwise_and) for k, a in zip(ks, (0, 128))]
    ks = [ts(k)(T.tf[:, a:a + 128], T.ti[:, a:a + 128], T.pw[:, 0:1], None, A.is_lt) for k, a in zip(ks, (0, 128))]

    need("gp", *k_dm)
    g.wait_ge(S.ld, 32)
    peers = [T.cores[q ^ d] for d in (1, 2, 3)]
    es = [e for e in topo.engines(core, peers[0])[::2] if all(e in topo.engines(core, d) for d in peers)]
    ids = [DstId(rid=topo.addr(d)[0], pnc=topo.addr(d)[1]) for d in peers]
    g.remote_dma_fused([RemoteDMATransfer(dst_ids=ids, dma_engine_mask=sum(1 << e for e in es), remote_sem=S.mk,
                                          srcs=[T.dmx[:, mine]], dsts=[T.dmx[:, mine] for d in peers])], local_sem=S.l0)
    left["l0"] += len(es)

    for a, c, b in ((0, 16, 0), (32, 16, 8), (64, 8, 0)):
        iota(T.ci[:, a:a + 16], [[1, 8], [c + 1, 2]], b)
        k_ci = iota(T.ci[:, a + 16:a + 32], [[1, 8], [-c, 2]], b + c)
    ts()(T.cc[:, 10:12], T.ramp[:, 3:8:4], T.pw[:, 32:33], None, A.mult)
    ts()(T.first[:], T.pw[:, 32:33], 512.0, None, A.mult)
    k = tp(k_ramp)(T.ct[:], T.ramp[:])
    fill()(T.ex[0:32, 0:16], half - 1.0)
    fill()(T.ex[0:32, 16:32], -1.0)
    k_gl = cp(k)(T.gls[:, 0:9], T.ct[:, 0:288:32])
    held, diagonal, last2, last = T.gls[:, 0:8], T.gls[:, 8:9], T.gl2[:, 0:2], T.gl2[:, 2:3]
    for rows, a, b in ((block(p4), MID, 0.0), (block(o), MID - 256.0, 256.0), (side(pb), MID, 384.0)):
        k_cc = pair(rows, 2, a, b, k_low)
    for b, a, c in ((p4, -257.0, 1.0), (o, -129.0, 1.0), (p4 ^ 2, -193.0, 1.0), (p4 ^ 3, 0.0, -1.0)):
        pair(block(b), 4, a, c)
    for a in (192, 480):
        act()(T.tr1[:, a:a + 64], T.ramp[:, 0:64], CP)
    for rows, a, b in ((block(p4), 1.0, BACK - 1.0), (block(o), -1.0, BACK + 192.0)):
        pair(rows, 0, a, b)
    blank(1, k_ramp)
    for a, b, c in ((0, 128, 10), (128, 288, 11)):
        ts()(T.one[:, a:b], T.ramp[:, a:b], 0.0, T.cc[:, c:c + 1], A.is_ge, A.add)

    H = {}
    nh = T.nn[:, 0:1]

    def own():
        k = quant()(T.q0[:, 130:260], T.s0[:, 130:260], T.xt[:, 520:1040])
        copy(1, 0, 0, 1, 257, "c1", ("l0", left["l0"]), k, k)
        copy(2, 320, 0, 2, 257, "c2")
        if not half:
            copy(3, 320, 0, 2, 256, "c3")
            copy(3, LAST + 256, 0, 0, 1, "c3")
        g.sync.dma_start(T.wt[:], T.w[:]).then_inc(S.lw, 16)
        return k

    def sets():
        k = H["masks"]
        return (cp(k, ks[1])(T.un[:, 0:128], T.tf[:].indirect(T.dmu[:, 0:8])),
                act(k)(T.un[:, 128:256], T.tf[:].indirect(T.dmu[:, 8:16]), CP))

    def counts():
        k = tp(H["scan"])(T.tr[:], T.zs[:])
        H["v1"] = act(H["scan"])(T.vu[:], T.zs[:].indirect(held), ID, T.cc[:, 2:3], -1.0)
        act()(T.vr[:], T.zs[:].indirect(held), ID, T.cc[:, 4:5], T.cc[:, 5:6])
        H["v2"] = blank(2)
        H["blank3"] = blank(3)
        return k

    def places01():
        ts(H["y"])(T.p1[side(pa), :], T.yy[side(pa), 3::8], T.cc[side(pa), 0:1], T.cc[side(pa), 1:2], A.mult, A.add)
        return [ts()(T.p1[block(a), :], T.yy[block(p4), 7::8], BACK - 1.0, None, A.add) for a in (pb, pb + 1)][1]

    def earlier(a):
        return tt(H["e%d" % (a - 1) if a > 1 else "counts"])(T.ex[block(a), :], T.ex[block(a - 1), :], T.tr[block(a - 1), 256:288], A.add)

    def lengths():
        k = tt(H["e3"])(T.tot[block(3), :], T.ex[block(3), S3:32:16], T.tr[block(3), 256 + S3:288:16], A.add)
        k = on("gp", g.partition_broadcast)(k)(T.nn[:], T.tot[96:97, :], 128)
        send(q ^ 4, T.n2[:], T.nn[:, 1:2], "rn", k)
        return k

    def rows3():
        if half:
            return H["blank3"]
        return [act(H["from3"])(T.win3[block(p4), 16 + 256 * h:272 + 256 * h], T.ramp[block(p4), 0:256], RELU,
                                T.cc[block(p4), 6 + h:7 + h], 0.5) for h in range(2)][1]

    def places3():
        if half:
            return ts(H["e3"], ("rn", 16))(T.p3[:], T.yy[:, 1::8], T.ex[:, S3:S3 + 1], T.n2[:], A.add, A.add)
        return ts(H["e3"])(T.p3[:], T.yy[:, 1::8], T.ex[:, S3:S3 + 1], None, A.add)

    def exchange0():
        k = H["off0"]
        ka, kb = pick(T.slq0[:], T.sls0[:], T.q0[:], T.s0[:], T.off0[:, 0:8], [k], [k])
        both(0, 0, 128, 257, "r0", ka, kb)
        copy(2, 192, 1, 257, 128, "c2", ("r0c", 16), ("r0s", 16))

    def exchange1():
        k = H["off1"]
        ka, kb = pick(T.slq1[:, 64:192], T.sls1[:, 64:192], T.q1[:], T.s1[:], T.off1[:, 4:12],
                      [k, ("c1", 32), ("r0c", 16)], [k, ("c1", 32), ("r0s", 16)])
        both(1, 0, 192, 0, "r1", ka, kb)
        if not half:
            copy(3, 0, 2, 0, 320, "c3", ("c2", 64), ("r1c", 16), ("r1s", 16))

    def exchange2(i):
        k, (a, b) = H["off2"], PARTS[i]
        ka, kb = pick(T.slq2[:, a:b], T.sls2[:, a:b], T.q2[:], T.s2[:], T.off2[:, a // 16:b // 16],
                      [k, ("c2", 64), ("r1c", 16)], [k, ("c2", 64), ("r1s", 16)])
        both(2, a, b, LAST + a, "r%d" % (2 + i), ka, kb)

    def numbers():
        k = act(("rn", 16))(T.cc[:, 9:10], T.n2[:], ID, 2.0 - half)
        act()(T.lnt[block(p4), 1:2], T.tr[block(p4), 256 + S3:257 + S3], CP)
        need("y", *act(H["tot"], k)(T.lnt[:, 0:1], nh, ID, T.cc[:, 9:10]))
        g.sync.dma_start(T.ln[:], T.lnt[32 * p4:32 * p4 + 1, 0:2]).then_inc(S.lnd, 16)

    def piece(i, a, b):
        ready = {2: ["p2", "v2"], 3: ["p3", "v2", "w3"]}[i] + ["s%d" % i] * (a > 0)
        H["s%d" % i] = scatter(i, a, b, T.vr, *[H[r] for r in ready])

    steps = {
        "tot": lengths, "w3": rows3, "p3": places3, "counts": counts, "sets": sets, "p1": places01, "ln": numbers,
        "masks": lambda: cp(k_gl, ("ld", 32), ("mk", 3 * len(es)))(T.dmu[:], T.dmx[:].indirect(diagonal)),
        "turn2": lambda: tp(k_ci)(T.cu[:], T.ci[:]),
        "lists2": lambda: cp(H["turn2"])(T.gl2[:, 0:3], T.cu[:, 0:96:32]),
        "scan": lambda: scan(*H["sets"])(T.zs[:], T.one[:], T.un[:], T.first[:], A.add, A.subtract),
        "unwanted": lambda: tp(*H["sets"])(T.ut[:], T.un[:, 0:256]),
        "y": lambda: scan(H["counts"], H["unwanted"])(T.yy[:], T.ut[:, SPARE::4], T.tr[:, SPARE:256:4], 0.0, A.mult, A.max),
        "xq0": lambda: quant(k_x, ("lx", 16))(T.q0[:, 0:130], T.s0[:, 0:130], T.xt[:, 0:520]), "xq1": own,
        "wq0": lambda: quant(("lw", 16))(T.wq[:, 0:128], T.ws[:, 0:128], T.wt[:, 0:512]),
        "wq1": lambda: quant()(T.wq[:, 128:256], T.ws[:, 128:256], T.wt[:, 512:1024]),
        "e1": lambda: earlier(1), "e2": lambda: earlier(2), "e3": lambda: earlier(3),
        "s1": lambda: scatter(1, 0, 8, T.vu, H["p1"], H["v1"]),
        "p2": lambda: ts(H["e3"], H["y"])(T.p2[:], T.yy[:, 5::8], T.ex[:, S2:S2 + 1], None, A.add),
        "j0": lambda: [join(1, T.z0[side(a), :], side(pb), H["tb1"]) for a in (pa, pb)][1],
        "j1": lambda: [join(1, T.z1[block(pa), 17 * a:17 * a + 17], block(pa + a), H["tb1"]) for a in range(2)][1],
        "off0": lambda: ts(H["j0"], H["lists2"])(T.off0[:], T.z0[:].indirect(last), -1.0, MID + 1.0, A.mult, A.add),
        "spread1": lambda: spread(1, T.z1[block(pa), 0:17], T.z1[block(pa), 17:34], H["j1"]),
        "off1": lambda: ts(H["spread1"])(T.off1[:], T.m1[:].indirect(last), -1.0, MID, A.mult, A.add),
        "off2": lambda: ts(H["spread2"])(T.off2[:], T.m2[:].indirect(last), LAST - EMPTY, None, A.add),
        "off3": lambda: ts(H["spread3"])(T.off3[:], T.m3[:].indirect(last2), LAST - EMPTY, LAST + 256.0, A.add, A.min),
        "early1": lambda: pick(T.slq1[:, 0:64], T.sls1[:, 0:64], T.q1[:, 0:257], T.s1[:, 0:257], T.off1[:, 0:4],
                               [H["off1"], ("c1", 32)], [H["off1"], ("c1", 32)]),
        "from3": lambda: half or [act(H["tot"])(T.cc[:, 6 + h:7 + h], nh, ID, 128.0 * h - 0.5, -0.5) for h in range(2)][1],
        "wide1": lambda: widen(1), "wide2": lambda: widen(2), "wide3": lambda: widen(3),
        "x0": exchange0, "x1": exchange1, "x2": lambda: exchange2(0), "x3": lambda: exchange2(1),
    }
    for i in (1, 2, 3):
        steps.update({"ta%d" % i: lambda i=i: turn(i, False, H["s%d" % i]), "tb%d" % i: lambda i=i: turn(i, True, H["s%d" % i])})
    for i in (2, 3):
        steps.update({
            "j%d" % i: lambda i=i: join(i, T["z%d" % i][:, 0:WIDE[i]], every, H["tb%d" % i]),
            "halve%d" % i: lambda i=i: halve(i, H["j%d" % i]),
            "J%d" % i: lambda i=i: [join(i, T["z%d" % i][0:64, a * WIDE[i]:(a + 1) * WIDE[i]], side(2 * a), H["tb%d" % i]) for a in range(2)][1],
            "H%d" % i: lambda i=i: [tt(H["J%d" % i])(T["h%d" % i][block(0), a * WIDE[i]:(a + 1) * WIDE[i]], T["z%d" % i][block(a), 0:WIDE[i]],
                                                   T["z%d" % i][block(a), WIDE[i]:2 * WIDE[i]], A.add) for a in range(2)][1],
            "S%d" % i: lambda i=i: H.update({"spread%d" % i: spread(i, T["h%d" % i][block(0), 0:WIDE[i]], T["h%d" % i][block(0), WIDE[i]:2 * WIDE[i]], H["H%d" % i])}),
            "spread%d" % i: lambda i=i: spread(i, T["h%d" % i][block(0), 0:WIDE[i]], T["h%d" % i][block(1), 0:WIDE[i]], H["halve%d" % i])})
    for name in ORDER[half]:
        if ":" in name:
            piece(*[int(c) for c in name[1:].split(":")])
        else:
            H[name] = steps[name]()

    def product(i):
        a, b = RUNS[half][i]
        parts = [(j, d) for j, (c, d) in enumerate(PARTS) if c < b]
        codes, scales = [[("r%d%s" % (2 + j, kind), 16) for j, d in parts] for kind in "cs"]
        if half:
            ka, kb = pick(T.qa[:, a:b], T.sa[:, a:b], T.q2[:], T.s2[:], T.off3[:, a // 16:b // 16], [H["off3"]], [H["off3"]])
        else:
            end = LAST + parts[-1][1] + (b > 256)
            ka, kb = pick(T.qa[:, a:b], T.sa[:, a:b], T.q3[:, 0:end], T.s3[:, 0:end], T.off3[:, a // 16:b // 16],
                          [H["off3"], ("c3", 96)] + codes, [H["off3"], ("c3", 96)] + scales)
        terms = [(T.q3, T.s3, LAST, codes + scales)] * (half and a < 256) + [(T.qa, T.sa, 0, (ka, kb))]
        for j, (qm, sm, c, waits) in enumerate(terms):
            ks = [mm(H["wq1"], *waits)(T.ps[:, 512 * (2 * i + w):512 * (2 * i + w) + b - a], T.wq[:, 128 * w:128 * w + 128],
                                       T.ws[:, 128 * w:128 * w + 128], qm[:, c + a:c + b], sm[:, c + a:c + b], j == 0, j == len(terms) - 1)
                  for w in range(2)]
        return ks

    def store(by, i, w):
        a, b = RUNS[half][i]
        out, got = T.ys[:, 512 * w + a:512 * w + b], T.ps[:, 512 * (2 * i + w):512 * (2 * i + w) + b - a]
        need("y", *(cp(ends[i][w])(out, got) if by == "v" else act(ends[i][w])(out, got, CP)))
        g.sync.dma_start(T.y[:, 512 * w + a:512 * w + b], out).then_inc(S.yo, 16)
        n_yo[0] += 16

    ends = {}
    for name in END[half]:
        if name[0] == "p":
            ends[int(name[1])] = product(int(name[1]))
        else:
            store(name[0], int(name[1]), int(name[2]))

    for kind in ("v", "s", "t", "gp"):
        need("gp", kind, n[kind])
    for sem in left:
        need("gp", sem, left[sem])
    g.wait_ge(S.yo, n_yo[0])
    g.wait_ge(S.lnd, 16)
